import numpy as np, ml_dtypes
CORES = [23,119,17,113]
N = 4
BF = ml_dtypes.bfloat16
def gentries(a):
    return np.ascontiguousarray(a.reshape(8, 16, -1).transpose(0, 2, 1)).reshape(8, -1)
def gtable(e):
    e = np.asarray(e); return np.ascontiguousarray(e.reshape(8, -1, 16).transpose(0, 2, 1)).reshape(128, -1).astype(np.int32)
V, G, L, SH, RO = 512, 192, 8192, 3, 2
W = V + (N - 1) * G; NV = N * V; TOP = 32640; END = 2 ** 23
def place(x, r):
    d = (r - x // V) % N
    return np.where(d == 0, x % V, V + (d - 1) * G + x % V)
def rising(x, n):
    x = np.sort(x, axis=-1); x[..., 1:] = np.where(x[..., 1:] == x[..., :-1], NV, x[..., 1:]); x = np.sort(x, axis=-1)
    return np.where((np.arange(4) < n[..., None]) & (x < NV), x, -1)
def counts(rng):
    return rng.choice(np.array([0, 1, 2, 2, 3, 3, 4]), (N, 8, 3, V))
def parts(rng, size, share, n):
    nets = rng.integers(0, W, (N, 8, 2 * V)); lv = np.zeros((N, 8, 3, V, 4), np.int64); r = np.arange(N)[:, None]
    for g in range(8):
        p = int(size[g])
        if p <= N * G // 2:
            x = rng.permutation(N * G)[:p]; pool = np.sort(x // G * V + x % G)
            nets[:, g] = np.where(rng.random((N, 2 * V)) < share, place(pool[rng.integers(0, p, (N, 2 * V))], r), nets[:, g])
        else:
            pool = np.sort(rng.permutation(NV)[:p])
        lv[:, g] = pool[rng.integers(0, p, (N, 3, V, 4))]
    tb = rng.integers(0, 65536, (N, 8, 3, V))
    return nets, rising(lv, n), tb, rng.integers(0, TOP + 1, (N, 8, 16, L)), rng.integers(0, 20001, (N, 8, 16, V))
def pack(nets, lv, tb, ce, rq):
    return {"fan": np.stack([gtable(x) for x in nets]), "cells": ce.reshape(N, 128, L).astype(np.float32).astype(BF), "req": rq.reshape(N, 128, V).astype(np.float32).astype(BF),
            "leaf0": np.ascontiguousarray(lv.transpose(0, 1, 2, 4, 3)).reshape(N, 8, 12 * V).astype(np.int32), "tab0": tb.reshape(N, 8, 3 * V).astype(np.int32)}
def setup_inputs(rng):
    return pack(*parts(rng, rng.permutation(np.array([4, 6, 8, 12, 20, 28, 200, NV])), 0.4, counts(rng)))
def setup_inputs_ties(rng):
    nets, lv, tb, ce, rq = parts(rng, rng.permutation(np.array([4, 5, 6, 8, 10, 12, 16, 24])), 0.5, counts(rng))
    ce = 256 * rng.integers(0, 3, ce.shape); rq = 256 * rng.integers(0, 2, rq.shape)
    g = rng.permutation(8); ce[:, g[0]] = 1024; rq[:, g[0]] = 0
    for i in (1, 2): ce[:, g[i]] = rng.integers(0, 2, ce[:, g[i]].shape); rq[:, g[i]] = 0
    rq = np.where(rng.random((N, 8, 1, V)) < 0.1, TOP, rq)
    return pack(nets, lv, tb, ce, rq)
def setup_inputs_bare(rng):
    n = counts(rng); n[:, ::2] = 0; n[:, 5] = rng.integers(0, 2, (N, 3, V)); n[rng.integers(0, N)] = 0
    nets, lv, tb, ce, rq = parts(rng, rng.permutation(np.array([4, 6, 8, 12, 20, 28, 200, NV])), 0.4, n)
    nets[:, 1] = np.tile(np.arange(V), 2); nets[:, 3, V:] = nets[:, 3, :V]; nets[:, 4, V::2] = nets[:, 4, :V:2]
    return pack(nets, lv, tb, ce, rq)
def setup_inputs_ends(rng):
    nets, lv, tb, ce, rq = parts(rng, np.full(8, 8), 0.0, counts(rng))
    for g in range(8):
        p = (4, 5, 6, 8)[g % 4]
        pool = np.sort(np.concatenate([np.array([0, NV - 1]), 1 + rng.permutation(NV - 2)[:p - 2]]))
        lv[:, g] = rising(pool[np.argsort(rng.random((N, 3, V, p)), axis=-1)[..., :4]], np.full((N, 3, V), 4))
        if g % 2 == 1: nets[:, g] = rng.choice(np.array([0, V - 1, V, W - 1]), (N, 2 * V))
    tb = np.where(rng.random(tb.shape) < 0.6, rng.choice(np.array([0, 65535, 1, 32768, 43690, 65534]), tb.shape), tb)
    ce = np.where(rng.random(ce.shape) < 0.4, TOP * rng.integers(0, 2, ce.shape), ce); ce[:, :, :, 0] = rng.integers(0, TOP + 1, (N, 8, 16)); ce[:, 7] = np.where(rng.random((N, 16, L)) < 0.98, TOP, ce[:, 7])
    rq = np.where(rng.random(rq.shape) < 0.2, rng.choice(np.array([0, 1, TOP]), rq.shape), rq); rq = np.where(rng.random((N, 8, 1, V)) < 0.1, 0, rq)
    return pack(nets, lv, tb, ce, rq)
def setup_inputs_alike(rng):
    nets, lv, tb, ce, rq = parts(rng, rng.integers(3, 7, 8), 1.0, counts(rng))
    lv[:, ::2, 1:] = lv[:, ::2, :1]; tb[:, ::2, 1:] = tb[:, ::2, :1]
    return pack(nets, lv, tb, ce, rq)
def setup_inputs_spread(rng):
    nets, lv, tb, ce, rq = parts(rng, rng.permutation(np.array([4, 6, 8, 12, 20, 28, 200, NV])), 0.4, counts(rng))
    ce = np.minimum(np.floor(np.exp2(15 * rng.random((N, 8, 1, L))) * rng.random((N, 8, 16, L))), TOP)
    rq = np.minimum(np.floor(np.exp2(15 * rng.random((N, 8, 1, V))) * rng.random((N, 8, 16, V))), TOP)
    w = rng.random(tb.shape); t2 = rng.integers(0, 65536, tb.shape); t3 = rng.integers(0, 65536, tb.shape)
    tb = np.where(w < 0.3, tb & t2 & t3, np.where(w < 0.6, tb | t2 | t3, tb))
    nets[:, ::2] = np.where(rng.random((N, 4, 2 * V)) < 0.5, np.floor(W * rng.random((N, 4, 2 * V)) ** 3).astype(np.int64), nets[:, ::2])
    return pack(nets, lv, tb, ce, rq)
def check_inputs(d):
    bad = []
    for k, lo, hi in (("fan", 0, W - 1), ("cells", 0, TOP), ("req", 0, TOP), ("leaf0", -1, NV - 1), ("tab0", 0, 65535)):
        x = np.asarray(d[k]).astype(np.float32)
        if not (np.all(x >= lo) and np.all(x <= hi) and np.all(np.floor(x) == x)): bad.append("range of " + k)
    x = np.asarray(d["leaf0"]).reshape(-1, 4, V); a, b = x[:, :-1], x[:, 1:]
    if not np.all((b == -1) | ((a >= 0) & (b > a))): bad.append("order of leaf0")
    return bad
def old_rows():
    o = np.zeros((16, 16), np.int32)
    for s in range(16):
        k = 0
        for p in range(4):
            if (s >> p) & 1:
                o[s] |= (((np.arange(16) >> p) & 1) << k).astype(np.int32); k += 1
    return o
OLD = old_rows()
def turned(x, u, t):
    p = np.sum(u[..., None, :] < x[..., :, None], axis=-1)
    s = np.sum(np.where((x < NV) & (p < 4), 1 << np.minimum(p, 3), 0), axis=-1)
    return (t[..., None] >> OLD[s]) & 1
def reference(fan, cells, req, leaf0, tab0):
    lv = leaf0.astype(np.int32).reshape(N, 8, 3, 4, V).transpose(0, 1, 2, 4, 3); lv = np.where(lv < 0, np.int32(NV), lv)
    tb = tab0.astype(np.int32).reshape(N, 8, 3, V); co = np.full((N, 8, 3, V), -1, np.int32)
    nets = np.stack([gentries(x) for x in fan]).astype(np.int64).reshape(N, 8, 2, V)
    ce = cells.astype(np.float32).astype(np.int32).reshape(N, 8, 16, L); rq = req.astype(np.float32).astype(np.int32).reshape(N, 8, 16, V)
    own = np.full((N, 8, 1, V, 4), NV, np.int32); own[..., 0] = np.arange(NV, dtype=np.int32).reshape(N, 1, 1, V)
    triv = np.full((N, 8, 1, V), 43690, np.int32); bits = np.arange(16, dtype=np.int32)
    for rnd in range(RO):
        al = np.concatenate([lv, own], axis=2); at = np.concatenate([tb, triv], axis=2)
        lv = np.full_like(lv, NV); tb = np.zeros_like(tb); co = np.full_like(co, -1)
        for r in range(N):
            wl = np.concatenate([al[r]] + [al[(r - d) % N][:, :, :G] for d in range(1, N)], axis=2)
            wt = np.concatenate([at[r]] + [at[(r - d) % N][:, :, :G] for d in range(1, N)], axis=2)
            ia = nets[r, :, 0][:, None, :]; ib = nets[r, :, 1][:, None, :]
            xa = np.repeat(np.take_along_axis(wl, ia[..., None], 2), 4, axis=1); ta = np.repeat(np.take_along_axis(wt, ia, 2), 4, axis=1)
            xb = np.tile(np.take_along_axis(wl, ib[..., None], 2), (1, 4, 1, 1)); tc = np.tile(np.take_along_axis(wt, ib, 2), (1, 4, 1))
            both = np.sort(np.concatenate([xa, xb], axis=-1), axis=-1)
            both[..., 1:] = np.where(both[..., 1:] == both[..., :-1], np.int32(NV), both[..., 1:]); both = np.sort(both, axis=-1)
            u = both[..., :4]; void = (both[..., 4] < NV) | (xa[..., 0] == NV) | (xb[..., 0] == NV)
            t = (65535 - np.sum((turned(xa, u, ta) & turned(xb, u, tc)) << bits, axis=-1)).astype(np.int32)
            c1 = ((t + 29 * (t >> 5)) & (L - 1)).reshape(8, 1, 16 * V); c2 = (t >> SH).reshape(8, 1, 16 * V)
            e = np.minimum(np.take_along_axis(ce[r], c1, 2), np.take_along_axis(ce[r], c2, 2)).reshape(8, 16, 16, V)
            cost = np.sum(np.maximum(e - rq[r][:, :, None, :], 0), axis=1)
            key = np.where(void, END, 16 * cost + np.arange(16)[None, :, None])
            for c in range(3):
                k = np.min(key, axis=1); full = k < END; i = (k & 15)[:, None, :]
                lv[r, :, c] = np.where(full[..., None], np.take_along_axis(u, i[..., None], 1)[:, 0], NV)
                tb[r, :, c] = np.where(full, np.take_along_axis(t, i, 1)[:, 0], 0); co[r, :, c] = np.where(full, k >> 4, -1)
                key = np.where((key >> 4) == (k >> 4)[:, None, :], END, key)
    yl = np.where(lv == NV, -1, lv).transpose(0, 1, 2, 4, 3)
    return {"yl": np.ascontiguousarray(yl).reshape(N, 8, 12 * V).astype(np.float32), "yt": tb.reshape(N, 8, 3 * V).astype(np.float32), "yc": co.reshape(N, 8, 3 * V).astype(np.float32)}

@@ -1,0 +1,556 @@
+import numpy as np
+from concourse.bass import DstId, RemoteDMATransfer
+from concourse.mybir import AluOpType as A, AxisListType, ActivationFunctionType as F
+
+NCH = 2
+V, G, NR, RO = 512, 192, 4, 2
+W = V + (NR - 1) * G
+CW = V // NCH; NVB = CW // 128; HH = 4 // NVB; HN = 128 // HH; N24 = NVB * 24; LW = CW // 16
+QV = (0, 1, 2, 3, 4, 6)
+TRIV = ((-65536, 0), (-820, 118784), (61696, 3824), (69632, -12544), (0, -131072), (0, -131072))
+TRIV0 = 174762.0
+MATS = ["I", "nI", "A0", "A1", "A2", "A3", "AL", "B0", "B1", "B2", "B3", "BL", "FA", "FB", "HA0", "HA1", "HB0", "HB1", "VK", "RM", "PB", "PN0", "PN1", "PN2"] \
+    + ["Z%s%d" % (s, q) for s in "AB" for q in range(6)] + ["D%s%d" % (s, q) for s in "AB" for q in range(6)]
+f32, bf, i32, u16, f16 = "float32", "bfloat16", "int32", "uint16", "float16"
+SCRATCH = {}
+def _sb(name, shape, dt, per=1):
+    for k in range(per):
+        SCRATCH[name + (str(k) if per > 1 else "")] = ("sbuf", [128] + list(shape), dt)
+for _n, _s, _d in (("MT", [len(MATS) * 8, 16], bf), ("ML", [12 * 96], bf), ("Z3", [8, 16], bf), ("Z2", [160], bf), ("ZF", [128], f32),
+                   ("PI", [8, 16], bf), ("C32", [8, 16], bf), ("I32", [128], f32), ("OC", [V], f32), ("QI", [3, 128], bf), ("D1", [32 * V], bf),
+                   ("IW", [3 * 160], bf), ("IW0", [160], bf),
+                   ("BO", [8], bf), ("BOF", [8], f32), ("BC", [48], f32), ("PC", [4], i32), ("ROW", [96], f32), ("TMP", [2 * 96], f32),
+                   ("PL", [80], i32), ("PF", [80], f32), ("PS", [3 * 80], i32), ("PM", [4 * 80], f32), ("WL", [5, 8, 16], bf), ("WC", [5, 16], bf),
+                   ("TI", [256], i32), ("TJ", [256], i32), ("BT", [256], bf), ("LUT", [1280], bf), ("RS", [CW], f32), ("RR", [CW], f32),
+                   ("fanI", [64], i32), ("L0", [64], u16), ("LW3", [NCH, 6, LW], u16), ("LWL", [NCH * 6 * LW], u16), ("INI", [V], i32), ("INF", [V], f32),
+                   ("CE", [8192], bf), ("RQ", [V], bf)):
+    _sb(_n, _s, _d)
+for _n, _s, _d in (("W0", [W], f32), ("WB", [3 * W], bf),
+                   ("G0", [2 * CW], f16), ("GW", [6 * CW], bf), ("SG", [9 * CW], bf), ("SE", [9 * CW], bf), ("EQ", [2 * CW], bf),
+                   ("R12", [4 * CW], bf), ("IX", [2 * CW], bf), ("VD", [CW], bf), ("AC", [2 * CW], f32), ("EI", [2 * CW], i32),
+                   ("ME", [4 * CW], i32), ("NF", [CW], f32), ("T5", [CW], i32), ("C1", [CW], u16), ("C2", [CW], u16),
+                   ("D0", [4096], bf), ("MX", [4096], bf), ("S1", [CW], f32), ("KB", [CW], f32), ("DD", [CW], f32),
+                   ("SM", [24 * N24], f32), ("SI", [6 * N24], i32), ("SS", [NVB * 8, 16], bf), ("SR", [CW], bf), ("LS", [2 * NVB, 96], f32),
+                   ("MN", [2 * NVB, 96], f32), ("FS", [NVB * 8, 16], f32), ("FT", [NVB * 8, 16], f32), ("FL", [8, 16], f32),
+                   ("LL", [HN], u16), ("GL", [16 * HN], bf), ("FO", [4 * N24], f32)):
+    _sb(_n, _s, _d, 2)
+for _k in range(8):
+    SCRATCH["B%d" % _k] = ("psum", [128, 512], f32)
+DMAS = ["leaf", "tab", "fan", "req", "cel", "oyl", "oyt", "oyc"]
+SEMAPHORES = ["sP", "sT", "sV", "sA", "sent"] + ["d" + x for x in DMAS] + ["arr%d%d" % (r, k) for r in range(RO) for k in range(2)]
+CYC = 0.00104; PEC = 0.00052; LAG = 0.08; FIX = 0.06; GC = 1.56
+SLACK = 0.8; GAIN = 0.1; BIAS = 5.0; GP = 2
+
+
+def lut_columns():
+    out = {}
+    for n in (1, 2, 3, 4):
+        for g0 in range(4):
+            for g1 in range(3 if n > 1 else 1):
+                for g2 in range(2 if n > 2 else 1):
+                    pl = [g0, g0 + g1 + 1, g0 + g1 + g2 + 2, g0 + g1 + g2 + 3][:n]
+                    if pl[-1] > 3: continue
+                    s = QV.index(g0 + 3 * g1 + 2 * g2)
+                    for b in range(2):
+                        w = [0] * 9
+                        for m in range(8):
+                            mm = m + 8 * (1 - b)
+                            o = sum(((mm >> p) & 1) << k for k, p in enumerate(pl))
+                            if o < 8: w[o] += 1 << m
+                        out[(n, 5 * (s // 2) + 2 * (s % 2) + b)] = w
+    for n in range(5):
+        for row, val in ((4, 8 * (n <= 1)), (9, 8 * (n <= 2)), (14, n if n else 8)):
+            out[(n, row)] = [0] * 8 + [val]
+    return out
+
+
+def masks(T, topo, r):
+    src = T.cores[r]; dst = [T.cores[(r + d) % NR] for d in range(1, NR)]
+    eng = [topo.engines(src, x) for x in dst]; used = []; out = [0] * len(dst)
+    for size in sorted(set(len(e) for e in eng)):
+        who = [k for k in range(len(dst)) if len(eng[k]) == size]
+        free = [e for e in eng[who[0]] if e not in used]
+        n = 1
+        while 2 * n * len(who) <= len(free): n *= 2
+        for t, k in enumerate(who):
+            mine = free[t * n:(t + 1) * n]; used += mine; out[k] = sum(1 << e for e in mine)
+    return out
+
+
+def rank_program(g, core, T, topo):
+    rank = T.rank_of(core)
+    if rank is None:
+        return
+    Q = {"P": g, "T": g.tensor, "V": g.vector, "A": g.scalar, "S": g.sync}
+    ops = []; track = {}; runs = {}; grid = {}; sess = {}; place = {}; nb = [0]; cur = [0]
+    sl = slice
+
+    def ap(name, *idx):
+        shape = SCRATCH[name][1] if name[0] != "@" else [128, 512]
+        if name not in grid: grid[name] = np.arange(int(np.prod(shape[1:]))).reshape(shape[1:])
+        if not idx or not isinstance(idx[0], tuple): idx = ((0, 128),) + idx
+        cols = grid[name][idx[1:]].ravel() if len(idx) > 1 else grid[name].ravel()
+        return ((slice(idx[0][0], idx[0][1]),) + idx[1:], name, cols)
+
+    def op(eng, fn, reads, writes, cost, lat=0.0, sem=None, val=None):
+        me = len(ops); deps = {}
+        for acc, wr in ((reads, False), (writes, True)):
+            for a in acc:
+                name, cols = a[1], a[2]
+                if name not in track: track[name] = (np.full(grid[name].size, -1), [])
+                lastw, rd = track[name]
+                for d in np.unique(lastw[cols]): deps[int(d)] = 1
+                if wr:
+                    m = np.zeros(lastw.size, bool); m[cols] = True; keep = []
+                    for d, c in rd:
+                        hit = m[c]
+                        if hit.any(): deps[d] = 1
+                        if not hit.all(): keep.append((d, c))
+                    rd[:] = keep
+                if ps(a):
+                    if name[0] == "@" and me not in sess.setdefault(name, []): sess[name].append(me)
+                    st = runs.setdefault(name, [None, [], []]); lab = eng if eng != "F" else me
+                    if st[0] != lab: st[0], st[2], st[1] = lab, st[1], []
+                    for d in st[2]: deps[d] = 1
+                    if eng == "T" and st[1]: deps[st[1][-1]] = 1
+                    if me not in st[1]: st[1].append(me)
+        for a in reads: track[a[1]][1].append((me, a[2]))
+        for a in writes: track[a[1]][0][a[2]] = me
+        deps.pop(-1, None); deps.pop(me, None)
+        ops.append(dict(eng=eng, ch=cur[0], fn=fn, deps=list(deps), cost=cost, lat=lat, sem=sem, val=val))
+        return me
+
+    def ps(a): return a[1][0] == "@" or SCRATCH[a[1]][0] == "psum"
+    def dty(a): return f32 if ps(a) else SCRATCH[a[1]][2]
+    def two(*a): return all(dty(z) in (bf, u16, f16) for z in a)
+    def vc(n): return FIX + max(64, n) * CYC
+    def x(a): return T[place.get(a[1], a[1])][a[0]] if isinstance(a, tuple) else a
+    def cols(*a): return [b for b in a if isinstance(b, tuple)]
+    def bank():
+        nb[0] += 1
+        return "@%d" % nb[0]
+    def tsf(o, a, s1, op0, s2=None, op1=None):
+        if op1 is None: return lambda q: q.tensor_scalar(x(o), x(a), x(s1), None, op0)
+        return lambda q: q.tensor_scalar(x(o), x(a), x(s1), x(s2), op0, op1)
+    def c1(o, a): return vc(len(a[2]) * (0.5 if two(o, a) else 1))
+    def ts(o, a, s1, op0, s2=None, op1=None): op("V", tsf(o, a, s1, op0, s2, op1), [a] + cols(s1, s2), [o], c1(o, a))
+    def tt(o, a, b, f):
+        op("V", lambda q: q.tensor_tensor(x(o), x(a), x(b), f), [a, b], [o], vc(len(a[2]) * (1 if ps(a) or ps(b) else 2)))
+    def cp(o, a): op("V", lambda q: q.tensor_copy(x(o), x(a)), [a], [o], c1(o, a))
+    def ms(o, c): op("V", lambda q: q.memset(x(o), c), [], [o], c1(o, o))
+    def red(o, a): op("V", lambda q: q.tensor_reduce(x(o), x(a), AxisListType.X, A.add), [a], [o], vc(len(a[2])))
+    def scan(o, a, b, f0, f1):
+        op("V", lambda q: q.tensor_tensor_scan(x(o), x(a), x(b), 0.0, f0, f1), [a, b], [o], vc(len(a[2]) * (0.5 if two(o, a, b) else 1)))
+    def actf(o, a, f, bias, scale): return lambda q: q.activation(x(o), x(a), f, bias=x(bias), scale=x(scale))
+    def act(o, a, f, bias=0.0, scale=1.0): op("A", actf(o, a, f, bias, scale), [a] + cols(bias, scale), [o], vc(len(a[2])))
+    def either(o, a, fa, fv):
+        op("F", {"A": actf(o, a, *fa), "V": tsf(o, a, *fv)}, [a] + cols(*fa, *fv), [o], {"A": vc(len(a[2])), "V": c1(o, a)})
+    def lin(o, a, scale=1.0, bias=0.0): either(o, a, (F.Identity, bias, scale), (scale, A.mult, bias, A.add))
+    def relu(o, a, scale=1.0): either(o, a, (F.Relu, 0.0, scale), (scale, A.mult, 0.0, A.max))
+    def mm(o, l, r, start=False, stop=False):
+        n = max(min(64, len(l[2])), len(r[2])) * (4 if dty(l) == f32 else 1)
+        op("T", lambda q: q.matmul(x(o), x(l), x(r), start, stop), [l, r], [o], 0.02 + n * PEC)
+    def group(items, after=None):
+        first = len(ops)
+        for k, it in enumerate(items): mm(it[0], it[1], it[2], k == 0, k == len(items) - 1)
+        d = ops[first]["deps"]
+        for z in [z for o in ops[first + 1:] for z in o["deps"]] + [first if after is None else after]:
+            if z < first and z not in d: d.append(z)
+        return first
+    def sel(o, a, pat, base, fill, cmp=None, cm=1):
+        op("P", lambda q: q.affine_select(x(o), x(a), pat, A.not_equal if cmp is None else cmp, fill, base, cm), [a], [o], 0.2 + 2 * len(o[2]) * CYC)
+    def iota(o, pat, base, cm, fl=False):
+        fn = (lambda q: q.iota(x(o), pat, base, cm, allow_small_or_imprecise_dtypes=True)) if fl else (lambda q: q.iota(x(o), pat, base, cm))
+        op("P", fn, [], [o], 0.15 + 2 * len(o[2]) * CYC)
+    def gat(o, win, off, kind):
+        w = lambda: x(win).indirect(x(off)); c = 0.07 + GC * len(o[2]) * CYC
+        if kind == "any": op("F", {"V": lambda q: q.tensor_copy(x(o), w()), "A": lambda q: q.activation(x(o), w(), F.Copy)}, [win, off], [o], {"A": c, "V": c})
+        else: op("V", lambda q: q.tensor_scalar(x(o), w(), kind, None, A.min), [win, off], [o], c)
+    def dma(name, o, a, rd, wr, nbytes):
+        op("S", lambda q: q.dma_start(o, a), rd, wr, 0.08, lat=2.0 + nbytes / 150e3, sem="d" + name, val=16)
+    def M(name, *idx):
+        k = MATS.index(name) * 8
+        return ap("MT", sl(k, k + 8), *(idx or (sl(0, 16),)))
+    def bc(k): return ap("BC", sl(k, k + 1))
+
+    dma("leaf", T.INI[0:96, :], T.leaf0[:, :], [], [ap("INI")], 2e5)
+    dma("tab", T.INI[96:120, :], T.tab0[:, :], [], [], 5e4); tabop = len(ops) - 1
+    dma("fan", T.fanI[:, :], T.fan[:, :], [], [ap("fanI")], 3e4)
+    dma("req", T.RQ[:, :], T.req[:, :], [], [ap("RQ")], 1e5)
+    dma("cel", T.CE[:, :], T.cells[:, :], [], [ap("CE")], 2e6)
+
+    ms(ap("ZF"), 0.0); ms(ap("Z3"), 0.0); ms(ap("Z2"), 0.0)
+    sel(ap("I32"), ap("ZF"), [[-1, 128]], 0, 1.0)
+    iota(ap("TI"), [[1, 256]], 0, 0); iota(ap("PC", sl(0, 1)), [[0, 1]], 0, 1)
+    sel(ap("IW0"), ap("Z2"), [[-1, 160]], 16, 1.0)
+    Z3 = ap("Z3"); G0P = [[-16, 8], [0, 4]]; GP16 = [[-16, 8], [0, 16]]
+    def side(s): return sl(12, 16) if s == "A" else sl(3, 16, 4)
+    def pat(s, st): return [[-16, 8], [-st, 4], [0, 4]] if s == "A" else [[-16, 8], [0, 4], [-st, 4]]
+    def triv(name, s, row, w): sel(M(name, side(s)), ap("Z3", sl(0, 8), side(s)), G0P, -row, w)
+    for s, w in (("A", 1.0), ("B", -1.0)):
+        for k in range(4):
+            sel(M(s + str(k)), Z3, pat(s, 4), -k, w)
+            if k: triv(s + str(k), s, -1000, 0.0)
+        sel(M(s + "L"), M("A3") if s == "A" else Z3, pat(s, 1), -13, w); triv(s + "L", s, 12, w)
+    lin(M("I"), ap("I32")); lin(M("nI"), ap("I32"), -1.0)
+    for s in "AB":
+        sel(M("F" + s), Z3, pat(s, 5), -4, -8.0); triv("F" + s, s, 15, -8.0)
+    for qq in range(2):
+        for s in "AB":
+            h = M("H%s%d" % (s, qq))
+            sel(h, Z3, pat(s, 5), -2 * qq, 256.0); sel(h, h, pat(s, 5), -2 * qq - 1, 1.0)
+    for q in range(6):
+        for s in "AB":
+            z = "Z%s%d" % (s, q)
+            sel(M(z), M("H%s%d" % (s, q % 2)), GP16, -15, -65536.0 * QV[q] ** 2); triv(z, s, 15, float(TRIV[q][1]))
+    iota(ap("PI"), [[0, 8], [1, 16]], 0, 0, True)
+    sel(M("VK"), ap("PI"), GP16, -15, 0.0, A.is_equal)
+    sel(M("VK", sl(0, 15)), M("VK", sl(0, 15)), [[-16, 8], [-1, 15]], 0, 2.0 ** 25)
+    ms(ap("C32"), -32.0)
+    sel(M("RM"), ap("C32"), GP16, 0, 0.0, A.is_ge); sel(M("RM"), M("RM"), [[16, 8], [0, 16]], 15, 0.0, A.is_ge, -1)
+    lin(ap("BO"), M("RM", sl(0, 1)), -1.0); lin(ap("BOF"), M("RM", sl(0, 1)), -1.0 / 32)
+    iota(ap("QI", 0), [[0, 8], [1, 4], [0, 4]], 0, 0, True); iota(ap("QI", 1), [[0, 32], [1, 4]], 0, 0, True)
+    tt(ap("QI", sl(0, 2)), ap("QI", sl(0, 2)), ap("QI", sl(0, 2)), A.mult); tt(ap("QI", 2), ap("QI", 0), ap("QI", 1), A.add)
+    lin(ap("QI", 2), ap("QI", 2), -65536.0, 65536.0)
+    def ML(k, a=0, b=96): return ap("ML", sl(96 * k + a, 96 * k + b))
+    def z2(n): return ap("Z2", sl(0, n))
+    U = 2.0 ** -13; P24 = [[-16, 8], [0, 3]]
+    for i in range(4):
+        if i < 3:
+            sel(ML(i), z2(96), [[-1, 4], [-16, 8], [0, 3]], -4 * i, U); sel(ML(i, 72), ML(i, 72), P24, -13 - i, U)
+        else:
+            sel(ML(i), z2(96), [[0, 4], [-16, 8], [0, 3]], -12, U); sel(ML(i, 24, 72), z2(48), [[0, 48]], 1000, 0.0)
+        for s, none in ((0, 0.5), (1, 0.375)):
+            k = 4 + 2 * i + s
+            sel(ML(k), z2(96), [[0, 4], [-16, 8], [-4, 3]], -2 * s - 1, -2.0); sel(ML(k), ML(k), [[0, 4], [-16, 8], [-1, 3]], -12, 2.0)
+            if i: sel(ML(k), ML(k), [[0, 4], [-16, 8], [-4, 3]], -2 * s, 4.0 * i); sel(ML(k), ML(k), [[0, 4], [-16, 8], [0, 3]], -15, -2.0 * i * i)
+            if i < 3: sel(ML(k, 72), ML(k, 72), P24, -15, -2.0 * i * i - none)
+            else: sel(ML(k, 24, 72), ML(k, 24, 72), [[0, 2], [-16, 8], [0, 3]], -15, -18.0 + none)
+    sel(M("PB"), ap("QI", 2), GP16, -15, 0.0, A.is_equal)
+    for c in range(3):
+        n = "PN%d" % c
+        sel(M(n), M("PB"), GP16, -4 * c - 1, -65536.0); sel(M(n), M(n), GP16, -4 * c - 3, -65536.0)
+        for i in (1, 2, 3):
+            for o, view in ((0, sl(4 * i, 4 * i + 4)), (2, sl(i, 16, 4))): sel(M(n, view), M(n, view), G0P, -4 * c - o, 131072.0 * i)
+    ts(ap("PC", sl(1, 2)), ap("PC", sl(0, 1)), 15, A.bitwise_and); ts(ap("PC", sl(2, 3)), ap("PC", sl(0, 1)), 3, A.bitwise_and)
+    p16 = ap("PC", sl(1, 2))
+    ts(bc(0), p16, 12.0, A.is_ge); ts(bc(1), ap("PC", sl(2, 3)), 3.0, A.is_equal); ts(bc(2), p16, 15.0, A.is_equal)
+    for e, h in ((0, 0.5), (1, -0.5)):
+        lin(bc(3 + e), bc(0), -4096.0, h); lin(bc(5 + e), bc(1), 3072.0, h); lin(bc(7 + e), bc(0), -4096.0, bc(5 + e))
+    lin(ap("BC", sl(23, 29)), ap("BC", sl(3, 9)), -256.0); ms(bc(44), -128.0); ms(bc(45), 128.0); ms(bc(46), 3.0); ms(bc(47), 2.0 ** 29)
+    lin(bc(9), bc(1), 8192.0, 4096.0); lin(bc(9), bc(0), -4096.0, bc(9)); lin(bc(10), bc(0), -4096.0)
+    lin(bc(11), bc(2), 1.0, -1.0)
+    ts(bc(12), bc(0), bc(1), A.add, -7.0, A.mult); lin(bc(13), bc(2), 19.0, -4.0); lin(bc(12), bc(12), 1.0, bc(13))
+    lin(bc(14), bc(0), TRIV0); lin(bc(15), bc(1), TRIV0)
+    for k, s in enumerate("AB"):
+        for q in range(6):
+            c = bc(32 + 6 * k + q)
+            lin(c, bc(k), TRIV[q][0] - 131072.0 * QV[q], 131072.0 * QV[q]); lin(M("D%s%d" % (s, q)), M("I"), c)
+    for w in range(3):
+        ts(bc(16), p16, 5.0 * w, A.is_ge); ts(bc(29 + w), p16, 5.0 * w + 5, A.is_lt, bc(16), A.mult)
+        lin(ap("IW", sl(160 * w, 160 * w + 160)), ap("IW0"), bc(29 + w))
+    ms(ap("RS"), 0.0); ms(ap("RS", sl(0, CW, 16)), 2.0 ** 34); ms(ap("RR"), 0.0); ms(ap("RR", sl(15, CW, 16)), 2.0 ** 34)
+    ms(ap("PF"), 0.0); lc = lut_columns(); seen = {}; fills = []
+    for (n, row), w in sorted(lc.items()):
+        for j in range(3):
+            val = w[3 * j] + (w[3 * j + 1] << 8) + (w[3 * j + 2] << 16)
+            if val: seen.setdefault((j, val), []).append(16 * n + row)
+    def fill(o, v):
+        z = ap("ZF", (o[0][0].start, o[0][0].stop), sl(0, len(o[2])))
+        op("F", {"A": actf(o, z, F.Identity, v, 1.0), "V": lambda q: q.memset(x(o), v)}, [z, o], [], {"A": vc(1), "V": vc(1)})
+        fills.append(len(ops) - 1)
+    for (j, val), cs in sorted(seen.items()):
+        while cs:
+            st = cs[1] - cs[0] if len(cs) > 1 else 1; k = 1
+            while k < len(cs) and cs[k] - cs[k - 1] == st: k += 1
+            fill(ap("PF", (32 * j, 32 * j + 32), sl(cs[0], cs[k - 1] + 1, st)), float(val))
+            cs = cs[k:]
+    pl = ap("PL"); cp(pl, ap("PF")); ops[-1]["deps"] += fills
+    ts(ap("PS", sl(0, 80)), pl, 255, A.bitwise_and)
+    ts(ap("PS", sl(80, 160)), pl, 8, A.logical_shift_right, 255, A.bitwise_and); ts(ap("PS", sl(160, 240)), pl, 16, A.logical_shift_right)
+    ms(ap("ROW"), 0.0); del fills[:]
+    for k in range(8): fill(ap("ROW", sl(32 * (k // 3) + k % 3, 32 * (k // 3) + k % 3 + 1)), 2.0 ** -k)
+    tt(ap("TMP", sl(0, 96)), ap("ROW"), ap("I32", sl(0, 96)), A.mult); ops[-1]["deps"] += fills; red(bc(18), ap("TMP", sl(0, 96)))
+    i66 = ap("I32", sl(66, 67))
+    lin(bc(19), bc(18), 0.5, -0.5); lin(bc(19), i66, 1.5, bc(19))
+    for y in range(3): red(bc(20 + y), ap("I32", sl(y, 96, 32)))
+    lin(bc(22), i66, -0.875, bc(22))
+    for y in range(3): ts(ap("PM", sl(80 * y, 80 * y + 80)), ap("PS", sl(80 * y, 80 * y + 80)), bc(20 + y), A.mult)
+    tt(ap("PM", sl(240, 320)), ap("PM", sl(0, 80)), ap("PM", sl(80, 160)), A.add); tt(ap("WC"), ap("PM", sl(240, 320)), ap("PM", sl(160, 240)), A.add)
+    for k in range(8): lin(ap("WL", sl(0, 5), k, sl(0, 16)), ap("WC"))
+    ts(ap("TJ"), ap("TI"), bc(18), A.mult, bc(19), A.add); ts(ap("TJ"), ap("TJ"), 1, A.bitwise_and); cp(ap("BT"), ap("TJ"))
+    for n0 in (0, 2, 4):
+        ns = [n for n in (n0, n0 + 1) if n < 5]; bn = bank()
+        group([(ap(bn, sl(256 * (n - n0), 256 * (n - n0) + 256)), ap("WL", n), ap("BT")) for n in ns])
+        lin(ap("LUT", sl(256 * n0, 256 * (ns[-1] + 1))), ap(bn, sl(0, 256 * len(ns))))
+    cp(ap("L0"), ap("fanI"))
+    for w in range(3):
+        for s in range(2): ts(ap("LW3", sl(0, NCH), 2 * w + s), ap("fanI", sl(32 * s, 32 * s + 32)), 3.0, A.mult, float(w), A.add)
+    cp(ap("LWL"), ap("LW3"))
+    for p in range(16): lin(ap("D1", sl(2 * p + 1, 32 * V, 32)), ap("RQ"))
+    for b in range(2):
+        b = str(b)
+        ms(ap("SS" + b), 0.0); ms(ap("SS" + b, sl(0, NVB * 8), sl(15, 16)), 1.0); ms(ap("FT" + b), 0.0); ms(ap("FL" + b), 0.0)
+        ms(ap("D0" + b, sl(0, 4096, 2)), -1.0)
+    op("V", lambda q: q.tensor_copy(T.INF[0:120, :], T.INI[0:120, :]), [ap("INI")], [ap("INF")], vc(512)); ops[-1]["deps"].append(tabop)
+
+    def sm(b, k, n=1): return ap("SM" + b, sl(k * N24, (k + n) * N24))
+    def si(b, k): return ap("SI" + b, sl(k * N24, (k + 1) * N24))
+    def prep(rnd, ch, b):
+        v0 = ch * CW; w0, wb = "W0%d" % rnd, "WB%d" % rnd
+        fs = lambda a, c, d=1: ap("FS" + b, sl(0, NVB * 8), sl(a, c, d))
+        own = ap("SM" + b, sl(22 * N24 + ch // 2 * NVB * 8, 22 * N24 + (ch // 2 + 1) * NVB * 8))
+        if rnd == 0:
+            t = ap("TMP", sl(96 + ch * NVB * 8, 96 + (ch + 1) * NVB * 8))
+            iota(t, [[128, NVB], [0, 8]], V * rank + v0, 1, True); lin(own, t, U)
+            tt(sm(b, 0, 4), sm(b, 0, 4), sm(b, 4, 4), A.max)
+        else: tt(sm(b, 1, 2), sm(b, 1, 2), sm(b, 5, 2), A.max)
+        lin(fs(12, 13), own)
+        for k in range(4): lin(fs(k, 12, 4), sm(b, k))
+        lin(sm(b, 8, 3), sm(b, 4, 3), 4.0); tt(sm(b, 12, 3), sm(b, 0, 3), sm(b, 8, 3), A.subtract)
+        lin(sm(b, 15), sm(b, 7), -1.0, 1.0)
+        tt(sm(b, 16, 2), sm(b, 12, 2), sm(b, 14, 2), A.max); tt(sm(b, 16), sm(b, 16), sm(b, 17), A.max); tt(fs(13, 16), sm(b, 16), sm(b, 4), A.max)
+        ts(si(b, 1), si(b, 0), 255, A.bitwise_and); ts(si(b, 2), si(b, 0), 8, A.logical_shift_right)
+        tt(ap("FT" + b, sl(0, NVB * 8), sl(0, 15, 5)), si(b, 2), sm(b, 15), A.mult)
+        tt(sm(b, 18, 2), sm(b, 4, 2), sm(b, 6, 2), A.add); tt(sm(b, 18), sm(b, 18), sm(b, 19), A.add)
+        lin(sm(b, 18), sm(b, 18), -256.0, 1024.0); tt(sm(b, 19), sm(b, 18), si(b, 1), A.add)
+        for h in range(HH):
+            for vb in range(NVB):
+                r = (h * NVB + vb) * 4
+                lin(ap("FL" + b, (h * HN, (h + 1) * HN), sl(0, 8), sl(r, r + 3)), ap("SM" + b, (h * HN, (h + 1) * HN), sl(19 * N24 + 24 * vb, 19 * N24 + 24 * vb + 24)))
+        bn = bank()
+        group([(ap(bn, sl(vb * 128, vb * 128 + 128)), ap("FS" + b, sl(vb * 8, vb * 8 + 8)), ap("I32")) for vb in range(NVB)])
+        lin(ap(w0, sl(v0, v0 + CW)), ap(bn, sl(0, CW)), 8192.0)
+        bn = bank()
+        group([(ap(bn, sl(0, HN)), ap("FL" + b), ap("I32", sl(h * HN, (h + 1) * HN))) for h in range(HH)])
+        cp(ap("LL" + b), ap(bn, sl(0, HN)))
+        gat(ap("GL" + b), ap("LUT"), ap("LL" + b), "any")
+        for w in range(3):
+            bn = bank()
+            it = [(ap(bn, sl(vb * 128 + h * HN, vb * 128 + (h + 1) * HN)), ap("IW", sl(160 * w + 16 + 5 * w - 5 * c, 160 * w + 144 + 5 * w - 5 * c)),
+                   ap("GL" + b, sl((h * NVB + vb) * 4 + c, 16 * HN, 16))) for vb in range(NVB) for h in range(HH) for c in range(3)]
+            if w == 0: it += [(ap(bn, sl(vb * 128, vb * 128 + 128)), ap("FT" + b, sl(vb * 8, vb * 8 + 8)), ap("I32")) for vb in range(NVB)]
+            group(it)
+            lin(ap(wb, sl(3 * v0 + w, 3 * (v0 + CW), 3)), ap(bn, sl(0, CW)), 1.0, bc(2))
+        if v0 < G <= v0 + CW:
+            for kind, name, m in ((0, w0, 1), (1, wb, 3)):
+                def send(q, kind=kind, name=name, m=m):
+                    tr = []
+                    for d in range(1, NR):
+                        rid, pid, se = topo.addr(T.cores[(rank + d) % NR]); o = m * (V + (d - 1) * G)
+                        tr.append(RemoteDMATransfer(dst_ids=[DstId(rid=rid, pnc=pid)], dma_engine_mask=masks(T, topo, rank)[d - 1],
+                                                    remote_sem=T.sem["arr%d%d" % (rnd, kind)], src=T[name][:, 0:m * G], dst=T[name][:, o:o + m * G]))
+                    q.remote_dma_fused(tr, local_sem=T.sem.sent)
+                op("P", send, [ap(name, sl(0, m * G))], [], 1.0, sem="none")
+                me = len(ops) - 1
+                n = sum(bin(masks(T, topo, (rank - d) % NR)[d - 1]).count("1") for d in range(1, NR))
+                op("X", None, [], [ap(name, sl(m * V, m * W))], 0.0, lat=5.0 + 3.0 * kind, sem="arr%d%d" % (rnd, kind), val=n)
+                ops[-1]["deps"].append(me)
+
+    for ch in range(NCH):
+        b = str(ch % 2); kb = bank()
+        group([(ap(kb, sl(k * N24 + vb * 24, k * N24 + vb * 24 + 24)), ap("INF", (0, 120), sl(ch * CW + vb * 128, ch * CW + vb * 128 + 128)),
+                ap("I32", (0, 120), sl(k, 96, 4) if k < 4 else sl(96, 120))) for vb in range(NVB) for k in range(5)])
+        lin(sm(b, 0, 4), ap(kb, sl(0, 4 * N24)), U); ts(sm(b, 4, 4), ap(kb, sl(0, 4 * N24)), 0.0, A.is_lt)
+        cp(si(b, 0), ap(kb, sl(4 * N24, 5 * N24)))
+        prep(0, ch, b)
+
+    CL = [(1, 0), (2, 0), (0, 1), (0, 2), (1, 1), (1, 2), (2, 1), (2, 2), (0, 0)]
+    H0, H1, H2 = sl(0, CW), sl(CW, 2 * CW), sl(0, 2 * CW)
+    for rnd in range(RO):
+        last = rnd == RO - 1; w0, wb = "W0%d" % rnd, "WB%d" % rnd
+        for ch in range(NCH):
+            b = str(ch % 2); kb = "B%d" % (6 + ch % 2); v0 = ch * CW; cur[0] = ch
+            ga, gb = ap("G0" + b, H0), ap("G0" + b, H1)
+            gat(ga, ap(w0), ap("L0", sl(ch * LW, (ch + 1) * LW)), 4096.0); gat(gb, ap(w0), ap("L0", sl(32 + ch * LW, 32 + (ch + 1) * LW)), 3072.0)
+            for w in range(3):
+                gat(ap("GW" + b, sl(2 * w * CW, 2 * (w + 1) * CW)), ap(wb), ap("LWL", sl((6 * ch + 2 * w) * LW, (6 * ch + 2 * w + 2) * LW)), "any")
+            gw = lambda w, s: ap("GW" + b, sl((2 * w + s) * CW, (2 * w + s + 1) * CW))
+            for t, bias in ((0, 3), (2, 5), (4, 7), (6, 7), (8, None)):
+                bn = bank(); cs = CL[t:t + 2]; it = []
+                for u, (k, l) in enumerate(cs): it += [(ap(bn, (H0, H1)[u]), M("A%d" % k), ga), (ap(bn, (H0, H1)[u]), M("B%d" % l), gb)]
+                group(it)
+                for e, name in ((0, "SG"), (1, "SE")):
+                    either(ap(name + b, sl(t * CW, (t + len(cs)) * CW)), ap(bn, sl(0, len(cs) * CW)),
+                           (F.Sigmoid, bc(44 + e) if bias is None else bc(20 + bias + e), 256.0), ((0.5, -0.5)[e] if bias is None else bc(bias + e), A.is_gt))
+            bn = bank()
+            group([(ap(bn, H0), M("AL"), ga), (ap(bn, H0), M("B3"), gb), (ap(bn, H1), M("A3"), ga), (ap(bn, H1), M("BL"), gb)])
+            ts(ap("EQ" + b, H0), ap(bn, H0), bc(9), A.is_equal); ts(ap("EQ" + b, H1), ap(bn, H1), bc(10), A.is_equal)
+            sg = lambda k, l: ap("SG" + b, sl(CL.index((k, l)) * CW, (CL.index((k, l)) + 1) * CW))
+            se = lambda k, l: ap("SE" + b, sl(CL.index((k, l)) * CW, (CL.index((k, l)) + 1) * CW))
+            for k in (1, 2):
+                bn = bank(); it = [(ap(bn, H0), M("FA"), gw(k - 1, 0)), (ap(bn, H1), M("FB"), gw(k - 1, 1))]
+                for l in range(3):
+                    it += [(ap(bn, H0), M("I"), sg(k, l)), (ap(bn, H1), M("I"), sg(l, k - 1))]
+                for l in range(3):
+                    it += [(ap(bn, H0), M("nI"), se(k - 1, l)), (ap(bn, H1), M("nI"), se(l, k))]
+                group(it)
+                relu(ap("R12" + b, sl((k - 1) * 2 * CW, k * 2 * CW)), ap(bn, H2), (3.0, 2.0)[k - 1])
+            bn = bank(); it = [(ap(bn, H1), M("nI"), se(l, 0)) for l in range(3)] + [(ap(bn, H0), M("I"), sg(0, l)) for l in range(3)]
+            it += [(ap(bn, (H0, H1)[s]), M("I"), ap("R12" + b, sl((2 * k + s) * CW, (2 * k + s + 1) * CW))) for k in range(2) for s in range(2)]
+            group(it); lin(ap("IX" + b, H0), ap(bn, H0)); lin(ap("IX" + b, H1), ap(bn, H1), 1.0, bc(46))
+            bn = bank(); it = [(ap(bn, H0), M("FA"), gw(2, 0)), (ap(bn, H0), M("FB"), gw(2, 1))]
+            it += [(ap(bn, H0), M("nI"), sg(k, l)) for k, l in CL] + [(ap(bn, H0), M("I"), se(k, l)) for k, l in CL]
+            it += [(ap(bn, H0), M("I"), ap("EQ" + b, h)) for h in (H0, H1)]
+            group(it); act(ap("VD" + b), ap(bn, H0), F.Relu, bc(12), bc(11))
+            prev = None
+            for q in range(6):
+                bn = bank(); it = []
+                for s, h in ((0, H0), (1, H1)):
+                    it += [(ap(bn, h), M("Z%s%d" % ("AB"[s], q)), gw(q // 2, s)), (ap(bn, h), M("D%s%d" % ("AB"[s], q)), ap("IX" + b, h))]
+                prev = group(it, prev)
+                if q == 0:
+                    for s, h in ((0, H0), (1, H1)): lin(ap("AC" + b, h), ap(bn, h), 1.0, bc(14 + s))
+                else: tt(ap(("EI" if q == 5 else "AC") + b), ap(bn, H2), ap("AC" + b), A.max)
+            for e, mk in ((0, 0x5555), (1, 0xAAAA)):
+                ts(ap("ME" + b, sl(2 * e * CW, 2 * (e + 1) * CW)), ap("EI" + b), mk, A.bitwise_and)
+            for e, mk in ((0, 0x5555), (1, 0xAAAA)):
+                tt(ap("EI" + b, (H0, H1)[e]), ap("ME" + b, sl(2 * e * CW, (2 * e + 1) * CW)), ap("ME" + b, sl((2 * e + 1) * CW, (2 * e + 2) * CW)), A.add)
+                ts(ap("EI" + b, (H0, H1)[e]), ap("EI" + b, (H0, H1)[e]), 1, A.logical_shift_right, mk, A.bitwise_and)
+            nf = ap("NF" + b)
+            tt(nf, ap("EI" + b, H0), ap("EI" + b, H1), A.add)
+            ts(ap("C2" + b), nf, -0.125, A.mult, 65531.5 / 8, A.add)
+            ts(ap("T5" + b), nf, -1.0 / 32, A.mult, 65519.5 / 32, A.add)
+            bn = bank(); ts(ap(bn, H0), ap("T5" + b), 29.0, A.mult, 65535.0, A.add)
+            tt(ap("T5" + b), ap(bn, H0), nf, A.subtract); ts(ap("T5" + b), ap("T5" + b), 8191, A.bitwise_and); cp(ap("C1" + b), ap("T5" + b))
+            blk = lambda name, vb, o=0, p=(0, 128): ap(name, p, sl(o + vb * 128, o + vb * 128 + 128))
+            it = [(blk(kb, vb), blk("VD" + b, vb), M("VK")) for vb in range(NVB)]
+            if last: it += [(blk(kb, vb), blk("RQ", vb, v0), M("RM")) for vb in range(NVB)]
+            for k, t in enumerate(it): mm(t[0], t[1], t[2], k == 0, False)
+            for vb in range(NVB):
+                r = str((ch * NVB + vb) % 2); o = 32 * (v0 + vb * 128); m = 128 // GP
+                for h in range(GP):
+                    c = sl(vb * 128 + h * m, vb * 128 + (h + 1) * m); lo, hi = 32 * h * m, 32 * (h + 1) * m
+                    gat(ap("D0" + r, sl(lo + 1, hi, 2)), ap("CE"), ap("C2" + b, c), "any"); gat(ap("D1", sl(o + lo, o + hi, 2)), ap("CE"), ap("C1" + b, c), "any")
+                    scan(ap("MX" + r, sl(lo, hi)), ap("D0" + r, sl(lo, hi)), ap("D1", sl(o + lo, o + hi)), A.min, A.max)
+                for p in range(16):
+                    mm(ap(kb, sl(vb * 128 + p, vb * 128 + 128, 16)), ap("MX" + r, sl(2 * p + 1, 4096, 32)), ap("BO"), False, p == 15 and vb == NVB - 1)
+            key = ap(kb, H0); rv = sl(CW - 1, None, -1); s1 = "S1" + b
+            for c in range(3):
+                scan(ap(s1), ap("RS"), key, A.add, A.min)
+                if c < 2:
+                    scan(ap("KB" + b, rv), ap("RR", rv), ap(s1, rv), A.add, A.min)
+                    tt(ap("DD" + b), key, ap("KB" + b), A.subtract)
+                    either(ap("DD" + b), ap("DD" + b), (F.Relu, bc(47), -2.0 ** 25), (16.0, A.is_lt, 2.0 ** 26, A.mult)); tt(key, key, ap("DD" + b), A.add)
+                lin(ap("SM" + b, sl(12 * N24 + c, 13 * N24, 3)), ap(s1, sl(15, CW, 16)))
+            ts(si(b, 3), sm(b, 12), 2.0 ** 25, A.min); ts(sm(b, 13), sm(b, 12), 2.0 ** 24, A.is_ge)
+            ts(si(b, 4), si(b, 3), 2, A.logical_shift_right, 3, A.bitwise_and); ts(si(b, 5), si(b, 3), 3, A.bitwise_and)
+            ss = lambda a, c, d=1: ap("SS" + b, sl(0, NVB * 8), sl(a, c, d))
+            for s in range(2):
+                cp(ss(2 * s, 12, 4), si(b, 4 + s)); act(ss(2 * s + 1, 12, 4), ss(2 * s, 12, 4), F.Square)
+            lin(ss(12, 15), sm(b, 13))
+            bn = bank(); prev = None
+            group([(blk(bn, vb), ap("SS" + b, sl(vb * 8, vb * 8 + 8)), M("I")) for vb in range(NVB)])
+            lin(ap("SR" + b), ap(bn, H0))
+            xn = [("AC" + b, 0), ("AC" + b, CW), ("KB" + b, 0)]
+            for c in range(3):
+                bn = bank(); group([(ap(bn, H0), M("PN%d" % c), ap("SR" + b))])
+                tt(ap(xn[c][0], sl(xn[c][1], xn[c][1] + CW)), ap(bn, H0), nf, A.min)
+            bn = bank()
+            group([(ap(bn, sl(vb * 24 + c, vb * 24 + 24, 3)), blk(xn[c][0], vb, xn[c][1]), ap("BOF")) for c in range(3) for vb in range(NVB)])
+            ts(si(b, 0), ap(bn, sl(0, N24)), -1.0, A.mult, 65535.0, A.add); ts(si(b, 0), si(b, 0), 65535, A.bitwise_and)
+            for i in range(4):
+                bn = bank(); it = []
+                for s in range(2):
+                    for vb in range(NVB):
+                        o = ap(bn, sl((s * NVB + vb) * 96, (s * NVB + vb + 1) * 96))
+                        it += [(o, blk("G0" + b, vb, s * CW), ML(i)), (o, blk("SR" + b, vb), ML(4 + 2 * i + s))]
+                prev = group(it, prev); o = ap(bn, sl(0, 2 * NVB * 96))
+                if i == 0: lin(ap("LS" + b), o)
+                else: tt(ap("LS" + b), o, ap("LS" + b), A.max)
+            sa, sb = sl(0, NVB), sl(NVB, 2 * NVB)
+            tt(ap("MN" + b, sa, sl(0, 72)), ap("LS" + b, sa, sl(0, 72)), ap("LS" + b, sb, sl(0, 72)), A.min)
+            tt(ap("MN" + b, sb), ap("LS" + b, sa), ap("LS" + b, sb), A.max)
+            mn = lambda k: ap("MN" + b, sa, sl(24 * k, 24 * k + 24))
+            mx = lambda k: ap("MN" + b, sb, sl(24 * k, 24 * k + 24))
+            def above(o, a, u): tt(o, a, u, A.is_le); tt(o, o, a, A.max)
+            lin(sm(b, 0), mn(0)); lin(sm(b, 15), mn(2))
+            above(sm(b, 14), mx(0), mn(0)); tt(sm(b, 1), sm(b, 14), mn(1), A.min)
+            above(sm(b, 16), mx(0), sm(b, 1)); above(sm(b, 17), mx(1), sm(b, 1)); above(sm(b, 18), mn(1), sm(b, 1))
+            tt(sm(b, 19, 2), sm(b, 15, 2), sm(b, 17, 2), A.min); tt(sm(b, 2), sm(b, 19), sm(b, 20), A.min)
+            above(sm(b, 3), mx(3), sm(b, 2))
+            ts(sm(b, 4, 4), sm(b, 0, 4), 0.3, A.is_ge)
+            if not last:
+                prep(rnd + 1, ch, b)
+            else:
+                lin(sm(b, 8, 4), sm(b, 0, 4), 1.0, U); lin(sm(b, 4, 4), sm(b, 4, 4), -1.0, 1.0)
+                for k in range(4): tt(ap("FO" + b, sl(k, 4 * N24, 4)), sm(b, 8 + k), sm(b, 4 + k), A.mult)
+                lin(sm(b, 14), sm(b, 13), -1.0, 1.0); tt(sm(b, 15), si(b, 0), sm(b, 14), A.mult)
+                ts(si(b, 4), si(b, 3), 5, A.logical_shift_right); tt(sm(b, 16), si(b, 4), sm(b, 14), A.mult); tt(sm(b, 16), sm(b, 16), sm(b, 13), A.subtract)
+                bn = bank(); kb = bank()
+                group([(blk(bn, vb, 0, (0, 96)), ap("FO" + b, sl(vb * 96, vb * 96 + 96)), ap("I32")) for vb in range(NVB)])
+                lin(ap("INF", (0, 96), sl(v0, v0 + CW)), ap(bn, (0, 96), H0), 8192.0, -1.0)
+                group([(blk(kb, vb, u * CW, (0, 24)), ap("SM" + b, sl((15 + u) * N24 + vb * 24, (15 + u) * N24 + vb * 24 + 24)), ap("I32")) for u in range(2) for vb in range(NVB)])
+                lin(ap("W00", (0, 24), sl(256 + v0, 256 + v0 + CW)), ap(kb, (0, 24), H0)); lin(ap("OC", (0, 24), sl(v0, v0 + CW)), ap(kb, (0, 24), H1))
+    dma("oyt", T.yt[:, :], T.W00[0:24, 256:256 + V], [ap("W00", sl(256, 256 + V))], [], 5e4); dma("oyc", T.yc[:, :], T.OC[0:24, :], [ap("OC")], [], 5e4)
+    dma("oyl", T.yl[:, :], T.INF[0:96, :], [ap("INF")], [], 2e5)
+
+    n = len(ops); succ = [[] for _ in ops]
+    for k, o in enumerate(ops):
+        for d in o["deps"]: succ[d].append(k)
+    def lag(d, k): return ops[d]["lat"] + (0.0 if ops[d]["eng"] == ops[k]["eng"] == "T" else LAG)
+    def cost(k): return ops[k]["cost"]["A"] if ops[k]["eng"] == "F" else ops[k]["cost"]
+    pri = [0.0] * n
+    for k in range(n - 1, -1, -1): pri[k] = cost(k) + max([lag(k, s) + pri[s] for s in succ[k]] + [ops[k]["lat"]])
+    pri = [p - BIAS * o["ch"] for p, o in zip(pri, ops)]
+    for k, o in enumerate(ops):
+        if o["eng"] == "P": pri[k] = 1e6 if o["sem"] or k < 20 or o["cost"] < 0.19 else -k
+    opens = {v[0]: name for name, v in sess.items()}; member = {}
+    for name, v in sess.items():
+        for k in v: member.setdefault(k, []).append(name)
+    todo = {name: len(v) for name, v in sess.items()}
+    banks = {"B%d" % k: [None, 0.0] for k in range(6)}
+    left = [len(o["deps"]) for o in ops]; rdy = [0.0] * n; free = dict.fromkeys("PTVASX", 0.0); pool = {e: [] for e in "PTVASXF"}; order = []
+    for k in range(n):
+        if not left[k]: pool[ops[k]["eng"]].append(k)
+    while len(order) < n:
+        idle = [(v[1], name) for name, v in banks.items() if v[0] is None or not todo[v[0]]]
+        tb = min(idle)[0] + LAG if idle else 1e9
+        when = lambda k: max(rdy[k], tb) if k in opens else rdy[k]
+        best = None
+        for e in free:
+            own = pool[e]; c = own + pool["F"] if e == "A" else own
+            if e == "V":
+                to = min([max(free[e], when(k)) for k in own] + [1e9])
+                c = own + [k for k in pool["F"] if max(free[e], when(k)) + ops[k]["cost"]["V"] <= min(to + SLACK, max(free["A"], when(k)) + ops[k]["cost"]["A"] - GAIN)]
+            if not c: continue
+            t = max(free[e], min(when(k) for k in c))
+            if best is None or t < best[0]: best = (t, e, c)
+        t, e, c = best
+        k = max((k for k in c if when(k) <= t + 0.03), key=lambda k: pri[k]); o = ops[k]
+        pool[o["eng"]].remove(k); t = max(t, when(k))
+        if o["eng"] == "F": o["eng"], o["fn"], o["cost"] = e, o["fn"][e], o["cost"][e]
+        if k in opens:
+            name = min(idle)[1]; old = banks[name][0]
+            for d in (sess[old] if old else []):
+                if d not in o["deps"]: o["deps"].append(d); succ[d].append(k)
+            banks[name][0] = opens[k]; place[opens[k]] = name
+        free[e] = t + o["cost"]; order.append(k); o["t"] = t
+        for name in member.get(k, []):
+            todo[name] -= 1; banks[place[name]][1] = max(banks[place[name]][1], free[e])
+        for s in succ[k]:
+            rdy[s] = max(rdy[s], free[e] + lag(k, s)); left[s] -= 1
+            if not left[s]: pool[ops[s]["eng"]].append(s)
+    cnt = dict.fromkeys("PTVA", 0); total = {}
+    for k in order:
+        o = ops[k]
+        if o["sem"] is None and any(not (o["eng"] == ops[s]["eng"] == "T") for s in succ[k]):
+            cnt[o["eng"]] += 1; o["sem"], o["val"], o["inc"] = "s" + o["eng"], cnt[o["eng"]], 1
+        elif o["eng"] == "S": o["inc"] = 16
+        if o["val"] is not None: total[o["sem"]] = o["val"]
+    seen = {e: {} for e in Q}
+    for k in order:
+        o = ops[k]; e = o["eng"]
+        if e == "X": continue
+        need = {}
+        for d in o["deps"]:
+            p = ops[d]
+            if p["eng"] == e == "T": continue
+            need[p["sem"]] = max(need.get(p["sem"], 0), p["val"])
+        for s, v in need.items():
+            if seen[e].get(s, 0) < v: Q[e].wait_ge(T.sem[s], v); seen[e][s] = v
+        ins = o["fn"](Q[e])
+        if "inc" in o: ins.then_inc(T.sem[o["sem"]], o["inc"])
+    total["sent"] = 2 * RO * sum(bin(m).count("1") for m in masks(T, topo, rank))
+    for s, v in total.items(): g.wait_ge(T.sem[s], v)
+    return ops, order

@@ -9,8 +9,8 @@ CW = V // NCH; NVB = CW // 128; HH = 4 // NVB; HN = 128 // HH; N24 = NVB * 24; L
 QV = (0, 1, 2, 3, 4, 6)
 TRIV = ((-65536, 0), (-820, 118784), (61696, 3824), (69632, -12544), (0, -131072), (0, -131072))
 TRIV0 = 174762.0
-MATS = ["I", "nI", "A0", "A1", "A2", "A3", "AL", "B0", "B1", "B2", "B3", "BL", "FA", "FB", "HA0", "HA1", "HB0", "HB1", "VK", "RM", "PB", "PN0", "PN1", "PN2"] \
-    + ["Z%s%d" % (s, q) for s in "AB" for q in range(6)] + ["D%s%d" % (s, q) for s in "AB" for q in range(6)]
+MATS = ["I", "nI", "I3", "I2", "A0", "A1", "A2", "A3", "AL", "B0", "B1", "B2", "B3", "BL", "FA", "FB", "HA0", "HA1", "HB0", "HB1", "VK", "RM",
+        "PB", "PN0", "PN1", "PN2"] + ["Z%s%d" % (s, q) for s in "AB" for q in range(6)] + ["D%s%d" % (s, q) for s in "AB" for q in range(6)]
 f32, bf, i32, u16, f16 = "float32", "bfloat16", "int32", "uint16", "float16"
 SCRATCH = {}
 def _sb(name, shape, dt, per=1):
@@ -27,6 +27,7 @@ for _n, _s, _d in (("MT", [len(MATS) * 8, 16], bf), ("ML", [12 * 96], bf), ("Z3"
     _sb(_n, _s, _d)
 for _n, _s, _d in (("W0", [W], f32), ("WB", [3 * W], bf),
                    ("G0", [2 * CW], f16), ("GW", [6 * CW], bf), ("SG", [9 * CW], bf), ("SE", [9 * CW], bf), ("EQ", [2 * CW], bf),
+                   ("FG", [2 * CW], bf), ("RW", [2 * CW], bf),
                    ("R12", [4 * CW], bf), ("IX", [2 * CW], bf), ("VD", [CW], bf), ("AC", [2 * CW], f32), ("EI", [2 * CW], i32),
                    ("ME", [4 * CW], i32), ("NF", [CW], f32), ("T5", [CW], i32), ("C1", [CW], u16), ("C2", [CW], u16),
                    ("D0", [4096], bf), ("MX", [4096], bf), ("S1", [CW], f32), ("KB", [CW], f32), ("DD", [CW], f32),
@@ -38,8 +39,8 @@ for _k in range(8):
     SCRATCH["B%d" % _k] = ("psum", [128, 512], f32)
 DMAS = ["leaf", "tab", "fan", "req", "cel", "oyl", "oyt", "oyc"]
 SEMAPHORES = ["sP", "sT", "sV", "sA", "sent"] + ["d" + x for x in DMAS] + ["arr%d%d" % (r, k) for r in range(RO) for k in range(2)]
-CYC = 0.00104; PEC = 0.00052; LAG = 0.08; FIX = 0.06; GC = 1.56
-SLACK = 0.8; GAIN = 0.1; BIAS = 5.0; GP = 2
+CYC = 0.00083; PEC = 0.00042; LAG = 0.08; FIX = 0.045; GC = 1.56
+SLACK = 0.6; GAIN = 0.3; BIAS = 1.0; TB = 12.0; GP = 2
 
 
 def lut_columns():
@@ -58,9 +59,6 @@ def lut_columns():
                             o = sum(((mm >> p) & 1) << k for k, p in enumerate(pl))
                             if o < 8: w[o] += 1 << m
                         out[(n, 5 * (s // 2) + 2 * (s % 2) + b)] = w
-    for n in range(5):
-        for row, val in ((4, 8 * (n <= 1)), (9, 8 * (n <= 2)), (14, n if n else 8)):
-            out[(n, row)] = [0] * 8 + [val]
     return out
 
 
@@ -82,7 +80,7 @@ def rank_program(g, core, T, topo):
     if rank is None:
         return
     Q = {"P": g, "T": g.tensor, "V": g.vector, "A": g.scalar, "S": g.sync}
-    ops = []; track = {}; runs = {}; grid = {}; sess = {}; place = {}; nb = [0]; cur = [0]
+    ops = []; track = {}; runs = {}; grid = {}; sess = {}; place = {}; nb = [0]; cur = [0, 0]
     sl = slice
 
     def ap(name, *idx):
@@ -117,7 +115,7 @@ def rank_program(g, core, T, topo):
         for a in reads: track[a[1]][1].append((me, a[2]))
         for a in writes: track[a[1]][0][a[2]] = me
         deps.pop(-1, None); deps.pop(me, None)
-        ops.append(dict(eng=eng, ch=cur[0], fn=fn, deps=list(deps), cost=cost, lat=lat, sem=sem, val=val))
+        ops.append(dict(eng=eng, ch=cur[0], up=cur[1], fn=fn, deps=list(deps), cost=cost, lat=lat, sem=sem, val=val))
         return me
 
     def ps(a): return a[1][0] == "@" or SCRATCH[a[1]][0] == "psum"
@@ -146,15 +144,15 @@ def rank_program(g, core, T, topo):
     def either(o, a, fa, fv):
         op("F", {"A": actf(o, a, *fa), "V": tsf(o, a, *fv)}, [a] + cols(*fa, *fv), [o], {"A": vc(len(a[2])), "V": c1(o, a)})
     def lin(o, a, scale=1.0, bias=0.0): either(o, a, (F.Identity, bias, scale), (scale, A.mult, bias, A.add))
-    def relu(o, a, scale=1.0): either(o, a, (F.Relu, 0.0, scale), (scale, A.mult, 0.0, A.max))
     def mm(o, l, r, start=False, stop=False):
         n = max(min(64, len(l[2])), len(r[2])) * (4 if dty(l) == f32 else 1)
         op("T", lambda q: q.matmul(x(o), x(l), x(r), start, stop), [l, r], [o], 0.02 + n * PEC)
-    def group(items, after=None):
+    def group(items, after=None, early=None):
         first = len(ops)
         for k, it in enumerate(items): mm(it[0], it[1], it[2], k == 0, k == len(items) - 1)
         d = ops[first]["deps"]
-        for z in [z for o in ops[first + 1:] for z in o["deps"]] + [first if after is None else after]:
+        more = [early] if early is not None else [z for o in ops[first + 1:] for z in o["deps"]]
+        for z in more + [first if after is None else after]:
             if z < first and z not in d: d.append(z)
         return first
     def sel(o, a, pat, base, fill, cmp=None, cm=1):
@@ -192,9 +190,11 @@ def rank_program(g, core, T, topo):
             sel(M(s + str(k)), Z3, pat(s, 4), -k, w)
             if k: triv(s + str(k), s, -1000, 0.0)
         sel(M(s + "L"), M("A3") if s == "A" else Z3, pat(s, 1), -13, w); triv(s + "L", s, 12, w)
-    lin(M("I"), ap("I32")); lin(M("nI"), ap("I32"), -1.0)
+    lin(M("I"), ap("I32")); lin(M("nI"), ap("I32"), -1.0); lin(M("I3"), ap("I32"), 3.0); lin(M("I2"), ap("I32"), 2.0)
     for s in "AB":
-        sel(M("F" + s), Z3, pat(s, 5), -4, -8.0); triv("F" + s, s, 15, -8.0)
+        for k, w in enumerate((0.875, 0.875, 0.875, -0.125) if s == "A" else (-0.875, 0.125, 0.125, 0.125)):
+            sel(M("F" + s), M("F" + s) if k else Z3, pat(s, 4), -k, w)
+        triv("F" + s, s, 12, 0.875 if s == "A" else -0.875)
     for qq in range(2):
         for s in "AB":
             h = M("H%s%d" % (s, qq))
@@ -239,13 +239,14 @@ def rank_program(g, core, T, topo):
         lin(bc(3 + e), bc(0), -4096.0, h); lin(bc(5 + e), bc(1), 3072.0, h); lin(bc(7 + e), bc(0), -4096.0, bc(5 + e))
     lin(ap("BC", sl(23, 29)), ap("BC", sl(3, 9)), -256.0); ms(bc(44), -128.0); ms(bc(45), 128.0); ms(bc(46), 3.0); ms(bc(47), 2.0 ** 29)
     lin(bc(9), bc(1), 8192.0, 4096.0); lin(bc(9), bc(0), -4096.0, bc(9)); lin(bc(10), bc(0), -4096.0)
-    lin(bc(11), bc(2), 1.0, -1.0)
-    ts(bc(12), bc(0), bc(1), A.add, -7.0, A.mult); lin(bc(13), bc(2), 19.0, -4.0); lin(bc(12), bc(12), 1.0, bc(13))
+    lin(bc(11), bc(2), 1.0, -1.0); lin(bc(12), bc(2), -11.0, 12.0)
     lin(bc(14), bc(0), TRIV0); lin(bc(15), bc(1), TRIV0)
+    cur[1] = -1
     for k, s in enumerate("AB"):
         for q in range(6):
             c = bc(32 + 6 * k + q)
             lin(c, bc(k), TRIV[q][0] - 131072.0 * QV[q], 131072.0 * QV[q]); lin(M("D%s%d" % (s, q)), M("I"), c)
+    cur[1] = 0
     for w in range(3):
         ts(bc(16), p16, 5.0 * w, A.is_ge); ts(bc(29 + w), p16, 5.0 * w + 5, A.is_lt, bc(16), A.mult)
         lin(ap("IW", sl(160 * w, 160 * w + 160)), ap("IW0"), bc(29 + w))
@@ -321,7 +322,7 @@ def rank_program(g, core, T, topo):
         bn = bank()
         group([(ap(bn, sl(vb * 128, vb * 128 + 128)), ap("FS" + b, sl(vb * 8, vb * 8 + 8)), ap("I32")) for vb in range(NVB)])
         lin(ap(w0, sl(v0, v0 + CW)), ap(bn, sl(0, CW)), 8192.0)
-        bn = bank()
+        bn = bank(); cur[1] = 1
         group([(ap(bn, sl(0, HN)), ap("FL" + b), ap("I32", sl(h * HN, (h + 1) * HN))) for h in range(HH)])
         cp(ap("LL" + b), ap(bn, sl(0, HN)))
         gat(ap("GL" + b), ap("LUT"), ap("LL" + b), "any")
@@ -332,6 +333,7 @@ def rank_program(g, core, T, topo):
             if w == 0: it += [(ap(bn, sl(vb * 128, vb * 128 + 128)), ap("FT" + b, sl(vb * 8, vb * 8 + 8)), ap("I32")) for vb in range(NVB)]
             group(it)
             lin(ap(wb, sl(3 * v0 + w, 3 * (v0 + CW), 3)), ap(bn, sl(0, CW)), 1.0, bc(2))
+        cur[1] = 0
         if v0 < G <= v0 + CW:
             for kind, name, m in ((0, w0, 1), (1, wb, 3)):
                 def send(q, kind=kind, name=name, m=m):
@@ -360,11 +362,12 @@ def rank_program(g, core, T, topo):
     for rnd in range(RO):
         last = rnd == RO - 1; w0, wb = "W0%d" % rnd, "WB%d" % rnd
         for ch in range(NCH):
-            b = str(ch % 2); kb = "B%d" % (6 + ch % 2); v0 = ch * CW; cur[0] = ch
+            b = str(ch % 2); kb = "B%d" % (6 + ch % 2); v0 = ch * CW; cur[0] = ch; cur[1] = 1 - ch
             ga, gb = ap("G0" + b, H0), ap("G0" + b, H1)
             gat(ga, ap(w0), ap("L0", sl(ch * LW, (ch + 1) * LW)), 4096.0); gat(gb, ap(w0), ap("L0", sl(32 + ch * LW, 32 + (ch + 1) * LW)), 3072.0)
             for w in range(3):
                 gat(ap("GW" + b, sl(2 * w * CW, 2 * (w + 1) * CW)), ap(wb), ap("LWL", sl((6 * ch + 2 * w) * LW, (6 * ch + 2 * w + 2) * LW)), "any")
+            ts(ap("FG" + b, H0), ga, 3000.0, A.is_lt, 8.0, A.mult); ts(ap("FG" + b, H1), gb, 3000.0, A.is_lt, -8.0, A.mult)
             gw = lambda w, s: ap("GW" + b, sl((2 * w + s) * CW, (2 * w + s + 1) * CW))
             for t, bias in ((0, 3), (2, 5), (4, 7), (6, 7), (8, None)):
                 bn = bank(); cs = CL[t:t + 2]; it = []
@@ -379,20 +382,21 @@ def rank_program(g, core, T, topo):
             sg = lambda k, l: ap("SG" + b, sl(CL.index((k, l)) * CW, (CL.index((k, l)) + 1) * CW))
             se = lambda k, l: ap("SE" + b, sl(CL.index((k, l)) * CW, (CL.index((k, l)) + 1) * CW))
             for k in (1, 2):
-                bn = bank(); it = [(ap(bn, H0), M("FA"), gw(k - 1, 0)), (ap(bn, H1), M("FB"), gw(k - 1, 1))]
+                bn = bank(); it = [(ap(bn, H0), M("A%d" % k), ap("FG" + b, H0)), (ap(bn, H1), M("B%d" % k), ap("FG" + b, H1))]
                 for l in range(3):
                     it += [(ap(bn, H0), M("I"), sg(k, l)), (ap(bn, H1), M("I"), sg(l, k - 1))]
                 for l in range(3):
                     it += [(ap(bn, H0), M("nI"), se(k - 1, l)), (ap(bn, H1), M("nI"), se(l, k))]
                 group(it)
-                relu(ap("R12" + b, sl((k - 1) * 2 * CW, k * 2 * CW)), ap(bn, H2), (3.0, 2.0)[k - 1])
+                lin(ap("RW" + b, (H0, H1)[k - 1]), ap(bn, H0))
+                either(ap("R12" + b, sl((k - 1) * 2 * CW, k * 2 * CW)), ap(bn, H2), (F.Relu, -8.0, 1.0), (-8.0, A.add, 0.0, A.max))
             bn = bank(); it = [(ap(bn, H1), M("nI"), se(l, 0)) for l in range(3)] + [(ap(bn, H0), M("I"), sg(0, l)) for l in range(3)]
-            it += [(ap(bn, (H0, H1)[s]), M("I"), ap("R12" + b, sl((2 * k + s) * CW, (2 * k + s + 1) * CW))) for k in range(2) for s in range(2)]
+            it += [(ap(bn, (H0, H1)[s]), M(("I3", "I2")[k]), ap("R12" + b, sl((2 * k + s) * CW, (2 * k + s + 1) * CW))) for k in range(2) for s in range(2)]
             group(it); lin(ap("IX" + b, H0), ap(bn, H0)); lin(ap("IX" + b, H1), ap(bn, H1), 1.0, bc(46))
-            bn = bank(); it = [(ap(bn, H0), M("FA"), gw(2, 0)), (ap(bn, H0), M("FB"), gw(2, 1))]
-            it += [(ap(bn, H0), M("nI"), sg(k, l)) for k, l in CL] + [(ap(bn, H0), M("I"), se(k, l)) for k, l in CL]
-            it += [(ap(bn, H0), M("I"), ap("EQ" + b, h)) for h in (H0, H1)]
-            group(it); act(ap("VD" + b), ap(bn, H0), F.Relu, bc(12), bc(11))
+            cur[1] = 0; bn = bank(); it = [(ap(bn, H0), M("FA"), ap("FG" + b, H0)), (ap(bn, H0), M("FB"), ap("FG" + b, H1))]
+            it += [(ap(bn, H0), M("nI"), sg(0, l)) for l in range(3)] + [(ap(bn, H0), M("I"), se(2, l)) for l in range(3)]
+            it += [(ap(bn, H0), M(m), ap(nm + b, h)) for m, nm in (("I", "EQ"), ("nI", "RW")) for h in (H0, H1)]
+            group(it); act(ap("VD" + b), ap(bn, H0), F.Relu, bc(12), bc(11)); cur[1] = 1 - ch
             prev = None
             for q in range(6):
                 bn = bank(); it = []
@@ -402,6 +406,7 @@ def rank_program(g, core, T, topo):
                 if q == 0:
                     for s, h in ((0, H0), (1, H1)): lin(ap("AC" + b, h), ap(bn, h), 1.0, bc(14 + s))
                 else: tt(ap(("EI" if q == 5 else "AC") + b), ap(bn, H2), ap("AC" + b), A.max)
+            cur[1] = 0
             for e, mk in ((0, 0x5555), (1, 0xAAAA)):
                 ts(ap("ME" + b, sl(2 * e * CW, 2 * (e + 1) * CW)), ap("EI" + b), mk, A.bitwise_and)
             for e, mk in ((0, 0x5555), (1, 0xAAAA)):
@@ -433,7 +438,7 @@ def rank_program(g, core, T, topo):
                     tt(ap("DD" + b), key, ap("KB" + b), A.subtract)
                     either(ap("DD" + b), ap("DD" + b), (F.Relu, bc(47), -2.0 ** 25), (16.0, A.is_lt, 2.0 ** 26, A.mult)); tt(key, key, ap("DD" + b), A.add)
                 lin(ap("SM" + b, sl(12 * N24 + c, 13 * N24, 3)), ap(s1, sl(15, CW, 16)))
-            ts(si(b, 3), sm(b, 12), 2.0 ** 25, A.min); ts(sm(b, 13), sm(b, 12), 2.0 ** 24, A.is_ge)
+            ts(si(b, 3), sm(b, 12), 2.0 ** 25, A.min); ksel = len(ops) - 1; ts(sm(b, 13), sm(b, 12), 2.0 ** 24, A.is_ge)
             ts(si(b, 4), si(b, 3), 2, A.logical_shift_right, 3, A.bitwise_and); ts(si(b, 5), si(b, 3), 3, A.bitwise_and)
             ss = lambda a, c, d=1: ap("SS" + b, sl(0, NVB * 8), sl(a, c, d))
             for s in range(2):
@@ -455,7 +460,7 @@ def rank_program(g, core, T, topo):
                     for vb in range(NVB):
                         o = ap(bn, sl((s * NVB + vb) * 96, (s * NVB + vb + 1) * 96))
                         it += [(o, blk("G0" + b, vb, s * CW), ML(i)), (o, blk("SR" + b, vb), ML(4 + 2 * i + s))]
-                prev = group(it, prev); o = ap(bn, sl(0, 2 * NVB * 96))
+                prev = group(it[0::2] + it[1::2], prev, ksel); o = ap(bn, sl(0, 2 * NVB * 96))
                 if i == 0: lin(ap("LS" + b), o)
                 else: tt(ap("LS" + b), o, ap("LS" + b), A.max)
             sa, sb = sl(0, NVB), sl(NVB, 2 * NVB)
@@ -492,7 +497,7 @@ def rank_program(g, core, T, topo):
     def cost(k): return ops[k]["cost"]["A"] if ops[k]["eng"] == "F" else ops[k]["cost"]
     pri = [0.0] * n
     for k in range(n - 1, -1, -1): pri[k] = cost(k) + max([lag(k, s) + pri[s] for s in succ[k]] + [ops[k]["lat"]])
-    pri = [p - BIAS * o["ch"] for p, o in zip(pri, ops)]
+    pri = [p - BIAS * o["ch"] + TB * o["up"] for p, o in zip(pri, ops)]
     for k, o in enumerate(ops):
         if o["eng"] == "P": pri[k] = 1e6 if o["sem"] or k < 20 or o["cost"] < 0.19 else -k
     opens = {v[0]: name for name, v in sess.items()}; member = {}

@@ -1,64 +1,74 @@
+import math
 import numpy as np
 from concourse.bass import DstId, RemoteDMATransfer
 from concourse.mybir import AluOpType as A, AxisListType, ActivationFunctionType as F
 
-NCH = 2
-V, G, NR, RO = 512, 192, 4, 2
+V, G, NR, RO, NB = 512, 192, 4, 2, 2
 W = V + (NR - 1) * G
-CW = V // NCH; NVB = CW // 128; HH = 4 // NVB; HN = 128 // HH; N24 = NVB * 24; LW = CW // 16
-QV = (0, 1, 2, 3, 4, 6)
-TRIV = ((-65536, 0), (-820, 118784), (61696, 3824), (69632, -12544), (0, -131072), (0, -131072))
-TRIV0 = 174762.0
-MATS = ["I", "nI", "I3", "I2", "A0", "A1", "A2", "A3", "AL", "B0", "B1", "B2", "B3", "BL", "FA", "FB", "HA0", "HA1", "HB0", "HB1", "VK", "RM",
-        "PB", "PN0", "PN1", "PN2"] + ["Z%s%d" % (s, q) for s in "AB" for q in range(6)] + ["D%s%d" % (s, q) for s in "AB" for q in range(6)]
+CW = 256; GP = 2; U = 2.0 ** -13; KU = 2.0 ** -25
+SLOTS = {1: [(0,), (0,), (2,), (2,), (1,), (3,)], 2: [(0, 1), (0, 2), (1, 2), (0, 3), (1, 3), (2, 3)],
+         3: [(0, 1, 3), (0, 1, 2), (0, 1, 2), (0, 2, 3), (0, 1, 2), (1, 2, 3)], 4: [None, None, None, (0, 1, 2, 3), None, None]}
+ROWS = {0: (0, 0, 1), 3: (0, 2, 3), 1: (0, 4, 4), 4: (1, 0, 1), 5: (1, 2, 3), 2: (1, 4, 4)}
+LINES = (4, 0, 3, 1, 5, 2)
+TRIV = {1: 0xAAAA, 4: 0xCCCC, 2: 0xF0F0, 5: 0xFF00}
+SLOPE = {"A": ((11, -13, 7), (-5, 2, 0), (14, -13, 6), (-10, 5, 0), (0, 0, 0), (18, -13, 7)),
+         "B": ((5, 0, 0), (15, -7, 3), (-8, 3, 0), (23, -16, 8), (0, 0, 0), (-12, 5, 0))}
+FOLD = {"A": (-6, -29, -51), "B": (2, -12, -45)}
+OFF = {"A": (-28, -52, -60), "B": (-72, -100, -60)}
+HEIGHT = {"A": (-89, -115, -119, -75, -124, 53), "B": (50, 22, -109, -102, -119, -82)}
+UW = (9, 9, -7); MUW = 5 / 64; THR = 4.125 / 16
+SIG = sorted(set(x for s in SLOPE.values() for r in s for x in r if x))
+ZEROED = ["A1", "A2", "B1", "B2", "TA0", "TA1", "TA2", "TB0", "TB1", "TB2", "UA", "UB", "PN"]
+MATS = ZEROED + ["A0", "B0", "AL", "AK", "BL", "BK", "U9", "U7", "X9", "nI", "VK", "RM", "PB", "PN0", "PN1", "PN2"] + \
+    ["Z%s%d" % (s, q) for s in "AB" for q in (0, 3, 4, 5)] + ["D%d" % x for x in SIG]
+MATH = ["Z%s%d" % (s, q) for s in "AB" for q in (1, 2)]
 f32, bf, i32, u16, f16 = "float32", "bfloat16", "int32", "uint16", "float16"
 SCRATCH = {}
 def _sb(name, shape, dt, per=1):
     for k in range(per):
         SCRATCH[name + (str(k) if per > 1 else "")] = ("sbuf", [128] + list(shape), dt)
-for _n, _s, _d in (("MT", [len(MATS) * 8, 16], bf), ("ML", [12 * 96], bf), ("Z3", [8, 16], bf), ("Z2", [160], bf), ("ZF", [128], f32),
-                   ("PI", [8, 16], bf), ("C32", [8, 16], bf), ("I32", [128], f32), ("OC", [V], f32), ("QI", [3, 128], bf), ("D1", [32 * V], bf),
-                   ("IW", [3 * 160], bf), ("IW0", [160], bf),
-                   ("BO", [8], bf), ("BOF", [8], f32), ("BC", [48], f32), ("PC", [4], i32), ("ROW", [96], f32), ("TMP", [2 * 96], f32),
-                   ("PL", [80], i32), ("PF", [80], f32), ("PS", [3 * 80], i32), ("PM", [4 * 80], f32), ("WL", [5, 8, 16], bf), ("WC", [5, 16], bf),
-                   ("TI", [256], i32), ("TJ", [256], i32), ("BT", [256], bf), ("LUT", [1280], bf), ("RS", [CW], f32), ("RR", [CW], f32),
-                   ("fanI", [64], i32), ("L0", [64], u16), ("LW3", [NCH, 6, LW], u16), ("LWL", [NCH * 6 * LW], u16), ("INI", [V], i32), ("INF", [V], f32),
-                   ("CE", [8192], bf), ("RQ", [V], bf)):
+for _n, _s, _d in (("MT", [len(MATS) * 8, 4, 4], bf), ("MH", [len(MATH) * 8, 4, 4], f16), ("ML", [12 * 8, 4, 3], bf), ("Z3", [8, 4, 4], bf),
+                   ("Z2", [160], bf), ("ZL", [8, 4, 3], bf), ("ZF", [128], f32), ("SEL", [8, 5, 3], f32), ("I0", [130], bf), ("I32", [128], f32),
+                   ("PI", [8, 4, 4], bf), ("CK", [8, 4, 4], bf), ("QI", [3, 128], bf), ("J0", [160], bf), ("JW", [4, 160], bf),
+                   ("TV", [48, 4, 4], bf), ("ON", [CW], bf), ("BO", [8], bf), ("BOF", [8], f32), ("BC", [48], f32), ("PC", [4], i32),
+                   ("ROW", [96], f32), ("TMP", [96], f32), ("OWN", [32], f32), ("PL", [64], i32), ("PF", [64], f32), ("PS", [3 * 64], i32),
+                   ("PM", [4 * 64], f32), ("WL", [4, 8, 16], bf), ("TI", [256], i32), ("TJ", [256], i32), ("BT", [256], bf), ("LUT", [1024], bf),
+                   ("RS", [CW], f32), ("RZ", [CW], f32), ("INI", [V], i32), ("INF", [V], f32)):
     _sb(_n, _s, _d)
-for _n, _s, _d in (("W0", [W], f32), ("WB", [3 * W], bf),
-                   ("G0", [2 * CW], f16), ("GW", [6 * CW], bf), ("SG", [9 * CW], bf), ("SE", [9 * CW], bf), ("EQ", [2 * CW], bf),
-                   ("FG", [2 * CW], bf), ("RW", [2 * CW], bf),
-                   ("R12", [4 * CW], bf), ("IX", [2 * CW], bf), ("VD", [CW], bf), ("AC", [2 * CW], f32), ("EI", [2 * CW], i32),
-                   ("ME", [4 * CW], i32), ("NF", [CW], f32), ("T5", [CW], i32), ("C1", [CW], u16), ("C2", [CW], u16),
-                   ("D0", [4096], bf), ("MX", [4096], bf), ("S1", [CW], f32), ("KB", [CW], f32), ("DD", [CW], f32),
-                   ("SM", [24 * N24], f32), ("SI", [6 * N24], i32), ("SS", [NVB * 8, 16], bf), ("SR", [CW], bf), ("LS", [2 * NVB, 96], f32),
-                   ("MN", [2 * NVB, 96], f32), ("FS", [NVB * 8, 16], f32), ("FT", [NVB * 8, 16], f32), ("FL", [8, 16], f32),
-                   ("LL", [HN], u16), ("GL", [16 * HN], bf), ("FO", [4 * N24], f32)):
-    _sb(_n, _s, _d, 2)
+for _n, _s, _d in (("W0", [W], f32), ("WB", [2 * W], bf)):
+    _sb(_n, _s, _d, NB * RO)
+for _n, _s, _d in (("CE", [8192], bf), ("RQ", [CW], bf), ("FN", [4, 16], i32), ("L0", [32], u16), ("LW", [64], u16), ("D1", [32 * CW], bf),
+                   ("G0", [2 * CW], f16), ("GW", [4 * CW], bf), ("HH", [11 * CW], bf), ("FE", [6 * CW], bf), ("RR", [CW], bf), ("VD", [CW], bf),
+                   ("AC", [2 * CW], f32), ("EI", [2 * CW], i32), ("ME", [4 * CW], i32), ("NF", [CW], f32), ("T5", [CW], i32),
+                   ("C1", [CW], u16), ("C2", [CW], u16), ("D0", [4096], bf), ("MX", [4096], bf), ("S1", [CW], f32), ("KB", [CW], f32),
+                   ("OB", [CW], bf), ("ZB", [CW, 3], f32), ("UN", [16, 24, 3], f32), ("IN", [16, 5, 3], f32), ("SI", [16, 6, 3], i32),
+                   ("SS", [16, 4, 4], bf), ("SR", [CW], bf), ("LS", [32, 4, 3], f32), ("FS", [16, 4, 4], f16), ("FT", [16, 16], bf),
+                   ("FL", [68, 4], f16), ("LL", [64], u16), ("GL", [1024], bf), ("FO", [20, 3, 4], f16), ("FP", [4, 2, 12], f32)):
+    _sb(_n, _s, _d, NB)
 for _k in range(8):
     SCRATCH["B%d" % _k] = ("psum", [128, 512], f32)
-DMAS = ["leaf", "tab", "fan", "req", "cel", "oyl", "oyt", "oyc"]
-SEMAPHORES = ["sP", "sT", "sV", "sA", "sent"] + ["d" + x for x in DMAS] + ["arr%d%d" % (r, k) for r in range(RO) for k in range(2)]
+DMAS = ["leaf", "tab"] + [x + str(b) + str(h) for x in ("fan", "req", "cel") for b in range(NB) for h in range(2)] + \
+    [x + str(b) for x in ("oyl", "oyt", "oyc") for b in range(NB)]
+SEMAPHORES = ["sP", "sT", "sV", "sA", "sent"] + ["d" + x for x in DMAS] + ["arr%d%d" % (r, k) for r in range(NB * RO) for k in range(2)]
 CYC = 0.00083; PEC = 0.00042; LAG = 0.08; FIX = 0.045; GC = 1.56
-SLACK = 0.6; GAIN = 0.3; BIAS = 1.0; TB = 12.0; GP = 2
+SLACK = 0.6; GAIN = 0.3; BIAS = 6.0; TB = 0.0; OPEN = False; D1P = (0, 1); LOOK = 0.03; PASSES = 8
+PLAN = {}
+SAME = {"INI": "EI1", "INF": "AC1", "TI": "T50", "TJ": "T51", "PM": "S10", "ME1": "ME0", "GL1": "GL0", "HH1": "HH0", "IN1": "IN0"}
+for _n in SAME: del SCRATCH[_n]
 
 
 def lut_columns():
     out = {}
-    for n in (1, 2, 3, 4):
-        for g0 in range(4):
-            for g1 in range(3 if n > 1 else 1):
-                for g2 in range(2 if n > 2 else 1):
-                    pl = [g0, g0 + g1 + 1, g0 + g1 + g2 + 2, g0 + g1 + g2 + 3][:n]
-                    if pl[-1] > 3: continue
-                    s = QV.index(g0 + 3 * g1 + 2 * g2)
-                    for b in range(2):
-                        w = [0] * 9
-                        for m in range(8):
-                            mm = m + 8 * (1 - b)
-                            o = sum(((mm >> p) & 1) << k for k, p in enumerate(pl))
-                            if o < 8: w[o] += 1 << m
-                        out[(n, 5 * (s // 2) + 2 * (s % 2) + b)] = w
+    for n, held in SLOTS.items():
+        for q, pl in enumerate(held):
+            if pl is None: continue
+            w, hi, lo = ROWS[q]
+            for row, half in ((hi, 1), (lo, 0)):
+                wt = [0] * 9
+                for m in range(8):
+                    o = sum((((m + 8 * half) >> p) & 1) << k for k, p in enumerate(pl))
+                    if o < 8: wt[o] += 1 << m
+                out[(4 - n, 5 * w + row)] = wt
     return out
 
 
@@ -81,9 +91,10 @@ def rank_program(g, core, T, topo):
         return
     Q = {"P": g, "T": g.tensor, "V": g.vector, "A": g.scalar, "S": g.sync}
     ops = []; track = {}; runs = {}; grid = {}; sess = {}; place = {}; nb = [0]; cur = [0, 0]
-    sl = slice
+    sl = slice; ALL = slice(None)
 
     def ap(name, *idx):
+        name = SAME.get(name, name)
         shape = SCRATCH[name][1] if name[0] != "@" else [128, 512]
         if name not in grid: grid[name] = np.arange(int(np.prod(shape[1:]))).reshape(shape[1:])
         if not idx or not isinstance(idx[0], tuple): idx = ((0, 128),) + idx
@@ -147,9 +158,9 @@ def rank_program(g, core, T, topo):
     def mm(o, l, r, start=False, stop=False):
         n = max(min(64, len(l[2])), len(r[2])) * (4 if dty(l) == f32 else 1)
         op("T", lambda q: q.matmul(x(o), x(l), x(r), start, stop), [l, r], [o], 0.02 + n * PEC)
-    def group(items, after=None, early=None):
+    def group(items, after=None, early=None, close=True):
         first = len(ops)
-        for k, it in enumerate(items): mm(it[0], it[1], it[2], k == 0, k == len(items) - 1)
+        for k, it in enumerate(items): mm(it[0], it[1], it[2], k == 0, close and k == len(items) - 1)
         d = ops[first]["deps"]
         more = [early] if early is not None else [z for o in ops[first + 1:] for z in o["deps"]]
         for z in more + [first if after is None else after]:
@@ -166,92 +177,106 @@ def rank_program(g, core, T, topo):
         else: op("V", lambda q: q.tensor_scalar(x(o), w(), kind, None, A.min), [win, off], [o], c)
     def dma(name, o, a, rd, wr, nbytes):
         op("S", lambda q: q.dma_start(o, a), rd, wr, 0.08, lat=2.0 + nbytes / 150e3, sem="d" + name, val=16)
+    def also(k): ops[-1]["deps"] += [z for z in k if z not in ops[-1]["deps"]]
     def M(name, *idx):
-        k = MATS.index(name) * 8
-        return ap("MT", sl(k, k + 8), *(idx or (sl(0, 16),)))
+        t, names = ("MH", MATH) if name in MATH else ("MT", MATS); k = names.index(name) * 8
+        return ap(t, sl(k, k + 8), *idx)
     def bc(k): return ap("BC", sl(k, k + 1))
+    def half(h): return (64 * h, 64 * h + 64)
+    I = ap("I0", sl(2, 130)); Z3 = ap("Z3")
+    H0, H1, H2 = sl(0, CW), sl(CW, 2 * CW), sl(0, 2 * CW)
 
-    dma("leaf", T.INI[0:96, :], T.leaf0[:, :], [], [ap("INI")], 2e5)
-    dma("tab", T.INI[96:120, :], T.tab0[:, :], [], [], 5e4); tabop = len(ops) - 1
-    dma("fan", T.fanI[:, :], T.fan[:, :], [], [ap("fanI")], 3e4)
-    dma("req", T.RQ[:, :], T.req[:, :], [], [ap("RQ")], 1e5)
-    dma("cel", T.CE[:, :], T.cells[:, :], [], [ap("CE")], 2e6)
+    INI, INF = T[SAME["INI"]], T[SAME["INF"]]
+    dma("leaf", INI[0:96, :], T.leaf0[:, :], [], [ap("INI")], 2e5)
+    dma("tab", INI[96:120, :], T.tab0[:, :], [], [], 5e4); tabop = len(ops) - 1
+    both = {}
+    for name, buf, size in (("fan", "FN", 3e4), ("req", "RQ", 5e4), ("cel", "CE", 2e6)):
+        for b in range(NB):
+            for h in range(2):
+                r = sl(64 * b, 64 * b + 64)
+                src = {"fan": T.fan[r, :], "req": T.req[r, CW * h:CW * (h + 1)], "cel": T.cells[r, :]}[name]
+                dma("%s%d%d" % (name, b, h), T[buf + str(b)][64 * h:64 * h + 64], src, [], [ap(buf + str(b))] if h else [], size * (b + 1))
+                both[(buf, b, h)] = len(ops) - 1
+            ops[-1]["deps"].append(both[(buf, b, 0)]); ops[-1]["pair"] = both[(buf, b, 0)]
 
-    ms(ap("ZF"), 0.0); ms(ap("Z3"), 0.0); ms(ap("Z2"), 0.0)
-    sel(ap("I32"), ap("ZF"), [[-1, 128]], 0, 1.0)
-    iota(ap("TI"), [[1, 256]], 0, 0); iota(ap("PC", sl(0, 1)), [[0, 1]], 0, 1)
-    sel(ap("IW0"), ap("Z2"), [[-1, 160]], 16, 1.0)
-    Z3 = ap("Z3"); G0P = [[-16, 8], [0, 4]]; GP16 = [[-16, 8], [0, 16]]
-    def side(s): return sl(12, 16) if s == "A" else sl(3, 16, 4)
-    def pat(s, st): return [[-16, 8], [-st, 4], [0, 4]] if s == "A" else [[-16, 8], [0, 4], [-st, 4]]
-    def triv(name, s, row, w): sel(M(name, side(s)), ap("Z3", sl(0, 8), side(s)), G0P, -row, w)
+    ms(ap("ZF"), 0.0); ms(ap("Z2"), 0.0); ms(Z3, 0.0); ms(ap("PF"), 0.0); ms(ap("ROW"), 0.0)
+    iota(ap("PC", sl(0, 1)), [[0, 1]], 0, 1)
+    sel(ap("I32"), ap("ZF"), [[-1, 128]], 0, 1.0); iota(ap("TI"), [[1, 256]], 0, 0)
+    ms(ap("SEL"), 0.0)
+    sel(ap("SEL", ALL, sl(0, 4)), ap("SEL", ALL, sl(0, 4)), [[-12, 8], [-1, 4], [-4, 3]], 0, 1.0)
+    sel(ap("SEL", ALL, 4), ap("SEL", ALL, 4), [[-3, 8], [-1, 3]], -96, 1.0)
+    for b in range(NB): iota(ap("OWN", sl(16 * b, 16 * b + 16)), [[128, 2], [CW, 2], [0, 4]], V * rank, 1, True)
+    sel(ap("I0"), ap("Z2", sl(0, 130)), [[-1, 130]], 2, 1.0)
+    sel(ap("J0"), ap("Z2"), [[-1, 160]], 16, 1.0)
+    sel(ap("J0", sl(80, 144)), ap("J0", sl(80, 144)), [[-1, 64]], 0, 1.0); sel(ap("J0", sl(16, 80)), ap("J0", sl(16, 80)), [[-1, 64]], -64, 1.0)
+    ms(ap("MT", sl(0, 8 * len(ZEROED))), 0.0)
+    G4 = [[-16, 8], [0, 4]]; G16 = [[-16, 8], [0, 16]]
+    def real(s): return (sl(0, 3), ALL) if s == "A" else (ALL, sl(0, 3))
+    def last(s): return (3, ALL) if s == "A" else (ALL, 3)
+    def pat(s, st, n=4): return [[-16, 8], [-st, n], [0, 4]] if s == "A" else [[-16, 8], [0, 4], [-st, n]]
+    def part(name, s, st, row, w): sel(M(name, *real(s)), M(name, *real(s)), pat(s, st, 3), -row, w)
     for s, w in (("A", 1.0), ("B", -1.0)):
-        for k in range(4):
-            sel(M(s + str(k)), Z3, pat(s, 4), -k, w)
-            if k: triv(s + str(k), s, -1000, 0.0)
-        sel(M(s + "L"), M("A3") if s == "A" else Z3, pat(s, 1), -13, w); triv(s + "L", s, 12, w)
-    lin(M("I"), ap("I32")); lin(M("nI"), ap("I32"), -1.0); lin(M("I3"), ap("I32"), 3.0); lin(M("I2"), ap("I32"), 2.0)
+        sel(M(s + "0"), Z3, pat(s, 1), 0, w)
+        for k in (1, 2): part(s + str(k), s, 1, 4 * k, w)
+    for s, w in (("A", 1.0), ("B", -1.0)):
+        sel(M(s + "L"), Z3, pat(s, 1), -12, w); sel(M(s + "L", *last(s)), ap("Z3", ALL, *last(s)), G4, -3, w)
+        sel(M(s + "K"), M(s + "L"), pat(s, 4), -7, 2048.0 * w)
     for s in "AB":
-        for k, w in enumerate((0.875, 0.875, 0.875, -0.125) if s == "A" else (-0.875, 0.125, 0.125, 0.125)):
-            sel(M("F" + s), M("F" + s) if k else Z3, pat(s, 4), -k, w)
-        triv("F" + s, s, 12, 0.875 if s == "A" else -0.875)
-    for qq in range(2):
+        for k in range(3): part("T%s%d" % (s, k), s, 4, 7, FOLD[s][k] / 16)
+    muA = MUW - sum(m * t for m, t in zip(UW, FOLD["A"])) / 16
+    part("UA", "A", 4, 7, muA); part("UB", "B", 4, 7, MUW)
+    for q0, q1 in ((4, 0), (3, 5), (1, 2)):
         for s in "AB":
-            h = M("H%s%d" % (s, qq))
-            sel(h, Z3, pat(s, 5), -2 * qq, 256.0); sel(h, h, pat(s, 5), -2 * qq - 1, 1.0)
-    for q in range(6):
-        for s in "AB":
-            z = "Z%s%d" % (s, q)
-            sel(M(z), M("H%s%d" % (s, q % 2)), GP16, -15, -65536.0 * QV[q] ** 2); triv(z, s, 15, float(TRIV[q][1]))
+            z = "Z%s%d" % (s, q0); hi, lo = ROWS[q0][1:]
+            sel(M(z), Z3, G16, -15, 256.0 * HEIGHT[s][q0])
+            if hi == lo: part(z, s, 5, lo, 257.0)
+            else: part(z, s, 5, hi, 256.0); part(z, s, 5, lo, 1.0)
+            sel(M("Z%s%d" % (s, q1)), M(z), G16, -15, 256.0 * HEIGHT[s][q1])
+    for q in (0, 3): sel(M("ZB%d" % q, *last("B")), M("ZB%d" % q, *last("B")), G4, -15, -65536.0)
     iota(ap("PI"), [[0, 8], [1, 16]], 0, 0, True)
-    sel(M("VK"), ap("PI"), GP16, -15, 0.0, A.is_equal)
-    sel(M("VK", sl(0, 15)), M("VK", sl(0, 15)), [[-16, 8], [-1, 15]], 0, 2.0 ** 25)
-    ms(ap("C32"), -32.0)
-    sel(M("RM"), ap("C32"), GP16, 0, 0.0, A.is_ge); sel(M("RM"), M("RM"), [[16, 8], [0, 16]], 15, 0.0, A.is_ge, -1)
-    lin(ap("BO"), M("RM", sl(0, 1)), -1.0); lin(ap("BOF"), M("RM", sl(0, 1)), -1.0 / 32)
-    iota(ap("QI", 0), [[0, 8], [1, 4], [0, 4]], 0, 0, True); iota(ap("QI", 1), [[0, 32], [1, 4]], 0, 0, True)
-    tt(ap("QI", sl(0, 2)), ap("QI", sl(0, 2)), ap("QI", sl(0, 2)), A.mult); tt(ap("QI", 2), ap("QI", 0), ap("QI", 1), A.add)
-    lin(ap("QI", 2), ap("QI", 2), -65536.0, 65536.0)
-    def ML(k, a=0, b=96): return ap("ML", sl(96 * k + a, 96 * k + b))
-    def z2(n): return ap("Z2", sl(0, n))
-    U = 2.0 ** -13; P24 = [[-16, 8], [0, 3]]
-    for i in range(4):
-        if i < 3:
-            sel(ML(i), z2(96), [[-1, 4], [-16, 8], [0, 3]], -4 * i, U); sel(ML(i, 72), ML(i, 72), P24, -13 - i, U)
-        else:
-            sel(ML(i), z2(96), [[0, 4], [-16, 8], [0, 3]], -12, U); sel(ML(i, 24, 72), z2(48), [[0, 48]], 1000, 0.0)
-        for s, none in ((0, 0.5), (1, 0.375)):
-            k = 4 + 2 * i + s
-            sel(ML(k), z2(96), [[0, 4], [-16, 8], [-4, 3]], -2 * s - 1, -2.0); sel(ML(k), ML(k), [[0, 4], [-16, 8], [-1, 3]], -12, 2.0)
-            if i: sel(ML(k), ML(k), [[0, 4], [-16, 8], [-4, 3]], -2 * s, 4.0 * i); sel(ML(k), ML(k), [[0, 4], [-16, 8], [0, 3]], -15, -2.0 * i * i)
-            if i < 3: sel(ML(k, 72), ML(k, 72), P24, -15, -2.0 * i * i - none)
-            else: sel(ML(k, 24, 72), ML(k, 24, 72), [[0, 2], [-16, 8], [0, 3]], -15, -18.0 + none)
-    sel(M("PB"), ap("QI", 2), GP16, -15, 0.0, A.is_equal)
-    for c in range(3):
-        n = "PN%d" % c
-        sel(M(n), M("PB"), GP16, -4 * c - 1, -65536.0); sel(M(n), M(n), GP16, -4 * c - 3, -65536.0)
-        for i in (1, 2, 3):
-            for o, view in ((0, sl(4 * i, 4 * i + 4)), (2, sl(i, 16, 4))): sel(M(n, view), M(n, view), G0P, -4 * c - o, 131072.0 * i)
+    sel(M("VK"), ap("PI"), G16, -15, 0.0, A.is_equal); sel(M("VK"), M("VK"), [[-1, 128]], 0, 1.0)
+    sel(M("VK", 3, sl(3, 4)), M("VK", 3, sl(3, 4)), [[-16, 8]], -15, 15.0)
+    ms(ap("CK"), -32.0 * KU)
+    sel(M("RM"), ap("CK"), G16, 0, 0.0, A.is_ge); sel(M("RM"), M("RM"), [[16, 8], [0, 16]], 15, 0.0, A.is_ge, -1)
+    lin(ap("BO"), M("RM", 0, 0), -1.0); lin(ap("BOF"), M("RM", 0, 0), -1.0 / (32 * KU))
+    for b in range(NB):
+        for p in range(16):
+            o = ap("D1%d" % b, sl(2 * p + 1, 32 * CW, 32))
+            if D1P[b]: sel(o, ap("RQ%d" % b), [[0, CW]], 1, 0.0, A.is_ge, 0)
+            else: lin(o, ap("RQ%d" % b))
+        if b == 0:
+            def ML(k, *idx): return ap("ML", sl(8 * k, 8 * k + 8), *idx)
+            ms(ap("ZL"), 0.0); ZL = ap("ZL"); L12 = [[-16, 8], [0, 12]]; L6 = [[-16, 8], [0, 6]]; mid = sl(1, 3)
+            def cpat(st): return [[-16, 8], [0, 4], [-st, 3]]
+            for i in range(3): sel(ML(i), ZL, [[-16, 8], [-4, 4], [0, 3]], -i, U)
+            sel(ML(3), ZL, L12, -3, U); sel(ML(3, mid), ap("ZL", ALL, mid), L6, 1000, 0.0)
+            for s, none in ((0, 0.5), (1, 0.375)):
+                k0 = 4 + s
+                sel(ML(k0), ZL, cpat(1), -8 - 4 * s, -2.0); sel(ML(k0), ML(k0), cpat(4), -3, 2.0)
+                for i in (1, 2, 3):
+                    k = k0 + 2 * i
+                    sel(ML(k), ML(k0), cpat(1), -4 * s, 4.0 * i); sel(ML(k), ML(k), L12, -15, -2.0 * i * i)
+                sel(ML(k0 + 6, mid), ML(k0 + 6, mid), L6, -15, none - 18.0)
+            iota(ap("QI", 0), [[0, 8], [1, 4], [0, 4]], 0, 0, True); iota(ap("QI", 1), [[0, 32], [1, 4]], 0, 0, True)
+            tt(ap("QI", sl(0, 2)), ap("QI", sl(0, 2)), ap("QI", sl(0, 2)), A.mult); tt(ap("QI", 2), ap("QI", 0), ap("QI", 1), A.add)
+            lin(ap("QI", 2), ap("QI", 2), -65536.0, 65536.0)
+            sel(M("PB"), ap("QI", 2), G16, -15, 0.0, A.is_equal)
+            sel(M("PN"), M("PN"), G16, -8, -65536.0); sel(M("PN"), M("PN"), G16, -12, -65536.0)
+            for i in (1, 2, 3):
+                for row, view in ((0, (i, ALL)), (4, (ALL, i))): sel(M("PN", *view), M("PN", *view), G4, -row, 131072.0 * i)
+            bn = bank(); it = []
+            for c in range(3):
+                o = ap(bn, sl(128 * c, 128 * c + 128)); it += [(o, ap("I0", sl(2 - c, 130 - c)), M("PN")), (o, I, M("PB"))]
+            group(it); k = 8 * MATS.index("PN0"); lin(ap("MT", sl(k, k + 24)), ap(bn, sl(0, 384)))
     ts(ap("PC", sl(1, 2)), ap("PC", sl(0, 1)), 15, A.bitwise_and); ts(ap("PC", sl(2, 3)), ap("PC", sl(0, 1)), 3, A.bitwise_and)
-    p16 = ap("PC", sl(1, 2))
-    ts(bc(0), p16, 12.0, A.is_ge); ts(bc(1), ap("PC", sl(2, 3)), 3.0, A.is_equal); ts(bc(2), p16, 15.0, A.is_equal)
-    for e, h in ((0, 0.5), (1, -0.5)):
-        lin(bc(3 + e), bc(0), -4096.0, h); lin(bc(5 + e), bc(1), 3072.0, h); lin(bc(7 + e), bc(0), -4096.0, bc(5 + e))
-    lin(ap("BC", sl(23, 29)), ap("BC", sl(3, 9)), -256.0); ms(bc(44), -128.0); ms(bc(45), 128.0); ms(bc(46), 3.0); ms(bc(47), 2.0 ** 29)
-    lin(bc(9), bc(1), 8192.0, 4096.0); lin(bc(9), bc(0), -4096.0, bc(9)); lin(bc(10), bc(0), -4096.0)
-    lin(bc(11), bc(2), 1.0, -1.0); lin(bc(12), bc(2), -11.0, 12.0)
-    lin(bc(14), bc(0), TRIV0); lin(bc(15), bc(1), TRIV0)
-    cur[1] = -1
-    for k, s in enumerate("AB"):
-        for q in range(6):
-            c = bc(32 + 6 * k + q)
-            lin(c, bc(k), TRIV[q][0] - 131072.0 * QV[q], 131072.0 * QV[q]); lin(M("D%s%d" % (s, q)), M("I"), c)
-    cur[1] = 0
-    for w in range(3):
-        ts(bc(16), p16, 5.0 * w, A.is_ge); ts(bc(29 + w), p16, 5.0 * w + 5, A.is_lt, bc(16), A.mult)
-        lin(ap("IW", sl(160 * w, 160 * w + 160)), ap("IW0"), bc(29 + w))
-    ms(ap("RS"), 0.0); ms(ap("RS", sl(0, CW, 16)), 2.0 ** 34); ms(ap("RR"), 0.0); ms(ap("RR", sl(15, CW, 16)), 2.0 ** 34)
-    ms(ap("PF"), 0.0); lc = lut_columns(); seen = {}; fills = []
+    p16 = ap("PC", sl(1, 2)); ta, tb, t15 = bc(0), bc(1), bc(2)
+    ts(ta, p16, 12.0, A.is_ge); ts(tb, ap("PC", sl(2, 3)), 3.0, A.is_equal); ts(t15, p16, 15.0, A.is_equal)
+    ts(bc(16), p16, 7.0, A.is_ge, tb, A.mult); lin(bc(3), bc(16), -8191.0, 8192.0); lin(bc(4), t15, 256.0)
+    for w in range(2):
+        ts(bc(16), p16, 5.0 * w, A.is_ge); ts(bc(5 + w), p16, 5.0 * w + 5, A.is_lt, bc(16), A.mult)
+        ts(bc(37 + w), ap("PC", sl(0, 1)), 64.0, A.is_ge, bc(5 + w), A.mult); tt(bc(5 + w), bc(5 + w), bc(37 + w), A.subtract)
+        lin(ap("JW", 2 * w), ap("J0"), bc(5 + w)); lin(ap("JW", 2 * w + 1), ap("J0"), bc(37 + w))
+    lc = lut_columns(); seen = {}; fills = []
     for (n, row), w in sorted(lc.items()):
         for j in range(3):
             val = w[3 * j] + (w[3 * j + 1] << 8) + (w[3 * j + 2] << 16)
@@ -266,147 +291,141 @@ def rank_program(g, core, T, topo):
             while k < len(cs) and cs[k] - cs[k - 1] == st: k += 1
             fill(ap("PF", (32 * j, 32 * j + 32), sl(cs[0], cs[k - 1] + 1, st)), float(val))
             cs = cs[k:]
-    pl = ap("PL"); cp(pl, ap("PF")); ops[-1]["deps"] += fills
-    ts(ap("PS", sl(0, 80)), pl, 255, A.bitwise_and)
-    ts(ap("PS", sl(80, 160)), pl, 8, A.logical_shift_right, 255, A.bitwise_and); ts(ap("PS", sl(160, 240)), pl, 16, A.logical_shift_right)
-    ms(ap("ROW"), 0.0); del fills[:]
+    pl = ap("PL"); cp(pl, ap("PF")); also(fills)
+    ts(ap("PS", sl(0, 64)), pl, 255, A.bitwise_and)
+    ts(ap("PS", sl(64, 128)), pl, 8, A.logical_shift_right, 255, A.bitwise_and); ts(ap("PS", sl(128, 192)), pl, 16, A.logical_shift_right)
+    del fills[:]
     for k in range(8): fill(ap("ROW", sl(32 * (k // 3) + k % 3, 32 * (k // 3) + k % 3 + 1)), 2.0 ** -k)
-    tt(ap("TMP", sl(0, 96)), ap("ROW"), ap("I32", sl(0, 96)), A.mult); ops[-1]["deps"] += fills; red(bc(18), ap("TMP", sl(0, 96)))
+    tt(ap("TMP"), ap("ROW"), ap("I32", sl(0, 96)), A.mult); also(fills); red(bc(18), ap("TMP"))
     i66 = ap("I32", sl(66, 67))
     lin(bc(19), bc(18), 0.5, -0.5); lin(bc(19), i66, 1.5, bc(19))
     for y in range(3): red(bc(20 + y), ap("I32", sl(y, 96, 32)))
-    lin(bc(22), i66, -0.875, bc(22))
-    for y in range(3): ts(ap("PM", sl(80 * y, 80 * y + 80)), ap("PS", sl(80 * y, 80 * y + 80)), bc(20 + y), A.mult)
-    tt(ap("PM", sl(240, 320)), ap("PM", sl(0, 80)), ap("PM", sl(80, 160)), A.add); tt(ap("WC"), ap("PM", sl(240, 320)), ap("PM", sl(160, 240)), A.add)
-    for k in range(8): lin(ap("WL", sl(0, 5), k, sl(0, 16)), ap("WC"))
+    for y in range(3): ts(ap("PM", sl(64 * y, 64 * y + 64)), ap("PS", sl(64 * y, 64 * y + 64)), bc(20 + y), A.mult)
+    tt(ap("PM", sl(192, 256)), ap("PM", sl(0, 64)), ap("PM", sl(64, 128)), A.add)
+    tt(ap("WL", ALL, 0), ap("PM", sl(192, 256)), ap("PM", sl(128, 192)), A.add)
+    for k in (1, 2, 4): lin(ap("WL", ALL, sl(k, 2 * k)), ap("WL", ALL, sl(0, k)))
     ts(ap("TJ"), ap("TI"), bc(18), A.mult, bc(19), A.add); ts(ap("TJ"), ap("TJ"), 1, A.bitwise_and); cp(ap("BT"), ap("TJ"))
-    for n0 in (0, 2, 4):
-        ns = [n for n in (n0, n0 + 1) if n < 5]; bn = bank()
-        group([(ap(bn, sl(256 * (n - n0), 256 * (n - n0) + 256)), ap("WL", n), ap("BT")) for n in ns])
-        lin(ap("LUT", sl(256 * n0, 256 * (ns[-1] + 1))), ap(bn, sl(0, 256 * len(ns))))
-    cp(ap("L0"), ap("fanI"))
-    for w in range(3):
-        for s in range(2): ts(ap("LW3", sl(0, NCH), 2 * w + s), ap("fanI", sl(32 * s, 32 * s + 32)), 3.0, A.mult, float(w), A.add)
-    cp(ap("LWL"), ap("LW3"))
-    for p in range(16): lin(ap("D1", sl(2 * p + 1, 32 * V, 32)), ap("RQ"))
-    for b in range(2):
-        b = str(b)
-        ms(ap("SS" + b), 0.0); ms(ap("SS" + b, sl(0, NVB * 8), sl(15, 16)), 1.0); ms(ap("FT" + b), 0.0); ms(ap("FL" + b), 0.0)
-        ms(ap("D0" + b, sl(0, 4096, 2)), -1.0)
-    op("V", lambda q: q.tensor_copy(T.INF[0:120, :], T.INI[0:120, :]), [ap("INI")], [ap("INF")], vc(512)); ops[-1]["deps"].append(tabop)
-
-    def sm(b, k, n=1): return ap("SM" + b, sl(k * N24, (k + n) * N24))
-    def si(b, k): return ap("SI" + b, sl(k * N24, (k + 1) * N24))
-    def prep(rnd, ch, b):
-        v0 = ch * CW; w0, wb = "W0%d" % rnd, "WB%d" % rnd
-        fs = lambda a, c, d=1: ap("FS" + b, sl(0, NVB * 8), sl(a, c, d))
-        own = ap("SM" + b, sl(22 * N24 + ch // 2 * NVB * 8, 22 * N24 + (ch // 2 + 1) * NVB * 8))
-        if rnd == 0:
-            t = ap("TMP", sl(96 + ch * NVB * 8, 96 + (ch + 1) * NVB * 8))
-            iota(t, [[128, NVB], [0, 8]], V * rank + v0, 1, True); lin(own, t, U)
-            tt(sm(b, 0, 4), sm(b, 0, 4), sm(b, 4, 4), A.max)
-        else: tt(sm(b, 1, 2), sm(b, 1, 2), sm(b, 5, 2), A.max)
-        lin(fs(12, 13), own)
-        for k in range(4): lin(fs(k, 12, 4), sm(b, k))
-        lin(sm(b, 8, 3), sm(b, 4, 3), 4.0); tt(sm(b, 12, 3), sm(b, 0, 3), sm(b, 8, 3), A.subtract)
-        lin(sm(b, 15), sm(b, 7), -1.0, 1.0)
-        tt(sm(b, 16, 2), sm(b, 12, 2), sm(b, 14, 2), A.max); tt(sm(b, 16), sm(b, 16), sm(b, 17), A.max); tt(fs(13, 16), sm(b, 16), sm(b, 4), A.max)
-        ts(si(b, 1), si(b, 0), 255, A.bitwise_and); ts(si(b, 2), si(b, 0), 8, A.logical_shift_right)
-        tt(ap("FT" + b, sl(0, NVB * 8), sl(0, 15, 5)), si(b, 2), sm(b, 15), A.mult)
-        tt(sm(b, 18, 2), sm(b, 4, 2), sm(b, 6, 2), A.add); tt(sm(b, 18), sm(b, 18), sm(b, 19), A.add)
-        lin(sm(b, 18), sm(b, 18), -256.0, 1024.0); tt(sm(b, 19), sm(b, 18), si(b, 1), A.add)
-        for h in range(HH):
-            for vb in range(NVB):
-                r = (h * NVB + vb) * 4
-                lin(ap("FL" + b, (h * HN, (h + 1) * HN), sl(0, 8), sl(r, r + 3)), ap("SM" + b, (h * HN, (h + 1) * HN), sl(19 * N24 + 24 * vb, 19 * N24 + 24 * vb + 24)))
+    for n0 in (0, 2):
         bn = bank()
-        group([(ap(bn, sl(vb * 128, vb * 128 + 128)), ap("FS" + b, sl(vb * 8, vb * 8 + 8)), ap("I32")) for vb in range(NVB)])
-        lin(ap(w0, sl(v0, v0 + CW)), ap(bn, sl(0, CW)), 8192.0)
-        bn = bank(); cur[1] = 1
-        group([(ap(bn, sl(0, HN)), ap("FL" + b), ap("I32", sl(h * HN, (h + 1) * HN))) for h in range(HH)])
-        cp(ap("LL" + b), ap(bn, sl(0, HN)))
-        gat(ap("GL" + b), ap("LUT"), ap("LL" + b), "any")
-        for w in range(3):
-            bn = bank()
-            it = [(ap(bn, sl(vb * 128 + h * HN, vb * 128 + (h + 1) * HN)), ap("IW", sl(160 * w + 16 + 5 * w - 5 * c, 160 * w + 144 + 5 * w - 5 * c)),
-                   ap("GL" + b, sl((h * NVB + vb) * 4 + c, 16 * HN, 16))) for vb in range(NVB) for h in range(HH) for c in range(3)]
-            if w == 0: it += [(ap(bn, sl(vb * 128, vb * 128 + 128)), ap("FT" + b, sl(vb * 8, vb * 8 + 8)), ap("I32")) for vb in range(NVB)]
-            group(it)
-            lin(ap(wb, sl(3 * v0 + w, 3 * (v0 + CW), 3)), ap(bn, sl(0, CW)), 1.0, bc(2))
-        cur[1] = 0
-        if v0 < G <= v0 + CW:
-            for kind, name, m in ((0, w0, 1), (1, wb, 3)):
-                def send(q, kind=kind, name=name, m=m):
-                    tr = []
-                    for d in range(1, NR):
-                        rid, pid, se = topo.addr(T.cores[(rank + d) % NR]); o = m * (V + (d - 1) * G)
-                        tr.append(RemoteDMATransfer(dst_ids=[DstId(rid=rid, pnc=pid)], dma_engine_mask=masks(T, topo, rank)[d - 1],
-                                                    remote_sem=T.sem["arr%d%d" % (rnd, kind)], src=T[name][:, 0:m * G], dst=T[name][:, o:o + m * G]))
-                    q.remote_dma_fused(tr, local_sem=T.sem.sent)
-                op("P", send, [ap(name, sl(0, m * G))], [], 1.0, sem="none")
-                me = len(ops) - 1
-                n = sum(bin(masks(T, topo, (rank - d) % NR)[d - 1]).count("1") for d in range(1, NR))
-                op("X", None, [], [ap(name, sl(m * V, m * W))], 0.0, lat=5.0 + 3.0 * kind, sem="arr%d%d" % (rnd, kind), val=n)
-                ops[-1]["deps"].append(me)
+        group([(ap(bn, (H0, H1)[u]), ap("WL", n0 + u), ap("BT")) for u in range(2)])
+        lin(ap("LUT", sl(256 * n0, 256 * n0 + 512)), ap(bn))
+    LN = math.log(9 / 7)
+    ms(bc(7), LN); lin(bc(8), ta, 4096.0 * 256, LN); lin(bc(9), tb, -3072.0 * 256, LN); lin(bc(10), ta, 4096.0 * 256, bc(9)); lin(bc(11), tb, -2.0 ** 24, LN)
+    for u, s in enumerate("AB"):
+        for k in range(3): lin(bc(24 + 3 * u + k), (ta, tb)[u], 3.0 * FOLD[s][k], float(OFF[s][k]))
+        lin(bc(14 + u), (ta, tb)[u], float(TRIV[4]))
+    lin(bc(30), ta, 3 * muA, 176.0 - THR - sum(m * o for m, o in zip(UW, OFF["A"])) / 16); lin(bc(30), tb, 3 * MUW, bc(30))
+    lin(bc(31), t15, 2.0 ** 20, 0.0); tt(bc(31), bc(31), bc(30), A.subtract); lin(bc(32), t15, -1.0, 1.0); lin(bc(32), t15, KU, bc(32))
+    lin(bc(33), t15, 128.0, -128.0); ts(bc(34), bc(30), bc(33), A.mult); lin(bc(34), t15, KU, bc(34))
+    pp = ap("PC", sl(0, 1))
+    ts(bc(35), pp, 96.0, A.is_lt, 8191.0, A.mult); lin(bc(35), bc(35), 1.0, 1.0)
+    ts(bc(16), pp, 96.0, A.is_ge); ts(bc(36), pp, 108.0, A.is_lt, bc(16), A.mult); lin(bc(36), bc(36), 1.0, -1.0)
+    for name, w in [("U9", 9 / 16), ("U7", -7 / 16), ("X9", 9.0), ("nI", -1.0)] + [("D%d" % v, 65536.0 * v) for v in SIG]: lin(M(name), I, w)
+    ms(ap("TV", (0, 64)), 0.0); ms(ap("ON", (0, 64)), 1.0); del fills[:]
+    TVQ = [(s, q) for s in "AB" for q in (1, 2, 5)]
+    for k, (s, q) in enumerate(TVQ):
+        for p, v in ((0, TRIV[q] & 0xFF00), (32, TRIV[q] & 0xFF)):
+            if v: fill(ap("TV", (p, p + 1), sl(8 * k, 8 * k + 8), *last(s)), float(v))
+    tvf = list(fills)
+    ms(ap("RS"), 0.0); ms(ap("RS", sl(0, CW, 16)), 2.0 ** 34); ms(ap("RZ"), 1.0); ms(ap("RZ", sl(0, CW, 16)), 0.0)
+    for b in range(NB):
+        b = str(b)
+        for h in range(2): cp(ap("L0" + b, half(h)), ap("FN" + b, half(h), sl(h, 4, 2)))
+        for w in range(2): ts(ap("LW" + b, sl(32 * w, 32 * w + 32)), ap("L0" + b), 2.0, A.mult, float(w), A.add)
+        ms(ap("SS" + b, ALL, 3, 3), 1.0); ms(ap("FT" + b), 0.0); ms(ap("FL" + b), 0.0); ms(ap("ZB" + b), 0.0); ms(ap("FO" + b, sl(16, 20)), 0.0)
+        ms(ap("D0" + b, sl(0, 4096, 2)), -1.0)
+        lin(ap("FS" + b, ALL, 0, 3), ap("OWN", sl(16 * int(b), 16 * int(b) + 16)), U)
+    op("V", lambda q: q.tensor_copy(INF[0:120, :], INI[0:120, :]), [ap("INI")], [ap("INF")], vc(512)); also([tabop])
 
-    for ch in range(NCH):
-        b = str(ch % 2); kb = bank()
-        group([(ap(kb, sl(k * N24 + vb * 24, k * N24 + vb * 24 + 24)), ap("INF", (0, 120), sl(ch * CW + vb * 128, ch * CW + vb * 128 + 128)),
-                ap("I32", (0, 120), sl(k, 96, 4) if k < 4 else sl(96, 120))) for vb in range(NVB) for k in range(5)])
-        lin(sm(b, 0, 4), ap(kb, sl(0, 4 * N24)), U); ts(sm(b, 4, 4), ap(kb, sl(0, 4 * N24)), 0.0, A.is_lt)
-        cp(si(b, 0), ap(kb, sl(4 * N24, 5 * N24)))
-        prep(0, ch, b)
+    def un(b, k, n=1, st=1): return ap("UN" + b, ALL, sl(k, k + (n - 1) * st + 1, st))
+    def si(b, k, n=1): return ap("SI" + b, ALL, sl(k, k + n))
+    def fs(b, k, n=1, st=1): return ap("FS" + b, ALL, sl(k, k + (n - 1) * st + 1, st), sl(0, 3))
+    def prep(rnd, b):
+        wn = str(RO * int(b) + rnd); w0, wb = "W0" + wn, "WB" + wn
+        mu = ap("FS" + b, ALL, sl(1, 4), 3)
+        tt(un(b, 20), un(b, 17), un(b, 18), A.add); tt(un(b, 20), un(b, 20), un(b, 19), A.add); tt(mu, un(b, 20), un(b, 21), A.mult)
+        bn = bank()
+        for d in range(2):
+            group([(ap(bn, half(d), sl(CW * h + 128 * vb, CW * h + 128 * vb + 128)), ap("FS" + b, sl(8 * vb + 4 * h, 8 * vb + 4 * h + 4)), I)
+                   for h in range(2) for vb in range(2)])
+        lin(ap(w0, sl(0, V)), ap(bn), bc(3))
+        ts(si(b, 1), si(b, 0), 255, A.bitwise_and); ts(si(b, 2), si(b, 0), 8, A.logical_shift_right, 255, A.bitwise_and)
+        ts(un(b, 23), mu, 256.0, A.mult); tt(ap("FL" + b, sl(3, 64, 4), sl(0, 3)), un(b, 23), si(b, 1), A.add)
+        ts(un(b, 22), mu, 0.0, A.is_equal); tt(ap("FT" + b, ALL, sl(ROWS[3][1], 15, 5)), si(b, 2), un(b, 22), A.mult)
+        bn = bank(); blocks = [(vb, hh) for vb in range(2) for hh in range(2)]
+        group([(ap(bn, sl(0, 64)), ap("FL" + b, sl(30 * vb + 3 - hh, 30 * vb + 35 - hh)),
+                ap("I0", sl(2 + 64 * hh, 66 + 64 * hh))) for vb, hh in blocks])
+        cp(ap("LL" + b), ap(bn, sl(0, 64)))
+        gat(ap("GL" + b), ap("LUT"), ap("LL" + b), "any")
+        for w in range(2):
+            bn = bank()
+            it = [(ap(bn, sl(CW * h + 128 * vb + 64 * hh, CW * h + 128 * vb + 64 * hh + 64)), ap("JW", 2 * w + h, sl(16 + 5 * w - 5 * c, 144 + 5 * w - 5 * c)),
+                   ap("GL" + b, sl(8 * vb + 4 * hh + c, 1024, 16))) for c in range(3) for h in range(2) for vb, hh in blocks]
+            if w == ROWS[3][0]:
+                it[8:8] = [(ap(bn, half(d), sl(CW * h + 128 * vb, CW * h + 128 * vb + 128)), ap("FT" + b, sl(8 * vb + 4 * h, 8 * vb + 4 * h + 4)), I)
+                       for d in range(2) for h in range(2) for vb in range(2)]
+            group(it)
+            lin(ap(wb, sl(w, 2 * V, 2)), ap(bn), 1.0, bc(4))
+        for kind, name, m in ((0, w0, 1), (1, wb, 2)):
+            def send(q, kind=kind, name=name, m=m):
+                tr = []
+                for d in range(1, NR):
+                    rid, pid, se = topo.addr(T.cores[(rank + d) % NR]); o = m * (V + (d - 1) * G)
+                    tr.append(RemoteDMATransfer(dst_ids=[DstId(rid=rid, pnc=pid)], dma_engine_mask=masks(T, topo, rank)[d - 1],
+                                                remote_sem=T.sem["arr%s%d" % (wn, kind)], src=T[name][:, 0:m * G], dst=T[name][:, o:o + m * G]))
+                q.remote_dma_fused(tr, local_sem=T.sem.sent)
+            op("P", send, [ap(name, sl(0, m * G))], [], 1.0, sem="none")
+            me = len(ops) - 1
+            n = sum(bin(masks(T, topo, (rank - d) % NR)[d - 1]).count("1") for d in range(1, NR))
+            op("X", None, [], [ap(name, sl(m * V, m * W))], 0.0, lat=5.0, sem="arr%s%d" % (wn, kind), val=n)
+            also([me])
+
+    for b in range(NB):
+        kb = bank(); r120 = (0, 120); cur[0] = b
+        group([(ap(kb, sl(60 * (2 * vb + h), 60 * (2 * vb + h + 1))), ap("INF", r120, sl(CW * h + 128 * vb, CW * h + 128 * vb + 128)),
+                ap("SEL", r120, sl(4 * b, 4 * b + 4))) for vb in range(2) for h in range(2)])
+        b = str(b); raw = ap("IN" + b, ALL, sl(0, 4))
+        lin(ap("IN" + b), ap(kb, sl(0, 240)))
+        ts(un(b, 16, 4), raw, 0.0, A.is_lt); lin(un(b, 7, 4), raw, U); cp(si(b, 0), ap("IN" + b, ALL, sl(4, 5)))
+        tt(fs(b, 0, 3), un(b, 7, 3), un(b, 16, 3), A.max)
+        tt(un(b, 11, 2), un(b, 7, 2), un(b, 9, 2), A.max); tt(un(b, 11), un(b, 11), un(b, 12), A.max); tt(fs(b, 3), un(b, 11), un(b, 16), A.max)
+        lin(un(b, 21), un(b, 16), -1.0, 1.0)
+        prep(0, b)
 
     CL = [(1, 0), (2, 0), (0, 1), (0, 2), (1, 1), (1, 2), (2, 1), (2, 2), (0, 0)]
-    H0, H1, H2 = sl(0, CW), sl(CW, 2 * CW), sl(0, 2 * CW)
     for rnd in range(RO):
-        last = rnd == RO - 1; w0, wb = "W0%d" % rnd, "WB%d" % rnd
-        for ch in range(NCH):
-            b = str(ch % 2); kb = "B%d" % (6 + ch % 2); v0 = ch * CW; cur[0] = ch; cur[1] = 1 - ch
+        fin = rnd == RO - 1
+        for bi in range(NB):
+            b = str(bi); kb = "B%d" % (6 + bi); wn = str(RO * bi + rnd); w0, wb = "W0" + wn, "WB" + wn; cur[0] = NB * rnd + bi; cur[1] = 1
             ga, gb = ap("G0" + b, H0), ap("G0" + b, H1)
-            gat(ga, ap(w0), ap("L0", sl(ch * LW, (ch + 1) * LW)), 4096.0); gat(gb, ap(w0), ap("L0", sl(32 + ch * LW, 32 + (ch + 1) * LW)), 3072.0)
-            for w in range(3):
-                gat(ap("GW" + b, sl(2 * w * CW, 2 * (w + 1) * CW)), ap(wb), ap("LWL", sl((6 * ch + 2 * w) * LW, (6 * ch + 2 * w + 2) * LW)), "any")
-            ts(ap("FG" + b, H0), ga, 3000.0, A.is_lt, 8.0, A.mult); ts(ap("FG" + b, H1), gb, 3000.0, A.is_lt, -8.0, A.mult)
+            gat(ga, ap(w0), ap("L0" + b, sl(0, 16)), 4096.0); gat(gb, ap(w0), ap("L0" + b, sl(16, 32)), 3072.0)
+            for w in range(2): gat(ap("GW" + b, sl(2 * w * CW, 2 * (w + 1) * CW)), ap(wb), ap("LW" + b, sl(32 * w, 32 * w + 32)), "any")
             gw = lambda w, s: ap("GW" + b, sl((2 * w + s) * CW, (2 * w + s + 1) * CW))
-            for t, bias in ((0, 3), (2, 5), (4, 7), (6, 7), (8, None)):
-                bn = bank(); cs = CL[t:t + 2]; it = []
-                for u, (k, l) in enumerate(cs): it += [(ap(bn, (H0, H1)[u]), M("A%d" % k), ga), (ap(bn, (H0, H1)[u]), M("B%d" % l), gb)]
+            hh = lambda t, n=1: ap("HH" + b, sl(t * CW, (t + n) * CW))
+            fe = lambda s, k: ap("FE" + b, sl((3 * s + k) * CW, (3 * s + k + 1) * CW))
+            for t, bias in ((0, 8), (2, 9), (4, 10), (6, 10)):
+                bn = bank(); it = []
+                for u, (k, l) in enumerate(CL[t:t + 2]): it += [(ap(bn, (H0, H1)[u]), M("A%d" % k), ga), (ap(bn, (H0, H1)[u]), M("B%d" % l), gb)]
+                group(it); act(hh(t, 2), ap(bn), F.Sigmoid, bc(bias), 256.0)
+            bn = bank(); group([(ap(bn, H0), M("A0"), ga), (ap(bn, H0), M("B0"), gb)]); act(hh(8), ap(bn, H0), F.Sigmoid, bc(7), 256.0)
+            for k in range(3):
+                bn = bank(); it = [(ap(bn, H0), M("TA%d" % k), ga), (ap(bn, H1), M("TB%d" % k), gb)]
+                for l in range(3): it += [(ap(bn, H0), I, hh(CL.index((k, l)))), (ap(bn, H1), I, hh(CL.index((l, k))))]
                 group(it)
-                for e, name in ((0, "SG"), (1, "SE")):
-                    either(ap(name + b, sl(t * CW, (t + len(cs)) * CW)), ap(bn, sl(0, len(cs) * CW)),
-                           (F.Sigmoid, bc(44 + e) if bias is None else bc(20 + bias + e), 256.0), ((0.5, -0.5)[e] if bias is None else bc(bias + e), A.is_gt))
-            bn = bank()
-            group([(ap(bn, H0), M("AL"), ga), (ap(bn, H0), M("B3"), gb), (ap(bn, H1), M("A3"), ga), (ap(bn, H1), M("BL"), gb)])
-            ts(ap("EQ" + b, H0), ap(bn, H0), bc(9), A.is_equal); ts(ap("EQ" + b, H1), ap(bn, H1), bc(10), A.is_equal)
-            sg = lambda k, l: ap("SG" + b, sl(CL.index((k, l)) * CW, (CL.index((k, l)) + 1) * CW))
-            se = lambda k, l: ap("SE" + b, sl(CL.index((k, l)) * CW, (CL.index((k, l)) + 1) * CW))
-            for k in (1, 2):
-                bn = bank(); it = [(ap(bn, H0), M("A%d" % k), ap("FG" + b, H0)), (ap(bn, H1), M("B%d" % k), ap("FG" + b, H1))]
-                for l in range(3):
-                    it += [(ap(bn, H0), M("I"), sg(k, l)), (ap(bn, H1), M("I"), sg(l, k - 1))]
-                for l in range(3):
-                    it += [(ap(bn, H0), M("nI"), se(k - 1, l)), (ap(bn, H1), M("nI"), se(l, k))]
-                group(it)
-                lin(ap("RW" + b, (H0, H1)[k - 1]), ap(bn, H0))
-                either(ap("R12" + b, sl((k - 1) * 2 * CW, k * 2 * CW)), ap(bn, H2), (F.Relu, -8.0, 1.0), (-8.0, A.add, 0.0, A.max))
-            bn = bank(); it = [(ap(bn, H1), M("nI"), se(l, 0)) for l in range(3)] + [(ap(bn, H0), M("I"), sg(0, l)) for l in range(3)]
-            it += [(ap(bn, (H0, H1)[s]), M(("I3", "I2")[k]), ap("R12" + b, sl((2 * k + s) * CW, (2 * k + s + 1) * CW))) for k in range(2) for s in range(2)]
-            group(it); lin(ap("IX" + b, H0), ap(bn, H0)); lin(ap("IX" + b, H1), ap(bn, H1), 1.0, bc(46))
-            cur[1] = 0; bn = bank(); it = [(ap(bn, H0), M("FA"), ap("FG" + b, H0)), (ap(bn, H0), M("FB"), ap("FG" + b, H1))]
-            it += [(ap(bn, H0), M("nI"), sg(0, l)) for l in range(3)] + [(ap(bn, H0), M("I"), se(2, l)) for l in range(3)]
-            it += [(ap(bn, H0), M(m), ap(nm + b, h)) for m, nm in (("I", "EQ"), ("nI", "RW")) for h in (H0, H1)]
-            group(it); act(ap("VD" + b), ap(bn, H0), F.Relu, bc(12), bc(11)); cur[1] = 1 - ch
+                for s in range(2): lin(fe(s, k), ap(bn, (H0, H1)[s]), 16.0, bc(24 + 3 * s + k))
             prev = None
-            for q in range(6):
+            for q in LINES:
                 bn = bank(); it = []
                 for s, h in ((0, H0), (1, H1)):
-                    it += [(ap(bn, h), M("Z%s%d" % ("AB"[s], q)), gw(q // 2, s)), (ap(bn, h), M("D%s%d" % ("AB"[s], q)), ap("IX" + b, h))]
-                prev = group(it, prev)
-                if q == 0:
+                    S = "AB"[s]
+                    it += [(ap(bn, h), M("D%d" % v), fe(s, k)) for k, v in enumerate(SLOPE[S][q]) if v]
+                    it += [(ap(bn, h), M("Z%s%d" % (S, q)), gw(ROWS[q][0], s))]
+                    if (S, q) in TVQ:
+                        k = TVQ.index((S, q)); it += [(ap(bn, h), ap("TV", (0, 33), sl(8 * k, 8 * k + 8)), ap("ON", (0, 33)))]
+                prev = group(it, prev); ops[prev]["deps"] += [z for z in tvf if z not in ops[prev]["deps"]]
+                if q == LINES[0]:
                     for s, h in ((0, H0), (1, H1)): lin(ap("AC" + b, h), ap(bn, h), 1.0, bc(14 + s))
-                else: tt(ap(("EI" if q == 5 else "AC") + b), ap(bn, H2), ap("AC" + b), A.max)
-            cur[1] = 0
+                else: tt(ap(("EI" if q == LINES[-1] else "AC") + b), ap(bn), ap("AC" + b), A.max)
             for e, mk in ((0, 0x5555), (1, 0xAAAA)):
                 ts(ap("ME" + b, sl(2 * e * CW, 2 * (e + 1) * CW)), ap("EI" + b), mk, A.bitwise_and)
             for e, mk in ((0, 0x5555), (1, 0xAAAA)):
@@ -418,124 +437,154 @@ def rank_program(g, core, T, topo):
             ts(ap("T5" + b), nf, -1.0 / 32, A.mult, 65519.5 / 32, A.add)
             bn = bank(); ts(ap(bn, H0), ap("T5" + b), 29.0, A.mult, 65535.0, A.add)
             tt(ap("T5" + b), ap(bn, H0), nf, A.subtract); ts(ap("T5" + b), ap("T5" + b), 8191, A.bitwise_and); cp(ap("C1" + b), ap("T5" + b))
+            cur[1] = 0
+            bn = bank()
+            group([(ap(bn, H0), M("AL"), ga), (ap(bn, H0), M("BK"), gb), (ap(bn, H1), M("AK"), ga), (ap(bn, H1), M("BL"), gb)])
+            act(hh(9), ap(bn, H0), F.Sigmoid, bc(11), 256.0); act(hh(10), ap(bn, H1), F.Sigmoid, bc(8), 256.0)
+            bn = bank(); o = ap(bn, H0)
+            it = [(o, M("UA"), ga), (o, M("UB"), gb), (o, M("X9"), hh(9)), (o, M("X9"), hh(10))] + [(o, M("U%d" % abs(m)), fe(0, k)) for k, m in enumerate(UW)]
+            group(it, close=not OPEN); lin(ap("RR" + b), o, 1.0, bc(30))
+            if OPEN: mm(o, M("nI"), ap("RR" + b), False, True)
+            else: bn = bank(); o = ap(bn, H0); group([(o, l, r) for _, l, r in it] + [(o, M("nI"), ap("RR" + b))])
+            either(ap("VD" + b), o, (F.Relu, bc(34), bc(33)), (bc(31), A.is_lt, bc(32), A.mult))
             blk = lambda name, vb, o=0, p=(0, 128): ap(name, p, sl(o + vb * 128, o + vb * 128 + 128))
-            it = [(blk(kb, vb), blk("VD" + b, vb), M("VK")) for vb in range(NVB)]
-            if last: it += [(blk(kb, vb), blk("RQ", vb, v0), M("RM")) for vb in range(NVB)]
+            it = [(blk(kb, vb), blk("VD" + b, vb), M("VK")) for vb in range(2)]
+            if fin: it += [(blk(kb, vb), blk("RQ" + b, vb), M("RM")) for vb in range(2)]
             for k, t in enumerate(it): mm(t[0], t[1], t[2], k == 0, False)
-            for vb in range(NVB):
-                r = str((ch * NVB + vb) % 2); o = 32 * (v0 + vb * 128); m = 128 // GP
+            for vb in range(2):
+                r = str(vb); o = 32 * 128 * vb; m = 128 // GP
                 for h in range(GP):
                     c = sl(vb * 128 + h * m, vb * 128 + (h + 1) * m); lo, hi = 32 * h * m, 32 * (h + 1) * m
-                    gat(ap("D0" + r, sl(lo + 1, hi, 2)), ap("CE"), ap("C2" + b, c), "any"); gat(ap("D1", sl(o + lo, o + hi, 2)), ap("CE"), ap("C1" + b, c), "any")
-                    scan(ap("MX" + r, sl(lo, hi)), ap("D0" + r, sl(lo, hi)), ap("D1", sl(o + lo, o + hi)), A.min, A.max)
+                    gat(ap("D0" + r, sl(lo + 1, hi, 2)), ap("CE" + b), ap("C2" + b, c), "any")
+                    gat(ap("D1" + b, sl(o + lo, o + hi, 2)), ap("CE" + b), ap("C1" + b, c), "any")
+                    scan(ap("MX" + r, sl(lo, hi)), ap("D0" + r, sl(lo, hi)), ap("D1" + b, sl(o + lo, o + hi)), A.min, A.max)
                 for p in range(16):
-                    mm(ap(kb, sl(vb * 128 + p, vb * 128 + 128, 16)), ap("MX" + r, sl(2 * p + 1, 4096, 32)), ap("BO"), False, p == 15 and vb == NVB - 1)
-            key = ap(kb, H0); rv = sl(CW - 1, None, -1); s1 = "S1" + b
+                    mm(ap(kb, sl(vb * 128 + p, vb * 128 + 128, 16)), ap("MX" + r, sl(2 * p + 1, 4096, 32)), ap("BO"), False, not OPEN and p == 15 and vb == 1)
+            key = ap(kb, H0); s1 = "S1" + b
             for c in range(3):
                 scan(ap(s1), ap("RS"), key, A.add, A.min)
+                lin(ap("ZB" + b, sl(0, CW, 16), c), ap(s1, sl(15, CW, 16)), 1.0, 16 * KU)
                 if c < 2:
-                    scan(ap("KB" + b, rv), ap("RR", rv), ap(s1, rv), A.add, A.min)
-                    tt(ap("DD" + b), key, ap("KB" + b), A.subtract)
-                    either(ap("DD" + b), ap("DD" + b), (F.Relu, bc(47), -2.0 ** 25), (16.0, A.is_lt, 2.0 ** 26, A.mult)); tt(key, key, ap("DD" + b), A.add)
-                lin(ap("SM" + b, sl(12 * N24 + c, 13 * N24, 3)), ap(s1, sl(15, CW, 16)))
-            ts(si(b, 3), sm(b, 12), 2.0 ** 25, A.min); ksel = len(ops) - 1; ts(sm(b, 13), sm(b, 12), 2.0 ** 24, A.is_ge)
+                    scan(ap("KB" + b), ap("RZ"), ap("ZB" + b, ALL, c), A.mult, A.add)
+                    tt(ap("OB" + b), key, ap("KB" + b), A.is_lt)
+                    if OPEN: mm(key, I, ap("OB" + b), False, c == 1)
+                    else: tt(key, key, ap("OB" + b), A.max)
+            keys = ap("ZB" + b, sl(0, CW, 16))
+            ts(si(b, 3), keys, 1.0, A.min, 1 / KU, A.mult); ksel = len(ops) - 1
             ts(si(b, 4), si(b, 3), 2, A.logical_shift_right, 3, A.bitwise_and); ts(si(b, 5), si(b, 3), 3, A.bitwise_and)
-            ss = lambda a, c, d=1: ap("SS" + b, sl(0, NVB * 8), sl(a, c, d))
-            for s in range(2):
-                cp(ss(2 * s, 12, 4), si(b, 4 + s)); act(ss(2 * s + 1, 12, 4), ss(2 * s, 12, 4), F.Square)
-            lin(ss(12, 15), sm(b, 13))
+            ss = lambda t: ap("SS" + b, ALL, sl(t, t + 2), sl(0, 3))
+            cp(ss(0), si(b, 4, 2)); act(ss(2), ss(0), F.Square); ts(ap("SS" + b, ALL, sl(0, 3), 3), keys, 0.5, A.is_ge)
             bn = bank(); prev = None
-            group([(blk(bn, vb), ap("SS" + b, sl(vb * 8, vb * 8 + 8)), M("I")) for vb in range(NVB)])
+            group([(blk(bn, vb), ap("SS" + b, sl(vb * 8, vb * 8 + 8)), I) for vb in range(2)])
             lin(ap("SR" + b), ap(bn, H0))
             xn = [("AC" + b, 0), ("AC" + b, CW), ("KB" + b, 0)]
             for c in range(3):
                 bn = bank(); group([(ap(bn, H0), M("PN%d" % c), ap("SR" + b))])
                 tt(ap(xn[c][0], sl(xn[c][1], xn[c][1] + CW)), ap(bn, H0), nf, A.min)
             bn = bank()
-            group([(ap(bn, sl(vb * 24 + c, vb * 24 + 24, 3)), blk(xn[c][0], vb, xn[c][1]), ap("BOF")) for c in range(3) for vb in range(NVB)])
-            ts(si(b, 0), ap(bn, sl(0, N24)), -1.0, A.mult, 65535.0, A.add); ts(si(b, 0), si(b, 0), 65535, A.bitwise_and)
+            group([(ap(bn, sl(vb * 24 + c, vb * 24 + 24, 3)), blk(xn[c][0], vb, xn[c][1]), ap("BOF")) for c in range(3) for vb in range(2)])
+            ts(si(b, 0), ap(bn, sl(0, 48)), -1.0, A.mult, 65535.0, A.add)
             for i in range(4):
                 bn = bank(); it = []
                 for s in range(2):
-                    for vb in range(NVB):
-                        o = ap(bn, sl((s * NVB + vb) * 96, (s * NVB + vb + 1) * 96))
+                    for vb in range(2):
+                        o = ap(bn, sl((2 * s + vb) * 96, (2 * s + vb + 1) * 96))
                         it += [(o, blk("G0" + b, vb, s * CW), ML(i)), (o, blk("SR" + b, vb), ML(4 + 2 * i + s))]
-                prev = group(it[0::2] + it[1::2], prev, ksel); o = ap(bn, sl(0, 2 * NVB * 96))
+                prev = group(it[0::2] + it[1::2], prev, ksel); o = ap(bn, sl(0, 384))
                 if i == 0: lin(ap("LS" + b), o)
                 else: tt(ap("LS" + b), o, ap("LS" + b), A.max)
-            sa, sb = sl(0, NVB), sl(NVB, 2 * NVB)
-            tt(ap("MN" + b, sa, sl(0, 72)), ap("LS" + b, sa, sl(0, 72)), ap("LS" + b, sb, sl(0, 72)), A.min)
-            tt(ap("MN" + b, sb), ap("LS" + b, sa), ap("LS" + b, sb), A.max)
-            mn = lambda k: ap("MN" + b, sa, sl(24 * k, 24 * k + 24))
-            mx = lambda k: ap("MN" + b, sb, sl(24 * k, 24 * k + 24))
+            sa, sb = sl(0, 16), sl(16, 32)
+            tt(un(b, 0, 3), ap("LS" + b, sa, sl(0, 3)), ap("LS" + b, sb, sl(0, 3)), A.min); tt(un(b, 3, 4), ap("LS" + b, sa), ap("LS" + b, sb), A.max)
             def above(o, a, u): tt(o, a, u, A.is_le); tt(o, o, a, A.max)
-            lin(sm(b, 0), mn(0)); lin(sm(b, 15), mn(2))
-            above(sm(b, 14), mx(0), mn(0)); tt(sm(b, 1), sm(b, 14), mn(1), A.min)
-            above(sm(b, 16), mx(0), sm(b, 1)); above(sm(b, 17), mx(1), sm(b, 1)); above(sm(b, 18), mn(1), sm(b, 1))
-            tt(sm(b, 19, 2), sm(b, 15, 2), sm(b, 17, 2), A.min); tt(sm(b, 2), sm(b, 19), sm(b, 20), A.min)
-            above(sm(b, 3), mx(3), sm(b, 2))
-            ts(sm(b, 4, 4), sm(b, 0, 4), 0.3, A.is_ge)
-            if not last:
-                prep(rnd + 1, ch, b)
+            above(un(b, 11), un(b, 3), un(b, 0)); tt(un(b, 8), un(b, 11), un(b, 1), A.min); tt(un(b, 12), un(b, 11), un(b, 1), A.max)
+            above(un(b, 13), un(b, 12), un(b, 8)); above(un(b, 14), un(b, 4), un(b, 8))
+            tt(un(b, 15), un(b, 14), un(b, 2), A.min); tt(un(b, 9), un(b, 15), un(b, 13), A.min)
+            if not fin:
+                lin(fs(b, 0, 2, 3), un(b, 0, 2, 6)); ts(un(b, 21), keys, 0.5, A.is_lt)
+                ts(un(b, 17, 2), un(b, 8, 2), 0.3, A.is_ge); tt(fs(b, 1, 2), un(b, 8, 2), un(b, 17, 2), A.max); tt(un(b, 19), un(b, 6), un(b, 9), A.is_le)
+                cur[1] = 1; prep(rnd + 1, b)
             else:
-                lin(sm(b, 8, 4), sm(b, 0, 4), 1.0, U); lin(sm(b, 4, 4), sm(b, 4, 4), -1.0, 1.0)
-                for k in range(4): tt(ap("FO" + b, sl(k, 4 * N24, 4)), sm(b, 8 + k), sm(b, 4 + k), A.mult)
-                lin(sm(b, 14), sm(b, 13), -1.0, 1.0); tt(sm(b, 15), si(b, 0), sm(b, 14), A.mult)
-                ts(si(b, 4), si(b, 3), 5, A.logical_shift_right); tt(sm(b, 16), si(b, 4), sm(b, 14), A.mult); tt(sm(b, 16), sm(b, 16), sm(b, 13), A.subtract)
-                bn = bank(); kb = bank()
-                group([(blk(bn, vb, 0, (0, 96)), ap("FO" + b, sl(vb * 96, vb * 96 + 96)), ap("I32")) for vb in range(NVB)])
-                lin(ap("INF", (0, 96), sl(v0, v0 + CW)), ap(bn, (0, 96), H0), 8192.0, -1.0)
-                group([(blk(kb, vb, u * CW, (0, 24)), ap("SM" + b, sl((15 + u) * N24 + vb * 24, (15 + u) * N24 + vb * 24 + 24)), ap("I32")) for u in range(2) for vb in range(NVB)])
-                lin(ap("W00", (0, 24), sl(256 + v0, 256 + v0 + CW)), ap(kb, (0, 24), H0)); lin(ap("OC", (0, 24), sl(v0, v0 + CW)), ap(kb, (0, 24), H1))
-    dma("oyt", T.yt[:, :], T.W00[0:24, 256:256 + V], [ap("W00", sl(256, 256 + V))], [], 5e4); dma("oyc", T.yc[:, :], T.OC[0:24, :], [ap("OC")], [], 5e4)
-    dma("oyl", T.yl[:, :], T.INF[0:96, :], [ap("INF")], [], 2e5)
+                lin(un(b, 7), un(b, 0)); above(un(b, 10), un(b, 6), un(b, 9))
+                ts(un(b, 16, 4), un(b, 7, 4), 0.3, A.is_ge, -4.0, A.mult)
+                for c in range(3): tt(ap("FO" + b, sa, c), ap("UN" + b, ALL, sl(7, 11), c), ap("UN" + b, ALL, sl(16, 20), c), A.add)
+                ts(un(b, 21), keys, 0.5, A.is_ge, -2.0 ** 22, A.mult)
+                ts(si(b, 1), si(b, 0), 65535, A.bitwise_and); ts(si(b, 2), si(b, 3), 5, A.logical_shift_right)
+                for u in range(2): tt(ap("FP" + b, ALL, u), si(b, 1 + u), un(b, 21), A.add)
+                bn = bank(); at = lambda k: sl(CW * (k % 2) + 128 * (k // 2), CW * (k % 2) + 128 * (k // 2) + 128)
+                group([(ap(bn, (0, 96), at(k)), ap("FO" + b, sl(4 * k, 4 * k + 8)), I) for k in range(4)])
+                group([(ap(bn, (96, 120), at(k)), ap("FP" + b, k), ap("I32")) for k in range(4)])
+                r120 = (0, 120); out = T["AC" + b]; r = sl(4 * bi, 4 * bi + 4)
+                ts(ap("AC" + b, r120), ap(bn, r120), ap("BC", r120, sl(35, 36)), A.mult, ap("BC", r120, sl(36, 37)), A.max)
+                dma("oyl" + b, T.yl[r, :], out[0:48, :], [ap("AC" + b)], [], 1e5)
+                dma("oyt" + b, T.yt[r, :], out[96:108, :], [ap("AC" + b)], [], 3e4); dma("oyc" + b, T.yc[r, :], out[108:120, :], [ap("AC" + b)], [], 3e4)
 
     n = len(ops); succ = [[] for _ in ops]
     for k, o in enumerate(ops):
-        for d in o["deps"]: succ[d].append(k)
-    def lag(d, k): return ops[d]["lat"] + (0.0 if ops[d]["eng"] == ops[k]["eng"] == "T" else LAG)
-    def cost(k): return ops[k]["cost"]["A"] if ops[k]["eng"] == "F" else ops[k]["cost"]
-    pri = [0.0] * n
-    for k in range(n - 1, -1, -1): pri[k] = cost(k) + max([lag(k, s) + pri[s] for s in succ[k]] + [ops[k]["lat"]])
-    pri = [p - BIAS * o["ch"] + TB * o["up"] for p, o in zip(pri, ops)]
+        for d in list(o["deps"]):
+            if "pair" in ops[d] and ops[d]["pair"] not in o["deps"]: o["deps"].append(ops[d]["pair"])
+    for o in ops:
+        if "pair" in o: o["deps"].remove(o["pair"])
     for k, o in enumerate(ops):
-        if o["eng"] == "P": pri[k] = 1e6 if o["sem"] or k < 20 or o["cost"] < 0.19 else -k
+        for d in o["deps"]: succ[d].append(k)
     opens = {v[0]: name for name, v in sess.items()}; member = {}
     for name, v in sess.items():
         for k in v: member.setdefault(k, []).append(name)
-    todo = {name: len(v) for name, v in sess.items()}
-    banks = {"B%d" % k: [None, 0.0] for k in range(6)}
-    left = [len(o["deps"]) for o in ops]; rdy = [0.0] * n; free = dict.fromkeys("PTVASX", 0.0); pool = {e: [] for e in "PTVASXF"}; order = []
-    for k in range(n):
-        if not left[k]: pool[ops[k]["eng"]].append(k)
-    while len(order) < n:
-        idle = [(v[1], name) for name, v in banks.items() if v[0] is None or not todo[v[0]]]
-        tb = min(idle)[0] + LAG if idle else 1e9
-        when = lambda k: max(rdy[k], tb) if k in opens else rdy[k]
-        best = None
-        for e in free:
-            own = pool[e]; c = own + pool["F"] if e == "A" else own
-            if e == "V":
-                to = min([max(free[e], when(k)) for k in own] + [1e9])
-                c = own + [k for k in pool["F"] if max(free[e], when(k)) + ops[k]["cost"]["V"] <= min(to + SLACK, max(free["A"], when(k)) + ops[k]["cost"]["A"] - GAIN)]
-            if not c: continue
-            t = max(free[e], min(when(k) for k in c))
-            if best is None or t < best[0]: best = (t, e, c)
-        t, e, c = best
-        k = max((k for k in c if when(k) <= t + 0.03), key=lambda k: pri[k]); o = ops[k]
-        pool[o["eng"]].remove(k); t = max(t, when(k))
-        if o["eng"] == "F": o["eng"], o["fn"], o["cost"] = e, o["fn"][e], o["cost"][e]
-        if k in opens:
-            name = min(idle)[1]; old = banks[name][0]
-            for d in (sess[old] if old else []):
-                if d not in o["deps"]: o["deps"].append(d); succ[d].append(k)
-            banks[name][0] = opens[k]; place[opens[k]] = name
-        free[e] = t + o["cost"]; order.append(k); o["t"] = t
-        for name in member.get(k, []):
-            todo[name] -= 1; banks[place[name]][1] = max(banks[place[name]][1], free[e])
-        for s in succ[k]:
-            rdy[s] = max(rdy[s], free[e] + lag(k, s)); left[s] -= 1
-            if not left[s]: pool[ops[s]["eng"]].append(s)
+    pred = [list(o["deps"]) for o in ops]; lat = [o["lat"] for o in ops]; kind = [o["eng"] for o in ops]
+    def cost(k, e): return ops[k]["cost"][e] if kind[k] == "F" else ops[k]["cost"]
+    def lag(d, k): return lat[d] + (0.0 if kind[d] == kind[k] == "T" else LAG)
+
+    def walk(pri, eng, back):
+        pre, post = (succ, pred) if back else (pred, succ); eng = list(eng)
+        todo = {name: len(v) for name, v in sess.items()}; at = {}; extra = []
+        banks = {"B%d" % k: [None, 0.0] for k in range(6)}
+        left = [len(p) for p in pre]; rdy = [lat[k] if back else 0.0 for k in range(n)]; free = dict.fromkeys("PTVASX", 0.0)
+        pool = {e: [] for e in "PTVASXF"}; order = []; start = [0.0] * n; end = 0.0
+        for k in range(n):
+            if not left[k]: pool[eng[k]].append(k)
+        while len(order) < n:
+            idle = [(v[1], name) for name, v in banks.items() if v[0] is None or not todo[v[0]]]
+            tb = min(idle)[0] + LAG if idle else 1e9
+            when = (lambda k: rdy[k]) if back else (lambda k: max(rdy[k], tb) if k in opens else rdy[k])
+            best = None
+            for e in free:
+                own = pool[e]; c = own + pool["F"] if e == "A" else own
+                if e == "V":
+                    to = min([max(free[e], when(k)) for k in own] + [1e9])
+                    c = own + [k for k in pool["F"] if max(free[e], when(k)) + cost(k, "V") <= min(to + SLACK, max(free["A"], when(k)) + cost(k, "A") - GAIN)]
+                if not c: continue
+                t = max(free[e], min(when(k) for k in c))
+                if best is None or t < best[0]: best = (t, e, c)
+            t, e, c = best
+            k = max((k for k in c if when(k) <= t + LOOK), key=lambda k: pri[k])
+            pool[eng[k]].remove(k); t = max(t, when(k)); eng[k] = e
+            if k in opens and not back:
+                name = min(idle)[1]; old = banks[name][0]
+                extra += [(d, k) for d in (sess[old] if old else [])]
+                banks[name][0] = opens[k]; at[opens[k]] = name
+            free[e] = t + cost(k, e); order.append(k); start[k] = t; end = max(end, free[e] + (0.0 if back else lat[k]))
+            for name in (member.get(k, []) if not back else []):
+                todo[name] -= 1; banks[at[name]][1] = max(banks[at[name]][1], free[e])
+            for s in post[k]:
+                rdy[s] = max(rdy[s], free[e] + (lag(s, k) if back else lag(k, s))); left[s] -= 1
+                if not left[s]: pool[eng[s]].append(s)
+        return end, order, start, eng, at, extra
+
+    if "plan" not in PLAN:
+        pri = [0.0] * n
+        for k in range(n - 1, -1, -1): pri[k] = cost(k, "A") + max([lag(k, s) + pri[s] for s in succ[k]] + [lat[k]])
+        pri = [p - BIAS * (o["ch"] % NB) + TB * o["up"] for p, o in zip(pri, ops)]
+        for k in range(PASSES):
+            w = walk(pri, kind, False)
+            if "plan" not in PLAN or w[0] < PLAN["plan"][0]: PLAN["plan"] = w
+            PLAN.setdefault("log", []).append(round(w[0], 1))
+            b = walk([t + cost(k, e) for k, (t, e) in enumerate(zip(w[2], w[3]))], w[3], True)
+            pri = [t + cost(k, e) for k, (t, e) in enumerate(zip(b[2], b[3]))]
+    end, order, start, eng, at, extra = PLAN["plan"]; place.update(at)
+    for d, k in extra:
+        if d not in ops[k]["deps"]: ops[k]["deps"].append(d); succ[d].append(k)
+    for k, o in enumerate(ops):
+        if o["eng"] == "F": o["eng"], o["fn"], o["cost"] = eng[k], o["fn"][eng[k]], o["cost"][eng[k]]
+        o["t"] = start[k]
     cnt = dict.fromkeys("PTVA", 0); total = {}
     for k in order:
         o = ops[k]
@@ -556,6 +605,6 @@ def rank_program(g, core, T, topo):
             if seen[e].get(s, 0) < v: Q[e].wait_ge(T.sem[s], v); seen[e][s] = v
         ins = o["fn"](Q[e])
         if "inc" in o: ins.then_inc(T.sem[o["sem"]], o["inc"])
-    total["sent"] = 2 * RO * sum(bin(m).count("1") for m in masks(T, topo, rank))
+    total["sent"] = 2 * NB * RO * sum(bin(m).count("1") for m in masks(T, topo, rank))
     for s, v in total.items(): g.wait_ge(T.sem[s], v)
     return ops, order

@@ -7,19 +7,22 @@ V, G, NR, RO, NB = 512, 192, 4, 2, 2
 W = V + (NR - 1) * G
 CW = 256; GP = 2; U = 2.0 ** -13; KU = 2.0 ** -25
 SLOTS = {1: [(0,), (0,), (2,), (2,), (1,), (3,)], 2: [(0, 1), (0, 2), (1, 2), (0, 3), (1, 3), (2, 3)],
-         3: [(0, 1, 3), (0, 1, 2), (0, 1, 2), (0, 2, 3), (0, 1, 2), (1, 2, 3)], 4: [None, None, None, (0, 1, 2, 3), None, None]}
+         3: [(0, 1, 3), (0, 1, 2), None, (0, 2, 3), None, (1, 2, 3)], 4: [None, None, None, (0, 1, 2, 3), None, None]}
 ROWS = {0: (0, 0, 1), 3: (0, 2, 3), 1: (0, 4, 4), 4: (1, 0, 1), 5: (1, 2, 3), 2: (1, 4, 4)}
 LINES = (4, 0, 3, 1, 5, 2)
 TRIV = {1: 0xAAAA, 4: 0xCCCC, 2: 0xF0F0, 5: 0xFF00}
-SLOPE = {"A": ((11, -13, 7), (-5, 2, 0), (14, -13, 6), (-10, 5, 0), (0, 0, 0), (18, -13, 7)),
-         "B": ((5, 0, 0), (15, -7, 3), (-8, 3, 0), (23, -16, 8), (0, 0, 0), (-12, 5, 0))}
-FOLD = {"A": (-6, -29, -51), "B": (2, -12, -45)}
-OFF = {"A": (-28, -52, -60), "B": (-72, -100, -60)}
-HEIGHT = {"A": (-89, -115, -119, -75, -124, 53), "B": (50, 22, -109, -102, -119, -82)}
+SLOPE = {"A": ((0, -11, 5), (-12, 0, 0), (12, -9, 4), (-30, 10, 0), (0, 0, 0), (15, -9, 5)),
+         "B": ((7, 0, 0), (15, -7, 3), (-9, 4, 0), (26, -18, 9), (0, 0, 0), (-19, 9, 0))}
+FOLD = {"A": (-2, -26, -55), "B": (0, -16, -48)}
+OFF = {"A": (0, 19, 5), "B": (-54, -48, -28)}
+HEIGHT = {"A": (70, -68, -79, -127, -153, -86), "B": (12, 54, -76, 95, -119, -90)}
+OFF3 = {"A": (-2, 17, 1), "B": (-8, 41, -53)}
+HEIGHT3 = {"A": (70, -130, -1, -1024, -143, -1), "B": (-1024, 60, -1, 95, -116, -1)}
 UW = (9, 9, -7); MUW = 5 / 64; THR = 4.125 / 16
 SIG = sorted(set(x for s in SLOPE.values() for r in s for x in r if x))
-ZEROED = ["A1", "A2", "B1", "B2", "TA0", "TA1", "TA2", "TB0", "TB1", "TB2", "UA", "UB", "PN"]
-MATS = ZEROED + ["A0", "B0", "AL", "AK", "BL", "BK", "U9", "U7", "X9", "nI", "VK", "RM", "PB", "PN0", "PN1", "PN2"] + \
+ZEROED = ["A1", "A2", "B1", "B2", "TA0", "TA1", "TA2", "TB1", "TB2", "UA", "UB", "PN"]
+MATS = ZEROED + ["A0", "B0", "AL", "AK", "BL", "BK", "U9", "U7", "X9", "RM", "PB", "PN0", "PN1", "PN2", "IM", "PL", "E3", "LA", "LB"] + \
+    ["PL%d" % k for k in range(6)] + \
     ["Z%s%d" % (s, q) for s in "AB" for q in (0, 3, 4, 5)] + ["D%d" % x for x in SIG]
 MATH = ["Z%s%d" % (s, q) for s in "AB" for q in (1, 2)]
 f32, bf, i32, u16, f16 = "float32", "bfloat16", "int32", "uint16", "float16"
@@ -27,22 +30,21 @@ SCRATCH = {}
 def _sb(name, shape, dt, per=1):
     for k in range(per):
         SCRATCH[name + (str(k) if per > 1 else "")] = ("sbuf", [128] + list(shape), dt)
-for _n, _s, _d in (("MT", [len(MATS) * 8, 4, 4], bf), ("MH", [len(MATH) * 8, 4, 4], f16), ("ML", [12 * 8, 4, 3], bf), ("Z3", [8, 4, 4], bf),
-                   ("Z2", [160], bf), ("ZL", [8, 4, 3], bf), ("ZF", [128], f32), ("SEL", [8, 5, 3], f32), ("I0", [130], bf), ("I32", [128], f32),
-                   ("PI", [8, 4, 4], bf), ("CK", [8, 4, 4], bf), ("QI", [3, 128], bf), ("J0", [160], bf), ("JW", [4, 160], bf),
-                   ("TV", [48, 4, 4], bf), ("ON", [CW], bf), ("BO", [8], bf), ("BOF", [8], f32), ("BC", [48], f32), ("PC", [4], i32),
-                   ("ROW", [96], f32), ("TMP", [96], f32), ("OWN", [32], f32), ("PL", [64], i32), ("PF", [64], f32), ("PS", [3 * 64], i32),
-                   ("PM", [4 * 64], f32), ("WL", [4, 8, 16], bf), ("TI", [256], i32), ("TJ", [256], i32), ("BT", [256], bf), ("LUT", [1024], bf),
+for _n, _s, _d in (("MT", [len(MATS) * 8, 4, 4], bf), ("MH", [len(MATH) * 8, 4, 4], f16), ("TM", [8, 4], bf), ("Z3", [8, 4, 4], bf),
+                   ("Z2", [160], bf), ("ZF", [128], f32), ("SEL", [8, 5, 3], f32), ("I0", [136], bf), ("I32", [128], f32),
+                   ("CK", [8, 4, 4], bf), ("QI", [3, 128], bf), ("J0", [160], bf), ("JW", [4, 160], bf),
+                   ("TV", [24, 4, 4], bf), ("ON", [CW], bf), ("BO", [8], bf), ("BOF", [8], f32), ("BC", [48], f32), ("PC", [4], i32),
+                   ("OWN", [32], f32), ("PL", [64], i32), ("PF", [64], f32), ("WL", [4, 8, 16], bf), ("TI", [256], i32), ("TJ", [256], i32), ("BT", [256], bf), ("LUT", [1024], bf),
                    ("RS", [CW], f32), ("RZ", [CW], f32), ("INI", [V], i32), ("INF", [V], f32)):
     _sb(_n, _s, _d)
 for _n, _s, _d in (("W0", [W], f32), ("WB", [2 * W], bf)):
     _sb(_n, _s, _d, NB * RO)
 for _n, _s, _d in (("CE", [8192], bf), ("RQ", [CW], bf), ("FN", [4, 16], i32), ("L0", [32], u16), ("LW", [64], u16), ("D1", [32 * CW], bf),
-                   ("G0", [2 * CW], f16), ("GW", [4 * CW], bf), ("HH", [11 * CW], bf), ("FE", [6 * CW], bf), ("RR", [CW], bf), ("VD", [CW], bf),
-                   ("AC", [2 * CW], f32), ("EI", [2 * CW], i32), ("ME", [4 * CW], i32), ("NF", [CW], f32), ("T5", [CW], i32),
-                   ("C1", [CW], u16), ("C2", [CW], u16), ("D0", [4096], bf), ("MX", [4096], bf), ("S1", [CW], f32), ("KB", [CW], f32),
-                   ("OB", [CW], bf), ("ZB", [CW, 3], f32), ("UN", [16, 24, 3], f32), ("IN", [16, 5, 3], f32), ("SI", [16, 6, 3], i32),
-                   ("SS", [16, 4, 4], bf), ("SR", [CW], bf), ("LS", [32, 4, 3], f32), ("FS", [16, 4, 4], f16), ("FT", [16, 16], bf),
+                   ("G0", [2, CW], f16), ("GW", [4 * CW], bf), ("HH", [9, CW], bf), ("HX", [2, CW], bf), ("FE", [6, CW], bf), ("RR", [CW], bf),
+                   ("VD", [CW], bf), ("AC", [2, CW], f32), ("EI", [2, CW], i32), ("ME", [4, CW], i32), ("NF", [CW], f32), ("T5", [CW], i32),
+                   ("C1", [CW], u16), ("C2", [CW], u16), ("D0", [4096], bf), ("MX", [4096], bf), ("S1", [CW, 3], f32), ("KB", [CW], f32),
+                   ("OB", [CW], bf), ("UN", [16, 28, 3], f32), ("IN", [16, 5, 3], f32), ("SI", [16, 6, 3], i32),
+                   ("SS", [16, 4, 4], bf), ("SR", [CW], bf), ("LS", [16, 4, 3], f32), ("LX", [6, CW], f16), ("FS", [16, 4, 4], f16), ("FT", [16, 16], bf),
                    ("FL", [68, 4], f16), ("LL", [64], u16), ("GL", [1024], bf), ("FO", [20, 3, 4], f16), ("FP", [4, 2, 12], f32)):
     _sb(_n, _s, _d, NB)
 for _k in range(8):
@@ -50,10 +52,14 @@ for _k in range(8):
 DMAS = ["leaf", "tab"] + [x + str(b) + str(h) for x in ("fan", "req", "cel") for b in range(NB) for h in range(2)] + \
     [x + str(b) for x in ("oyl", "oyt", "oyc") for b in range(NB)]
 SEMAPHORES = ["sP", "sT", "sV", "sA", "sent"] + ["d" + x for x in DMAS] + ["arr%d%d" % (r, k) for r in range(NB * RO) for k in range(2)]
-CYC = 0.00083; PEC = 0.00042; LAG = 0.08; FIX = 0.045; GC = 1.56
-SLACK = 0.6; GAIN = 0.3; BIAS = 6.0; TB = 0.0; OPEN = False; D1P = (0, 1); LOOK = 0.03; PASSES = 8
+CYC = 0.00083; PEC = 0.00042; LAG = 0.08; FIX = 0.045; AFIX = 0.02; GC = 1.56; WIRE = 6.0
+VG = ("A", "A", "A", "any")
+SLACK = 0.6; GAIN = 0.1; LEADS = (3, 5, 6, 7, 9); D1P = (0, 1); LOOK = 0.03; PASSES = 6
+XF = (0, 0, 1, 1)
+HS = (1, 1, 1, 1); AS = (2, 1, 1, 2); CS = (1, 1, 1, 2)
 PLAN = {}
-SAME = {"INI": "EI1", "INF": "AC1", "TI": "T50", "TJ": "T51", "PM": "S10", "ME1": "ME0", "GL1": "GL0", "HH1": "HH0", "IN1": "IN0"}
+SAME = {"INI": "EI1", "INF": "AC1", "TI": "T50", "TJ": "T51", "ME1": "ME0", "GL1": "GL0", "HH1": "HH0", "HX1": "HX0", "IN1": "IN0", "LX1": "LX0", "LS1": "LS0",
+        "RR1": "RR0", "OB1": "OB0", "SR1": "SR0", "FO1": "FO0", "FP1": "FP0"}
 for _n in SAME: del SCRATCH[_n]
 
 
@@ -147,13 +153,16 @@ def rank_program(g, core, T, topo):
         op("V", lambda q: q.tensor_tensor(x(o), x(a), x(b), f), [a, b], [o], vc(len(a[2]) * (1 if ps(a) or ps(b) else 2)))
     def cp(o, a): op("V", lambda q: q.tensor_copy(x(o), x(a)), [a], [o], c1(o, a))
     def ms(o, c): op("V", lambda q: q.memset(x(o), c), [], [o], c1(o, o))
+    def mf(o, c):
+        z = ap("CE0", sl(0, len(o[2])))
+        op("F", {"A": actf(o, z, F.Identity, c, 0.0), "V": lambda q: q.memset(x(o), c)}, [z], [o], {"A": vc(len(o[2])) + AFIX, "V": c1(o, o)})
     def red(o, a): op("V", lambda q: q.tensor_reduce(x(o), x(a), AxisListType.X, A.add), [a], [o], vc(len(a[2])))
     def scan(o, a, b, f0, f1):
         op("V", lambda q: q.tensor_tensor_scan(x(o), x(a), x(b), 0.0, f0, f1), [a, b], [o], vc(len(a[2]) * (0.5 if two(o, a, b) else 1)))
     def actf(o, a, f, bias, scale): return lambda q: q.activation(x(o), x(a), f, bias=x(bias), scale=x(scale))
-    def act(o, a, f, bias=0.0, scale=1.0): op("A", actf(o, a, f, bias, scale), [a] + cols(bias, scale), [o], vc(len(a[2])))
+    def act(o, a, f, bias=0.0, scale=1.0): op("A", actf(o, a, f, bias, scale), [a] + cols(bias, scale), [o], vc(len(a[2])) + AFIX)
     def either(o, a, fa, fv):
-        op("F", {"A": actf(o, a, *fa), "V": tsf(o, a, *fv)}, [a] + cols(*fa, *fv), [o], {"A": vc(len(a[2])), "V": c1(o, a)})
+        op("F", {"A": actf(o, a, *fa), "V": tsf(o, a, *fv)}, [a] + cols(*fa, *fv), [o], {"A": vc(len(a[2])) + AFIX, "V": c1(o, a)})
     def lin(o, a, scale=1.0, bias=0.0): either(o, a, (F.Identity, bias, scale), (scale, A.mult, bias, A.add))
     def mm(o, l, r, start=False, stop=False):
         n = max(min(64, len(l[2])), len(r[2])) * (4 if dty(l) == f32 else 1)
@@ -174,6 +183,7 @@ def rank_program(g, core, T, topo):
     def gat(o, win, off, kind):
         w = lambda: x(win).indirect(x(off)); c = 0.07 + GC * len(o[2]) * CYC
         if kind == "any": op("F", {"V": lambda q: q.tensor_copy(x(o), w()), "A": lambda q: q.activation(x(o), w(), F.Copy)}, [win, off], [o], {"A": c, "V": c})
+        elif kind == "A": op("A", lambda q: q.activation(x(o), w(), F.Copy), [win, off], [o], c)
         else: op("V", lambda q: q.tensor_scalar(x(o), w(), kind, None, A.min), [win, off], [o], c)
     def dma(name, o, a, rd, wr, nbytes):
         op("S", lambda q: q.dma_start(o, a), rd, wr, 0.08, lat=2.0 + nbytes / 150e3, sem="d" + name, val=16)
@@ -183,7 +193,8 @@ def rank_program(g, core, T, topo):
         return ap(t, sl(k, k + 8), *idx)
     def bc(k): return ap("BC", sl(k, k + 1))
     def half(h): return (64 * h, 64 * h + 64)
-    I = ap("I0", sl(2, 130)); Z3 = ap("Z3")
+    def shift(k): return ap("I0", sl(8 - k, 136 - k))
+    I = shift(0); Z3 = ap("Z3")
     H0, H1, H2 = sl(0, CW), sl(CW, 2 * CW), sl(0, 2 * CW)
 
     INI, INF = T[SAME["INI"]], T[SAME["INF"]]
@@ -199,14 +210,14 @@ def rank_program(g, core, T, topo):
                 both[(buf, b, h)] = len(ops) - 1
             ops[-1]["deps"].append(both[(buf, b, 0)]); ops[-1]["pair"] = both[(buf, b, 0)]
 
-    ms(ap("ZF"), 0.0); ms(ap("Z2"), 0.0); ms(Z3, 0.0); ms(ap("PF"), 0.0); ms(ap("ROW"), 0.0)
+    ms(ap("ZF"), 0.0); ms(ap("Z2"), 0.0); ms(Z3, 0.0); ms(ap("PF"), 0.0)
     iota(ap("PC", sl(0, 1)), [[0, 1]], 0, 1)
     sel(ap("I32"), ap("ZF"), [[-1, 128]], 0, 1.0); iota(ap("TI"), [[1, 256]], 0, 0)
     ms(ap("SEL"), 0.0)
     sel(ap("SEL", ALL, sl(0, 4)), ap("SEL", ALL, sl(0, 4)), [[-12, 8], [-1, 4], [-4, 3]], 0, 1.0)
     sel(ap("SEL", ALL, 4), ap("SEL", ALL, 4), [[-3, 8], [-1, 3]], -96, 1.0)
     for b in range(NB): iota(ap("OWN", sl(16 * b, 16 * b + 16)), [[128, 2], [CW, 2], [0, 4]], V * rank, 1, True)
-    sel(ap("I0"), ap("Z2", sl(0, 130)), [[-1, 130]], 2, 1.0)
+    sel(ap("I0"), ap("Z2", sl(0, 136)), [[-1, 136]], 8, 1.0)
     sel(ap("J0"), ap("Z2"), [[-1, 160]], 16, 1.0)
     sel(ap("J0", sl(80, 144)), ap("J0", sl(80, 144)), [[-1, 64]], 0, 1.0); sel(ap("J0", sl(16, 80)), ap("J0", sl(16, 80)), [[-1, 64]], -64, 1.0)
     ms(ap("MT", sl(0, 8 * len(ZEROED))), 0.0)
@@ -222,8 +233,9 @@ def rank_program(g, core, T, topo):
         sel(M(s + "L"), Z3, pat(s, 1), -12, w); sel(M(s + "L", *last(s)), ap("Z3", ALL, *last(s)), G4, -3, w)
         sel(M(s + "K"), M(s + "L"), pat(s, 4), -7, 2048.0 * w)
     for s in "AB":
-        for k in range(3): part("T%s%d" % (s, k), s, 4, 7, FOLD[s][k] / 16)
-    muA = MUW - sum(m * t for m, t in zip(UW, FOLD["A"])) / 16
+        for k in range(3):
+            if FOLD[s][k]: part("T%s%d" % (s, k), s, 4, 7, FOLD[s][k] / 16)
+    muA = 5 + MUW - sum(m * t for m, t in zip(UW, FOLD["A"])) / 16
     part("UA", "A", 4, 7, muA); part("UB", "B", 4, 7, MUW)
     for q0, q1 in ((4, 0), (3, 5), (1, 2)):
         for s in "AB":
@@ -232,10 +244,10 @@ def rank_program(g, core, T, topo):
             if hi == lo: part(z, s, 5, lo, 257.0)
             else: part(z, s, 5, hi, 256.0); part(z, s, 5, lo, 1.0)
             sel(M("Z%s%d" % (s, q1)), M(z), G16, -15, 256.0 * HEIGHT[s][q1])
-    for q in (0, 3): sel(M("ZB%d" % q, *last("B")), M("ZB%d" % q, *last("B")), G4, -15, -65536.0)
-    iota(ap("PI"), [[0, 8], [1, 16]], 0, 0, True)
-    sel(M("VK"), ap("PI"), G16, -15, 0.0, A.is_equal); sel(M("VK"), M("VK"), [[-1, 128]], 0, 1.0)
-    sel(M("VK", 3, sl(3, 4)), M("VK", 3, sl(3, 4)), [[-16, 8]], -15, 15.0)
+    for s in "AB":
+        for q in (0, 3, 1, 5, 2):
+            z = M("Z%s%d" % (s, q), *last(s))
+            if HEIGHT3[s][q] != HEIGHT[s][q]: sel(z, z, G4, -15, 256.0 * HEIGHT3[s][q] + (TRIV[q] / 256 if q in (2, 5) else 0.0))
     ms(ap("CK"), -32.0 * KU)
     sel(M("RM"), ap("CK"), G16, 0, 0.0, A.is_ge); sel(M("RM"), M("RM"), [[16, 8], [0, 16]], 15, 0.0, A.is_ge, -1)
     lin(ap("BO"), M("RM", 0, 0), -1.0); lin(ap("BOF"), M("RM", 0, 0), -1.0 / (32 * KU))
@@ -245,18 +257,20 @@ def rank_program(g, core, T, topo):
             if D1P[b]: sel(o, ap("RQ%d" % b), [[0, CW]], 1, 0.0, A.is_ge, 0)
             else: lin(o, ap("RQ%d" % b))
         if b == 0:
-            def ML(k, *idx): return ap("ML", sl(8 * k, 8 * k + 8), *idx)
-            ms(ap("ZL"), 0.0); ZL = ap("ZL"); L12 = [[-16, 8], [0, 12]]; L6 = [[-16, 8], [0, 6]]; mid = sl(1, 3)
-            def cpat(st): return [[-16, 8], [0, 4], [-st, 3]]
-            for i in range(3): sel(ML(i), ZL, [[-16, 8], [-4, 4], [0, 3]], -i, U)
-            sel(ML(3), ZL, L12, -3, U); sel(ML(3, mid), ap("ZL", ALL, mid), L6, 1000, 0.0)
-            for s, none in ((0, 0.5), (1, 0.375)):
-                k0 = 4 + s
-                sel(ML(k0), ZL, cpat(1), -8 - 4 * s, -2.0); sel(ML(k0), ML(k0), cpat(4), -3, 2.0)
-                for i in (1, 2, 3):
-                    k = k0 + 2 * i
-                    sel(ML(k), ML(k0), cpat(1), -4 * s, 4.0 * i); sel(ML(k), ML(k), L12, -15, -2.0 * i * i)
-                sel(ML(k0 + 6, mid), ML(k0 + 6, mid), L6, -15, none - 18.0)
+            TM = ap("TM"); ms(TM, U); KL = 8192.0
+            sel(TM, TM, [[-16, 8], [-4, 4]], 0, 0.0, A.is_ge); sel(TM, TM, [[16, 8], [4, 4]], 3, 0.0, A.is_ge, -1)
+            sel(ap("TM", ALL, 3), ap("TM", ALL, 3), [[-16, 8]], -3, U)
+            sel(M("PL"), Z3, G16, -8, -KL); sel(M("E3"), Z3, G16, -3, 2 * KL); sel(M("LA"), Z3, G16, -15, -16 * KL)
+            for i in (1, 2, 3): sel(M("PL", ALL, i), M("PL", ALL, i), G4, 0, 2 * KL * i)
+            for i in (0, 1, 2): sel(M("LA", ALL, i), M("LA", ALL, i), G4, -15, -KL * i * i)
+            sel(M("LA", 0, sl(3, 4)), M("LA", 0, sl(3, 4)), [[-16, 8]], -15, -9 * KL); lin(M("LB"), M("LA"))
+            for s, none in (("A", 4096.0), ("B", 3072.0)): sel(M("L" + s, sl(1, 3), 3), M("L" + s, sl(1, 3), 3), [[-16, 8], [0, 2]], -15, none - 9 * KL)
+            for u in range(2):
+                bn = bank(); it = []
+                for k in range(3 * u, 3 * u + 3):
+                    o = ap(bn, sl(128 * (k % 3), 128 * (k % 3) + 128)); c, s = k // 2, k % 2
+                    it += [(o, shift(c + 4 * s), M("PL")), (o, shift(4 * c), M("E3")), (o, I, M("L" + "AB"[s]))]
+                group(it); k = 8 * MATS.index("PL%d" % (3 * u)); lin(ap("MT", sl(k, k + 24)), ap(bn, sl(0, 384)))
             iota(ap("QI", 0), [[0, 8], [1, 4], [0, 4]], 0, 0, True); iota(ap("QI", 1), [[0, 32], [1, 4]], 0, 0, True)
             tt(ap("QI", sl(0, 2)), ap("QI", sl(0, 2)), ap("QI", sl(0, 2)), A.mult); tt(ap("QI", 2), ap("QI", 0), ap("QI", 1), A.add)
             lin(ap("QI", 2), ap("QI", 2), -65536.0, 65536.0)
@@ -266,24 +280,25 @@ def rank_program(g, core, T, topo):
                 for row, view in ((0, (i, ALL)), (4, (ALL, i))): sel(M("PN", *view), M("PN", *view), G4, -row, 131072.0 * i)
             bn = bank(); it = []
             for c in range(3):
-                o = ap(bn, sl(128 * c, 128 * c + 128)); it += [(o, ap("I0", sl(2 - c, 130 - c)), M("PN")), (o, I, M("PB"))]
+                o = ap(bn, sl(128 * c, 128 * c + 128)); it += [(o, shift(c), M("PN")), (o, I, M("PB"))]
             group(it); k = 8 * MATS.index("PN0"); lin(ap("MT", sl(k, k + 24)), ap(bn, sl(0, 384)))
     ts(ap("PC", sl(1, 2)), ap("PC", sl(0, 1)), 15, A.bitwise_and); ts(ap("PC", sl(2, 3)), ap("PC", sl(0, 1)), 3, A.bitwise_and)
     p16 = ap("PC", sl(1, 2)); ta, tb, t15 = bc(0), bc(1), bc(2)
     ts(ta, p16, 12.0, A.is_ge); ts(tb, ap("PC", sl(2, 3)), 3.0, A.is_equal); ts(t15, p16, 15.0, A.is_equal)
     ts(bc(16), p16, 7.0, A.is_ge, tb, A.mult); lin(bc(3), bc(16), -8191.0, 8192.0); lin(bc(4), t15, 256.0)
+    lin(bc(39), bc(16), -1.0, 1.0); lin(M("IM"), I, bc(39))
     for w in range(2):
         ts(bc(16), p16, 5.0 * w, A.is_ge); ts(bc(5 + w), p16, 5.0 * w + 5, A.is_lt, bc(16), A.mult)
         ts(bc(37 + w), ap("PC", sl(0, 1)), 64.0, A.is_ge, bc(5 + w), A.mult); tt(bc(5 + w), bc(5 + w), bc(37 + w), A.subtract)
         lin(ap("JW", 2 * w), ap("J0"), bc(5 + w)); lin(ap("JW", 2 * w + 1), ap("J0"), bc(37 + w))
     lc = lut_columns(); seen = {}; fills = []
     for (n, row), w in sorted(lc.items()):
-        for j in range(3):
-            val = w[3 * j] + (w[3 * j + 1] << 8) + (w[3 * j + 2] << 16)
+        for j in range(4):
+            val = w[2 * j] + (w[2 * j + 1] << 8)
             if val: seen.setdefault((j, val), []).append(16 * n + row)
     def fill(o, v):
         z = ap("ZF", (o[0][0].start, o[0][0].stop), sl(0, len(o[2])))
-        op("F", {"A": actf(o, z, F.Identity, v, 1.0), "V": lambda q: q.memset(x(o), v)}, [z, o], [], {"A": vc(1), "V": vc(1)})
+        op("F", {"A": actf(o, z, F.Identity, v, 1.0), "V": lambda q: q.memset(x(o), v)}, [z, o], [], {"A": vc(1) + AFIX, "V": vc(1)})
         fills.append(len(ops) - 1)
     for (j, val), cs in sorted(seen.items()):
         while cs:
@@ -291,20 +306,14 @@ def rank_program(g, core, T, topo):
             while k < len(cs) and cs[k] - cs[k - 1] == st: k += 1
             fill(ap("PF", (32 * j, 32 * j + 32), sl(cs[0], cs[k - 1] + 1, st)), float(val))
             cs = cs[k:]
-    pl = ap("PL"); cp(pl, ap("PF")); also(fills)
-    ts(ap("PS", sl(0, 64)), pl, 255, A.bitwise_and)
-    ts(ap("PS", sl(64, 128)), pl, 8, A.logical_shift_right, 255, A.bitwise_and); ts(ap("PS", sl(128, 192)), pl, 16, A.logical_shift_right)
-    del fills[:]
-    for k in range(8): fill(ap("ROW", sl(32 * (k // 3) + k % 3, 32 * (k // 3) + k % 3 + 1)), 2.0 ** -k)
-    tt(ap("TMP"), ap("ROW"), ap("I32", sl(0, 96)), A.mult); also(fills); red(bc(18), ap("TMP"))
-    i66 = ap("I32", sl(66, 67))
-    lin(bc(19), bc(18), 0.5, -0.5); lin(bc(19), i66, 1.5, bc(19))
-    for y in range(3): red(bc(20 + y), ap("I32", sl(y, 96, 32)))
-    for y in range(3): ts(ap("PM", sl(64 * y, 64 * y + 64)), ap("PS", sl(64 * y, 64 * y + 64)), bc(20 + y), A.mult)
-    tt(ap("PM", sl(192, 256)), ap("PM", sl(0, 64)), ap("PM", sl(64, 128)), A.add)
-    tt(ap("WL", ALL, 0), ap("PM", sl(192, 256)), ap("PM", sl(128, 192)), A.add)
+    p32 = ap("PC", sl(3, 4)); ts(p32, ap("PC", sl(0, 1)), 31, A.bitwise_and); FLOOR = -0.5 + 2.0 ** -9
+    ts(bc(20), p32, 1.0, A.is_equal); lin(bc(21), bc(20), 2.0 ** -8 - 1, 1.0); lin(bc(22), bc(20), FLOOR)
+    lin(ap("PL"), ap("PF"), bc(21), bc(22)); also(fills); ts(ap("PL"), ap("PL"), 255, A.bitwise_and)
+    lin(ap("WL", ALL, 0), ap("PL"))
     for k in (1, 2, 4): lin(ap("WL", ALL, sl(k, 2 * k)), ap("WL", ALL, sl(0, k)))
-    ts(ap("TJ"), ap("TI"), bc(18), A.mult, bc(19), A.add); ts(ap("TJ"), ap("TJ"), 1, A.bitwise_and); cp(ap("BT"), ap("TJ"))
+    for j in range(4): ms(ap("BC", (32 * j, 32 * j + 32), sl(18, 19)), 4.0 ** -j)
+    ts(bc(19), p32, -0.5, A.mult, 1.0, A.add); ts(bc(19), bc(19), 0.0, A.max, bc(18), A.mult)
+    lin(ap("TJ"), ap("TI"), bc(19), FLOOR); ts(ap("TJ"), ap("TJ"), 1, A.bitwise_and); lin(ap("BT"), ap("TJ"))
     for n0 in (0, 2):
         bn = bank()
         group([(ap(bn, (H0, H1)[u]), ap("WL", n0 + u), ap("BT")) for u in range(2)])
@@ -312,30 +321,33 @@ def rank_program(g, core, T, topo):
     LN = math.log(9 / 7)
     ms(bc(7), LN); lin(bc(8), ta, 4096.0 * 256, LN); lin(bc(9), tb, -3072.0 * 256, LN); lin(bc(10), ta, 4096.0 * 256, bc(9)); lin(bc(11), tb, -2.0 ** 24, LN)
     for u, s in enumerate("AB"):
-        for k in range(3): lin(bc(24 + 3 * u + k), (ta, tb)[u], 3.0 * FOLD[s][k], float(OFF[s][k]))
-        lin(bc(14 + u), (ta, tb)[u], float(TRIV[4]))
-    lin(bc(30), ta, 3 * muA, 176.0 - THR - sum(m * o for m, o in zip(UW, OFF["A"])) / 16); lin(bc(30), tb, 3 * MUW, bc(30))
-    lin(bc(31), t15, 2.0 ** 20, 0.0); tt(bc(31), bc(31), bc(30), A.subtract); lin(bc(32), t15, -1.0, 1.0); lin(bc(32), t15, KU, bc(32))
-    lin(bc(33), t15, 128.0, -128.0); ts(bc(34), bc(30), bc(33), A.mult); lin(bc(34), t15, KU, bc(34))
+        for k in range(3): lin(bc(24 + 3 * u + k), (ta, tb)[u], 3.0 * FOLD[s][k] + OFF3[s][k] - OFF[s][k], float(OFF[s][k]))
+        lin(bc(14 + u), (ta, tb)[u], TRIV[4] + 65536.0 * (HEIGHT3[s][4] - HEIGHT[s][4]))
     pp = ap("PC", sl(0, 1))
     ts(bc(35), pp, 96.0, A.is_lt, 8191.0, A.mult); lin(bc(35), bc(35), 1.0, 1.0)
     ts(bc(16), pp, 96.0, A.is_ge); ts(bc(36), pp, 108.0, A.is_lt, bc(16), A.mult); lin(bc(36), bc(36), 1.0, -1.0)
-    for name, w in [("U9", 9 / 16), ("U7", -7 / 16), ("X9", 9.0), ("nI", -1.0)] + [("D%d" % v, 65536.0 * v) for v in SIG]: lin(M(name), I, w)
+    for name, w in [("U9", 9 / 16), ("U7", -7 / 16), ("X9", 9.0)] + [("D%d" % v, 65536.0 * v) for v in SIG]: lin(M(name), I, w)
     ms(ap("TV", (0, 64)), 0.0); ms(ap("ON", (0, 64)), 1.0); del fills[:]
-    TVQ = [(s, q) for s in "AB" for q in (1, 2, 5)]
+    TVQ = [(s, 1) for s in "AB"]
     for k, (s, q) in enumerate(TVQ):
         for p, v in ((0, TRIV[q] & 0xFF00), (32, TRIV[q] & 0xFF)):
             if v: fill(ap("TV", (p, p + 1), sl(8 * k, 8 * k + 8), *last(s)), float(v))
     tvf = list(fills)
-    ms(ap("RS"), 0.0); ms(ap("RS", sl(0, CW, 16)), 2.0 ** 34); ms(ap("RZ"), 1.0); ms(ap("RZ", sl(0, CW, 16)), 0.0)
+    def tv(k, *idx): return ap("TV", (0, 33), sl(8 * k, 8 * k + 8), *idx)
+    base, base3 = [157.0 - THR - sum(m * o for m, o in zip(UW, off["A"])) / 16 for off in (OFF, OFF3)]
+    base3 += 3 * muA
+    for view, v in (((), base), (last("A"), base3), (last("B"), base + 3 * MUW), ((3, sl(3, 4)), base3 + 3 * MUW)):
+        for p, y in ((0, float(math.floor(v))), (32, v - math.floor(v))): ms(ap("TV", (p, p + 1), sl(16, 24), *view), y)
+    mf(ap("RS"), 0.0); mf(ap("RS", sl(0, CW, 16)), 2.0 ** 34); mf(ap("RZ"), KU); mf(ap("RZ", sl(15, CW, 16)), 2.0 ** 34)
     for b in range(NB):
         b = str(b)
-        for h in range(2): cp(ap("L0" + b, half(h)), ap("FN" + b, half(h), sl(h, 4, 2)))
-        for w in range(2): ts(ap("LW" + b, sl(32 * w, 32 * w + 32)), ap("L0" + b), 2.0, A.mult, float(w), A.add)
-        ms(ap("SS" + b, ALL, 3, 3), 1.0); ms(ap("FT" + b), 0.0); ms(ap("FL" + b), 0.0); ms(ap("ZB" + b), 0.0); ms(ap("FO" + b, sl(16, 20)), 0.0)
-        ms(ap("D0" + b, sl(0, 4096, 2)), -1.0)
+        for h in range(2): lin(ap("L0" + b, half(h)), ap("FN" + b, half(h), sl(h, 4, 2)))
+        for w in range(2): lin(ap("LW" + b, sl(32 * w, 32 * w + 32)), ap("L0" + b), 2.0, float(w))
+        mf(ap("SS" + b, ALL, 3, 3), 1.0); ms(ap("FT" + b), 0.0); ms(ap("FL" + b), 0.0)
+        mf(ap("D0" + b, sl(0, 4096, 2)), -1.0)
         lin(ap("FS" + b, ALL, 0, 3), ap("OWN", sl(16 * int(b), 16 * int(b) + 16)), U)
-    op("V", lambda q: q.tensor_copy(INF[0:120, :], INI[0:120, :]), [ap("INI")], [ap("INF")], vc(512)); also([tabop])
+    mf(ap("FO0", sl(16, 20)), 0.0)
+    for h in range(2): lin(ap("INF", (0, 120), h), ap("INI", (0, 120), h)); also([tabop])
 
     def un(b, k, n=1, st=1): return ap("UN" + b, ALL, sl(k, k + (n - 1) * st + 1, st))
     def si(b, k, n=1): return ap("SI" + b, ALL, sl(k, k + n))
@@ -350,19 +362,18 @@ def rank_program(g, core, T, topo):
                    for h in range(2) for vb in range(2)])
         lin(ap(w0, sl(0, V)), ap(bn), bc(3))
         ts(si(b, 1), si(b, 0), 255, A.bitwise_and); ts(si(b, 2), si(b, 0), 8, A.logical_shift_right, 255, A.bitwise_and)
-        ts(un(b, 23), mu, 256.0, A.mult); tt(ap("FL" + b, sl(3, 64, 4), sl(0, 3)), un(b, 23), si(b, 1), A.add)
+        lin(un(b, 23), mu, 256.0); tt(ap("FL" + b, sl(3, 64, 4), sl(0, 3)), un(b, 23), si(b, 1), A.add)
         ts(un(b, 22), mu, 0.0, A.is_equal); tt(ap("FT" + b, ALL, sl(ROWS[3][1], 15, 5)), si(b, 2), un(b, 22), A.mult)
         bn = bank(); blocks = [(vb, hh) for vb in range(2) for hh in range(2)]
-        group([(ap(bn, sl(0, 64)), ap("FL" + b, sl(30 * vb + 3 - hh, 30 * vb + 35 - hh)),
-                ap("I0", sl(2 + 64 * hh, 66 + 64 * hh))) for vb, hh in blocks])
-        cp(ap("LL" + b), ap(bn, sl(0, 64)))
+        group([(ap(bn, sl(0, 64)), ap("FL" + b, sl(31 * vb + 3 - 2 * hh, 31 * vb + 35 - 2 * hh)), ap("I0", sl(8 + hh, 136, 2))) for vb, hh in blocks])
+        lin(ap("LL" + b), ap(bn, sl(0, 64)))
         gat(ap("GL" + b), ap("LUT"), ap("LL" + b), "any")
         for w in range(2):
             bn = bank()
-            it = [(ap(bn, sl(CW * h + 128 * vb + 64 * hh, CW * h + 128 * vb + 64 * hh + 64)), ap("JW", 2 * w + h, sl(16 + 5 * w - 5 * c, 144 + 5 * w - 5 * c)),
-                   ap("GL" + b, sl(8 * vb + 4 * hh + c, 1024, 16))) for c in range(3) for h in range(2) for vb, hh in blocks]
+            it = [(ap(bn, sl(CW * h + 128 * vb, CW * h + 128 * vb + 128)), ap("JW", 2 * w + h, sl(16 + 5 * w - 5 * c, 144 + 5 * w - 5 * c)),
+                   ap("GL" + b, sl(4 * vb + c, 1024, 8))) for c in range(3) for h in range(2) for vb in range(2)]
             if w == ROWS[3][0]:
-                it[8:8] = [(ap(bn, half(d), sl(CW * h + 128 * vb, CW * h + 128 * vb + 128)), ap("FT" + b, sl(8 * vb + 4 * h, 8 * vb + 4 * h + 4)), I)
+                it[4:4] = [(ap(bn, half(d), sl(CW * h + 128 * vb, CW * h + 128 * vb + 128)), ap("FT" + b, sl(8 * vb + 4 * h, 8 * vb + 4 * h + 4)), I)
                        for d in range(2) for h in range(2) for vb in range(2)]
             group(it)
             lin(ap(wb, sl(w, 2 * V, 2)), ap(bn), 1.0, bc(4))
@@ -377,16 +388,18 @@ def rank_program(g, core, T, topo):
             op("P", send, [ap(name, sl(0, m * G))], [], 1.0, sem="none")
             me = len(ops) - 1
             n = sum(bin(masks(T, topo, (rank - d) % NR)[d - 1]).count("1") for d in range(1, NR))
-            op("X", None, [], [ap(name, sl(m * V, m * W))], 0.0, lat=5.0, sem="arr%s%d" % (wn, kind), val=n)
+            op("X", None, [], [ap(name, sl(m * V, m * W))], 0.0, lat=WIRE, sem="arr%s%d" % (wn, kind), val=n)
             also([me])
+            if wn + str(kind) == "01":
+                for h in range(2): ops[both[("CE", 1, h)]]["deps"].append(len(ops) - 1)
 
     for b in range(NB):
         kb = bank(); r120 = (0, 120); cur[0] = b
-        group([(ap(kb, sl(60 * (2 * vb + h), 60 * (2 * vb + h + 1))), ap("INF", r120, sl(CW * h + 128 * vb, CW * h + 128 * vb + 128)),
+        group([(ap(kb, sl(60 * (2 * vb + h), 60 * (2 * vb + h + 1))), ap("INF", r120, h, sl(128 * vb, 128 * vb + 128)),
                 ap("SEL", r120, sl(4 * b, 4 * b + 4))) for vb in range(2) for h in range(2)])
         b = str(b); raw = ap("IN" + b, ALL, sl(0, 4))
         lin(ap("IN" + b), ap(kb, sl(0, 240)))
-        ts(un(b, 16, 4), raw, 0.0, A.is_lt); lin(un(b, 7, 4), raw, U); cp(si(b, 0), ap("IN" + b, ALL, sl(4, 5)))
+        ts(un(b, 16, 4), raw, 0.0, A.is_lt); lin(un(b, 7, 4), raw, U); lin(si(b, 0), ap("IN" + b, ALL, sl(4, 5)))
         tt(fs(b, 0, 3), un(b, 7, 3), un(b, 16, 3), A.max)
         tt(un(b, 11, 2), un(b, 7, 2), un(b, 9, 2), A.max); tt(un(b, 11), un(b, 11), un(b, 12), A.max); tt(fs(b, 3), un(b, 11), un(b, 16), A.max)
         lin(un(b, 21), un(b, 16), -1.0, 1.0)
@@ -396,123 +409,133 @@ def rank_program(g, core, T, topo):
     for rnd in range(RO):
         fin = rnd == RO - 1
         for bi in range(NB):
-            b = str(bi); kb = "B%d" % (6 + bi); wn = str(RO * bi + rnd); w0, wb = "W0" + wn, "WB" + wn; cur[0] = NB * rnd + bi; cur[1] = 1
-            ga, gb = ap("G0" + b, H0), ap("G0" + b, H1)
-            gat(ga, ap(w0), ap("L0" + b, sl(0, 16)), 4096.0); gat(gb, ap(w0), ap("L0" + b, sl(16, 32)), 3072.0)
+            b = str(bi); wn = str(RO * bi + rnd); w0, wb = "W0" + wn, "WB" + wn; cur[0] = NB * rnd + bi; cur[1] = 1
+            gat(ap("G0" + b, 0), ap(w0), ap("L0" + b, sl(0, 16)), 4096.0); gat(ap("G0" + b, 1), ap(w0), ap("L0" + b, sl(16, 32)), 3072.0)
             for w in range(2): gat(ap("GW" + b, sl(2 * w * CW, 2 * (w + 1) * CW)), ap(wb), ap("LW" + b, sl(32 * w, 32 * w + 32)), "any")
-            gw = lambda w, s: ap("GW" + b, sl((2 * w + s) * CW, (2 * w + s + 1) * CW))
-            hh = lambda t, n=1: ap("HH" + b, sl(t * CW, (t + n) * CW))
-            fe = lambda s, k: ap("FE" + b, sl((3 * s + k) * CW, (3 * s + k + 1) * CW))
-            for t, bias in ((0, 8), (2, 9), (4, 10), (6, 10)):
-                bn = bank(); it = []
-                for u, (k, l) in enumerate(CL[t:t + 2]): it += [(ap(bn, (H0, H1)[u]), M("A%d" % k), ga), (ap(bn, (H0, H1)[u]), M("B%d" % l), gb)]
-                group(it); act(hh(t, 2), ap(bn), F.Sigmoid, bc(bias), 256.0)
-            bn = bank(); group([(ap(bn, H0), M("A0"), ga), (ap(bn, H0), M("B0"), gb)]); act(hh(8), ap(bn, H0), F.Sigmoid, bc(7), 256.0)
-            for k in range(3):
-                bn = bank(); it = [(ap(bn, H0), M("TA%d" % k), ga), (ap(bn, H1), M("TB%d" % k), gb)]
-                for l in range(3): it += [(ap(bn, H0), I, hh(CL.index((k, l)))), (ap(bn, H1), I, hh(CL.index((l, k))))]
-                group(it)
-                for s in range(2): lin(fe(s, k), ap(bn, (H0, H1)[s]), 16.0, bc(24 + 3 * s + k))
-            prev = None
-            for q in LINES:
-                bn = bank(); it = []
-                for s, h in ((0, H0), (1, H1)):
-                    S = "AB"[s]
-                    it += [(ap(bn, h), M("D%d" % v), fe(s, k)) for k, v in enumerate(SLOPE[S][q]) if v]
-                    it += [(ap(bn, h), M("Z%s%d" % (S, q)), gw(ROWS[q][0], s))]
-                    if (S, q) in TVQ:
-                        k = TVQ.index((S, q)); it += [(ap(bn, h), ap("TV", (0, 33), sl(8 * k, 8 * k + 8)), ap("ON", (0, 33)))]
-                prev = group(it, prev); ops[prev]["deps"] += [z for z in tvf if z not in ops[prev]["deps"]]
-                if q == LINES[0]:
-                    for s, h in ((0, H0), (1, H1)): lin(ap("AC" + b, h), ap(bn, h), 1.0, bc(14 + s))
-                else: tt(ap(("EI" if q == LINES[-1] else "AC") + b), ap(bn), ap("AC" + b), A.max)
-            for e, mk in ((0, 0x5555), (1, 0xAAAA)):
-                ts(ap("ME" + b, sl(2 * e * CW, 2 * (e + 1) * CW)), ap("EI" + b), mk, A.bitwise_and)
-            for e, mk in ((0, 0x5555), (1, 0xAAAA)):
-                tt(ap("EI" + b, (H0, H1)[e]), ap("ME" + b, sl(2 * e * CW, (2 * e + 1) * CW)), ap("ME" + b, sl((2 * e + 1) * CW, (2 * e + 2) * CW)), A.add)
-                ts(ap("EI" + b, (H0, H1)[e]), ap("EI" + b, (H0, H1)[e]), 1, A.logical_shift_right, mk, A.bitwise_and)
-            nf = ap("NF" + b)
-            tt(nf, ap("EI" + b, H0), ap("EI" + b, H1), A.add)
-            ts(ap("C2" + b), nf, -0.125, A.mult, 65531.5 / 8, A.add)
-            ts(ap("T5" + b), nf, -1.0 / 32, A.mult, 65519.5 / 32, A.add)
-            bn = bank(); ts(ap(bn, H0), ap("T5" + b), 29.0, A.mult, 65535.0, A.add)
-            tt(ap("T5" + b), ap(bn, H0), nf, A.subtract); ts(ap("T5" + b), ap("T5" + b), 8191, A.bitwise_and); cp(ap("C1" + b), ap("T5" + b))
-            cur[1] = 0
-            bn = bank()
+
+            def head(cs):
+                m = cs.stop - cs.start; P0, P1, P2 = sl(0, m), sl(m, 2 * m), sl(0, 2 * m); PP = (P0, P1)
+                ga, gb = ap("G0" + b, 0, cs), ap("G0" + b, 1, cs)
+                hh = lambda t, n=1: ap("HH" + b, sl(t, t + n), cs)
+                fe = lambda s, k: ap("FE" + b, 3 * s + k, cs)
+                for t, bias in ((0, 8), (2, 9), (4, 10), (6, 10)):
+                    bn = bank(); it = []
+                    for u, (k, l) in enumerate(CL[t:t + 2]): it += [(ap(bn, PP[u]), M("A%d" % k), ga), (ap(bn, PP[u]), M("B%d" % l), gb)]
+                    group(it); act(hh(t, 2), ap(bn, P2), F.Sigmoid, bc(bias), 256.0)
+                bn = bank(); group([(ap(bn, P0), M("A0"), ga), (ap(bn, P0), M("B0"), gb)]); act(hh(8), ap(bn, P0), F.Sigmoid, bc(7), 256.0)
+                for k in range(3):
+                    bn = bank(); it = [(ap(bn, PP[s]), M("T%s%d" % ("AB"[s], k)), (ga, gb)[s]) for s in range(2) if FOLD["AB"[s]][k]]
+                    for l in range(3): it += [(ap(bn, P0), I, hh(CL.index((k, l)))), (ap(bn, P1), I, hh(CL.index((l, k))))]
+                    group(it)
+                    for s in range(2): lin(fe(s, k), ap(bn, PP[s]), 16.0, bc(24 + 3 * s + k))
+                prev = None; ac = ap("AC" + b, ALL, cs); ei = ap("EI" + b, ALL, cs)
+                for q in LINES:
+                    bn = bank(); it = []
+                    for s in range(2):
+                        S = "AB"[s]; o = ap(bn, PP[s])
+                        it += [(o, M("D%d" % v), fe(s, k)) for k, v in enumerate(SLOPE[S][q]) if v]
+                        at = (2 * ROWS[q][0] + s) * CW
+                        it += [(o, M("Z%s%d" % (S, q)), ap("GW" + b, sl(at + cs.start, at + cs.stop)))]
+                        if (S, q) in TVQ: it += [(o, tv(TVQ.index((S, q))), ap("ON", (0, 33), P0))]
+                    prev = group(it, prev); ops[prev]["deps"] += [z for z in tvf if z not in ops[prev]["deps"]]
+                    if q == LINES[0]:
+                        for s in range(2): lin(ap("AC" + b, s, cs), ap(bn, PP[s]), 1.0, bc(14 + s))
+                    else: tt(ei if q == LINES[-1] else ac, ap(bn, P2), ac, A.max)
+
+            def codes(cs):
+                m = cs.stop - cs.start; P0 = sl(0, m); ei = ap("EI" + b, ALL, cs)
+                for e, mk in ((0, 0x5555), (1, 0xAAAA)): ts(ap("ME" + b, sl(2 * e, 2 * e + 2), cs), ei, mk, A.bitwise_and)
+                for e, mk in ((0, 0x5555), (1, 0xAAAA)):
+                    o = ap("EI" + b, e, cs)
+                    tt(o, ap("ME" + b, 2 * e, cs), ap("ME" + b, 2 * e + 1, cs), A.add); ts(o, o, 1, A.logical_shift_right, mk, A.bitwise_and)
+                nf = ap("NF" + b, cs); t5 = ap("T5" + b, cs)
+                tt(nf, ap("EI" + b, 0, cs), ap("EI" + b, 1, cs), A.add)
+                lin(ap("C2" + b, cs), nf, -0.125, 65531.5 / 8); lin(t5, nf, -1.0 / 32, 65519.5 / 32)
+                bn = bank(); lin(ap(bn, P0), t5, 29.0, 65535.0)
+                tt(t5, ap(bn, P0), nf, A.subtract); ts(t5, t5, 8191, A.bitwise_and); lin(ap("C1" + b, cs), t5)
+            n = HS[NB * rnd + bi]
+            for u in range(n): head(sl(u * CW // n, (u + 1) * CW // n))
+            n = AS[NB * rnd + bi]
+            for u in range(n): codes(sl(u * CW // n, (u + 1) * CW // n))
+            cur[1] = 0; nf = ap("NF" + b)
+            bn = bank(); ga, gb = ap("G0" + b, 0), ap("G0" + b, 1); hx = (ap("HX" + b, 0), ap("HX" + b, 1))
             group([(ap(bn, H0), M("AL"), ga), (ap(bn, H0), M("BK"), gb), (ap(bn, H1), M("AK"), ga), (ap(bn, H1), M("BL"), gb)])
-            act(hh(9), ap(bn, H0), F.Sigmoid, bc(11), 256.0); act(hh(10), ap(bn, H1), F.Sigmoid, bc(8), 256.0)
+            act(hx[0], ap(bn, H0), F.Sigmoid, bc(11), 256.0); act(hx[1], ap(bn, H1), F.Sigmoid, bc(8), 256.0)
             bn = bank(); o = ap(bn, H0)
-            it = [(o, M("UA"), ga), (o, M("UB"), gb), (o, M("X9"), hh(9)), (o, M("X9"), hh(10))] + [(o, M("U%d" % abs(m)), fe(0, k)) for k, m in enumerate(UW)]
-            group(it, close=not OPEN); lin(ap("RR" + b), o, 1.0, bc(30))
-            if OPEN: mm(o, M("nI"), ap("RR" + b), False, True)
-            else: bn = bank(); o = ap(bn, H0); group([(o, l, r) for _, l, r in it] + [(o, M("nI"), ap("RR" + b))])
-            either(ap("VD" + b), o, (F.Relu, bc(34), bc(33)), (bc(31), A.is_lt, bc(32), A.mult))
-            blk = lambda name, vb, o=0, p=(0, 128): ap(name, p, sl(o + vb * 128, o + vb * 128 + 128))
-            it = [(blk(kb, vb), blk("VD" + b, vb), M("VK")) for vb in range(2)]
-            if fin: it += [(blk(kb, vb), blk("RQ" + b, vb), M("RM")) for vb in range(2)]
-            for k, t in enumerate(it): mm(t[0], t[1], t[2], k == 0, False)
+            it = [(o, M("UA"), ga), (o, M("UB"), gb), (o, M("X9"), hx[0]), (o, M("X9"), hx[1]), (o, tv(len(TVQ)), ap("ON", (0, 33)))]
+            group(it + [(o, M("U%d" % abs(m)), ap("FE" + b, k)) for k, m in enumerate(UW)])
+            lin(ap("RR" + b), o); tt(ap("VD" + b), o, ap("RR" + b), A.is_lt)
+            blk = lambda name, vb, *s: ap(name, *s, sl(vb * 128, vb * 128 + 128))
+            n = CS[NB * rnd + bi]
             for vb in range(2):
                 r = str(vb); o = 32 * 128 * vb; m = 128 // GP
                 for h in range(GP):
                     c = sl(vb * 128 + h * m, vb * 128 + (h + 1) * m); lo, hi = 32 * h * m, 32 * (h + 1) * m
-                    gat(ap("D0" + r, sl(lo + 1, hi, 2)), ap("CE" + b), ap("C2" + b, c), "any")
-                    gat(ap("D1" + b, sl(o + lo, o + hi, 2)), ap("CE" + b), ap("C1" + b, c), "any")
+                    gat(ap("D0" + r, sl(lo + 1, hi, 2)), ap("CE" + b), ap("C2" + b, c), VG[cur[0]])
+                    gat(ap("D1" + b, sl(o + lo, o + hi, 2)), ap("CE" + b), ap("C1" + b, c), VG[cur[0]])
                     scan(ap("MX" + r, sl(lo, hi)), ap("D0" + r, sl(lo, hi)), ap("D1" + b, sl(o + lo, o + hi)), A.min, A.max)
+                if n == 2 or vb == 0:
+                    kb = bank(); vs = [vb] if n == 2 else [0, 1]; gate = len(ops) - 1
+                    it = [(blk(kb, v), blk("VD" + b, v), I) for v in vs]
+                    if fin: it += [(blk(kb, v), blk("RQ" + b, v), M("RM")) for v in vs]
+                    for k, t in enumerate(it):
+                        mm(t[0], t[1], t[2], k == 0, False)
+                        if k == 0: also([gate])
                 for p in range(16):
-                    mm(ap(kb, sl(vb * 128 + p, vb * 128 + 128, 16)), ap("MX" + r, sl(2 * p + 1, 4096, 32)), ap("BO"), False, not OPEN and p == 15 and vb == 1)
-            key = ap(kb, H0); s1 = "S1" + b
-            for c in range(3):
-                scan(ap(s1), ap("RS"), key, A.add, A.min)
-                lin(ap("ZB" + b, sl(0, CW, 16), c), ap(s1, sl(15, CW, 16)), 1.0, 16 * KU)
-                if c < 2:
-                    scan(ap("KB" + b), ap("RZ"), ap("ZB" + b, ALL, c), A.mult, A.add)
-                    tt(ap("OB" + b), key, ap("KB" + b), A.is_lt)
-                    if OPEN: mm(key, I, ap("OB" + b), False, c == 1)
-                    else: tt(key, key, ap("OB" + b), A.max)
-            keys = ap("ZB" + b, sl(0, CW, 16))
-            ts(si(b, 3), keys, 1.0, A.min, 1 / KU, A.mult); ksel = len(ops) - 1
+                    mm(ap(kb, sl(vb * 128 + p, vb * 128 + 128, 16)), ap("MX" + r, sl(2 * p + 1, 4096, 32)), ap("BO"), False, p == 15 and vb == vs[-1])
+                if vb < vs[-1]: continue
+                c0, c9 = 128 * vs[0], 128 * vb + 128; cs = sl(c0, c9); rv = sl(c9 - 1, c0 - 1 if c0 else None, -1); key = ap(kb, cs)
+                for c in range(3):
+                    scan(ap("S1" + b, rv, c), ap("RZ", rv), ap(kb, rv), A.add, A.min)
+                    if c < 2:
+                        scan(ap("KB" + b, cs), ap("RS", cs), ap("S1" + b, cs, c), A.add, A.min)
+                        tt(ap("OB" + b, cs), key, ap("KB" + b, cs), A.is_le); tt(key, key, ap("OB" + b, cs), A.max)
+                    ksel = len(ops) - 1
+            keys = ap("S1" + b, sl(0, CW, 16))
+            lin(si(b, 3), keys, 1 / KU)
             ts(si(b, 4), si(b, 3), 2, A.logical_shift_right, 3, A.bitwise_and); ts(si(b, 5), si(b, 3), 3, A.bitwise_and)
             ss = lambda t: ap("SS" + b, ALL, sl(t, t + 2), sl(0, 3))
-            cp(ss(0), si(b, 4, 2)); act(ss(2), ss(0), F.Square); ts(ap("SS" + b, ALL, sl(0, 3), 3), keys, 0.5, A.is_ge)
+            lin(ss(0), si(b, 4, 2)); act(ss(2), si(b, 4, 2), F.Square); ts(ap("SS" + b, ALL, sl(0, 3), 3), keys, 0.5, A.is_ge)
             bn = bank(); prev = None
             group([(blk(bn, vb), ap("SS" + b, sl(vb * 8, vb * 8 + 8)), I) for vb in range(2)])
             lin(ap("SR" + b), ap(bn, H0))
-            xn = [("AC" + b, 0), ("AC" + b, CW), ("KB" + b, 0)]
+            xn = [("AC" + b, 0), ("AC" + b, 1), ("KB" + b,)]
             for c in range(3):
-                bn = bank(); group([(ap(bn, H0), M("PN%d" % c), ap("SR" + b))])
-                tt(ap(xn[c][0], sl(xn[c][1], xn[c][1] + CW)), ap(bn, H0), nf, A.min)
+                bn = bank(); o = ap(bn, H0)
+                if XF[cur[0]]:
+                    group([(o, ap("I32"), nf), (o, M("PN%d" % c), ap("SR" + b))]); either(ap(*xn[c]), o, (F.Relu, -65536.0, 1.0), (-65536.0, A.add, 0.0, A.max))
+                else: group([(o, M("PN%d" % c), ap("SR" + b))]); tt(ap(*xn[c]), o, nf, A.min)
             bn = bank()
-            group([(ap(bn, sl(vb * 24 + c, vb * 24 + 24, 3)), blk(xn[c][0], vb, xn[c][1]), ap("BOF")) for c in range(3) for vb in range(2)])
-            ts(si(b, 0), ap(bn, sl(0, 48)), -1.0, A.mult, 65535.0, A.add)
-            for i in range(4):
-                bn = bank(); it = []
-                for s in range(2):
-                    for vb in range(2):
-                        o = ap(bn, sl((2 * s + vb) * 96, (2 * s + vb + 1) * 96))
-                        it += [(o, blk("G0" + b, vb, s * CW), ML(i)), (o, blk("SR" + b, vb), ML(4 + 2 * i + s))]
-                prev = group(it[0::2] + it[1::2], prev, ksel); o = ap(bn, sl(0, 384))
-                if i == 0: lin(ap("LS" + b), o)
-                else: tt(ap("LS" + b), o, ap("LS" + b), A.max)
-            sa, sb = sl(0, 16), sl(16, 32)
-            tt(un(b, 0, 3), ap("LS" + b, sa, sl(0, 3)), ap("LS" + b, sb, sl(0, 3)), A.min); tt(un(b, 3, 4), ap("LS" + b, sa), ap("LS" + b, sb), A.max)
+            group([(ap(bn, sl(vb * 24 + c, vb * 24 + 24, 3)), blk(xn[c][0], vb, *xn[c][1:]), ap("BOF")) for c in range(3) for vb in range(2)])
+            lin(si(b, 0), ap(bn, sl(0, 48)), -1.0, 65535.0)
+            for c in range(3):
+                bn = bank()
+                group([(ap(bn, (H0, H1)[s]), M("IM"), ap("G0" + b, s)) for s in range(2)] +
+                      [(ap(bn, (H0, H1)[s]), M("PL%d" % (2 * c + s)), ap("SR" + b)) for s in range(2)], early=ksel)
+                either(ap("LX" + b, sl(2 * c, 2 * c + 2)), ap(bn), (F.Relu, 0.0, 1.0), (0.0, A.max))
+            bn = bank()
+            group([(ap(bn, sl(96 * (2 * s + vb) + c, 96 * (2 * s + vb + 1), 3)), blk("LX" + b, vb, 2 * c + s), ap("TM"))
+                   for c in range(3) for s in range(2) for vb in range(2)])
+            sa = sl(0, 16); lin(ap("LS" + b), ap(bn, sl(0, 192)))
+            tt(un(b, 0, 4), ap(bn, sl(192, 384)), ap("LS" + b), A.min); tt(un(b, 24, 4), ap(bn, sl(192, 384)), ap("LS" + b), A.max)
             def above(o, a, u): tt(o, a, u, A.is_le); tt(o, o, a, A.max)
-            above(un(b, 11), un(b, 3), un(b, 0)); tt(un(b, 8), un(b, 11), un(b, 1), A.min); tt(un(b, 12), un(b, 11), un(b, 1), A.max)
-            above(un(b, 13), un(b, 12), un(b, 8)); above(un(b, 14), un(b, 4), un(b, 8))
+            above(un(b, 11), un(b, 24), un(b, 0)); tt(un(b, 8), un(b, 11), un(b, 1), A.min); tt(un(b, 12), un(b, 11), un(b, 1), A.max)
+            above(un(b, 13), un(b, 12), un(b, 8)); above(un(b, 14), un(b, 25), un(b, 8))
             tt(un(b, 15), un(b, 14), un(b, 2), A.min); tt(un(b, 9), un(b, 15), un(b, 13), A.min)
             if not fin:
-                lin(fs(b, 0, 2, 3), un(b, 0, 2, 6)); ts(un(b, 21), keys, 0.5, A.is_lt)
-                ts(un(b, 17, 2), un(b, 8, 2), 0.3, A.is_ge); tt(fs(b, 1, 2), un(b, 8, 2), un(b, 17, 2), A.max); tt(un(b, 19), un(b, 6), un(b, 9), A.is_le)
+                lin(fs(b, 0, 2, 3), un(b, 0, 2, 27)); ts(un(b, 21), keys, 0.5, A.is_lt)
+                ts(un(b, 17, 2), un(b, 8, 2), 0.3, A.is_ge); tt(fs(b, 1, 2), un(b, 8, 2), un(b, 17, 2), A.max); tt(un(b, 19), un(b, 27), un(b, 9), A.is_le)
                 cur[1] = 1; prep(rnd + 1, b)
             else:
-                lin(un(b, 7), un(b, 0)); above(un(b, 10), un(b, 6), un(b, 9))
+                lin(un(b, 7), un(b, 0)); above(un(b, 10), un(b, 27), un(b, 9))
                 ts(un(b, 16, 4), un(b, 7, 4), 0.3, A.is_ge, -4.0, A.mult)
                 for c in range(3): tt(ap("FO" + b, sa, c), ap("UN" + b, ALL, sl(7, 11), c), ap("UN" + b, ALL, sl(16, 20), c), A.add)
                 ts(un(b, 21), keys, 0.5, A.is_ge, -2.0 ** 22, A.mult)
                 ts(si(b, 1), si(b, 0), 65535, A.bitwise_and); ts(si(b, 2), si(b, 3), 5, A.logical_shift_right)
                 for u in range(2): tt(ap("FP" + b, ALL, u), si(b, 1 + u), un(b, 21), A.add)
                 bn = bank(); at = lambda k: sl(CW * (k % 2) + 128 * (k // 2), CW * (k % 2) + 128 * (k // 2) + 128)
-                group([(ap(bn, (0, 96), at(k)), ap("FO" + b, sl(4 * k, 4 * k + 8)), I) for k in range(4)])
                 group([(ap(bn, (96, 120), at(k)), ap("FP" + b, k), ap("I32")) for k in range(4)])
+                group([(ap(bn, (0, 96), at(k)), ap("FO" + b, sl(4 * k, 4 * k + 8)), I) for k in range(4)])
                 r120 = (0, 120); out = T["AC" + b]; r = sl(4 * bi, 4 * bi + 4)
                 ts(ap("AC" + b, r120), ap(bn, r120), ap("BC", r120, sl(35, 36)), A.mult, ap("BC", r120, sl(36, 37)), A.max)
                 dma("oyl" + b, T.yl[r, :], out[0:48, :], [ap("AC" + b)], [], 1e5)
@@ -536,7 +559,7 @@ def rank_program(g, core, T, topo):
     def walk(pri, eng, back):
         pre, post = (succ, pred) if back else (pred, succ); eng = list(eng)
         todo = {name: len(v) for name, v in sess.items()}; at = {}; extra = []
-        banks = {"B%d" % k: [None, 0.0] for k in range(6)}
+        banks = {"B%d" % k: [None, 0.0] for k in range(8)}
         left = [len(p) for p in pre]; rdy = [lat[k] if back else 0.0 for k in range(n)]; free = dict.fromkeys("PTVASX", 0.0)
         pool = {e: [] for e in "PTVASXF"}; order = []; start = [0.0] * n; end = 0.0
         for k in range(n):
@@ -572,13 +595,15 @@ def rank_program(g, core, T, topo):
     if "plan" not in PLAN:
         pri = [0.0] * n
         for k in range(n - 1, -1, -1): pri[k] = cost(k, "A") + max([lag(k, s) + pri[s] for s in succ[k]] + [lat[k]])
-        pri = [p - BIAS * (o["ch"] % NB) + TB * o["up"] for p, o in zip(pri, ops)]
-        for k in range(PASSES):
-            w = walk(pri, kind, False)
-            if "plan" not in PLAN or w[0] < PLAN["plan"][0]: PLAN["plan"] = w
-            PLAN.setdefault("log", []).append(round(w[0], 1))
-            b = walk([t + cost(k, e) for k, (t, e) in enumerate(zip(w[2], w[3]))], w[3], True)
-            pri = [t + cost(k, e) for k, (t, e) in enumerate(zip(b[2], b[3]))]
+        path = pri
+        for lead in LEADS:
+            pri = [p - lead * (o["ch"] % NB) for p, o in zip(path, ops)]
+            for k in range(PASSES):
+                w = walk(pri, kind, False)
+                if "plan" not in PLAN or w[0] < PLAN["plan"][0]: PLAN["plan"] = w
+                PLAN.setdefault("log", []).append(round(w[0], 1))
+                b = walk([t + cost(k, e) for k, (t, e) in enumerate(zip(w[2], w[3]))], w[3], True)
+                pri = [t + cost(k, e) for k, (t, e) in enumerate(zip(b[2], b[3]))]
     end, order, start, eng, at, extra = PLAN["plan"]; place.update(at)
     for d, k in extra:
         if d not in ops[k]["deps"]: ops[k]["deps"].append(d); succ[d].append(k)

@@ -14,10 +14,11 @@ TRIV = {1: 0xAAAA, 4: 0xCCCC, 2: 0xF0F0, 5: 0xFF00}
 SLOPE = {"A": ((0, -11, 5), (-12, 0, 0), (12, -9, 4), (-30, 10, 0), (0, 0, 0), (15, -9, 5)),
          "B": ((7, 0, 0), (15, -7, 3), (-9, 4, 0), (26, -18, 9), (0, 0, 0), (-19, 9, 0))}
 FOLD = {"A": (-2, -26, -55), "B": (0, -16, -48)}
-OFF = {"A": (0, 19, 5), "B": (-54, -48, -28)}
-HEIGHT = {"A": (70, -68, -79, -127, -153, -86), "B": (12, 54, -76, 95, -119, -90)}
-OFF3 = {"A": (-2, 17, 1), "B": (-8, 41, -53)}
-HEIGHT3 = {"A": (70, -130, -1, -1024, -143, -1), "B": (-1024, 60, -1, 95, -116, -1)}
+OFF = {"A": (4, 29, -6), "B": (-52, -59, -45)}
+HEIGHT = {"A": (170, -85, -75, -170, -235, -83), "B": (0, 0, -12, 0, -117, 49)}
+OFF3 = {"A": (-2, 27, 17), "B": (-39, -28, -38)}
+HEIGHT3 = {"A": (170, 0, -1, -1020, -95, -1), "B": (-1020, 0, -1, -1020, -113, -1)}
+CONST = (170.0, 256.0)
 UW = (9, 9, -7); MUW = 5 / 64; THR = 4.125 / 16
 SIG = sorted(set(x for s in SLOPE.values() for r in s for x in r if x))
 ZEROED = ["A1", "A2", "B1", "B2", "TA0", "TA1", "TA2", "TB1", "TB2", "UA", "UB", "PN"]
@@ -33,7 +34,7 @@ def _sb(name, shape, dt, per=1):
 for _n, _s, _d in (("MT", [len(MATS) * 8, 4, 4], bf), ("MH", [len(MATH) * 8, 4, 4], f16), ("TM", [8, 4], bf), ("Z3", [8, 4, 4], bf),
                    ("Z2", [160], bf), ("ZF", [128], f32), ("SEL", [8, 5, 3], f32), ("I0", [136], bf), ("I32", [128], f32),
                    ("CK", [8, 4, 4], bf), ("QI", [3, 128], bf), ("J0", [160], bf), ("JW", [4, 160], bf),
-                   ("TV", [24, 4, 4], bf), ("ON", [CW], bf), ("BO", [8], bf), ("BOF", [8], f32), ("BC", [48], f32), ("PC", [4], i32),
+                   ("TV", [8, 4, 4], bf), ("ON", [CW], bf), ("BO", [8], bf), ("BOF", [8], f32), ("BC", [48], f32), ("PC", [4], i32),
                    ("OWN", [32], f32), ("PL", [64], i32), ("PF", [64], f32), ("WL", [4, 8, 16], bf), ("TI", [256], i32), ("TJ", [256], i32), ("BT", [256], bf), ("LUT", [1024], bf),
                    ("RS", [CW], f32), ("RZ", [CW], f32), ("INI", [V], i32), ("INF", [V], f32)):
     _sb(_n, _s, _d)
@@ -43,8 +44,8 @@ for _n, _s, _d in (("CE", [8192], bf), ("RQ", [CW], bf), ("FN", [4, 16], i32), (
                    ("G0", [2, CW], f16), ("GW", [4 * CW], bf), ("HH", [9, CW], bf), ("HX", [2, CW], bf), ("FE", [6, CW], bf), ("RR", [CW], bf),
                    ("VD", [CW], bf), ("AC", [2, CW], f32), ("EI", [2, CW], i32), ("ME", [4, CW], i32), ("NF", [CW], f32), ("T5", [CW], i32),
                    ("C1", [CW], u16), ("C2", [CW], u16), ("D0", [4096], bf), ("MX", [4096], bf), ("S1", [CW, 3], f32), ("KB", [CW], f32),
-                   ("OB", [CW], bf), ("UN", [16, 28, 3], f32), ("IN", [16, 5, 3], f32), ("SI", [16, 6, 3], i32),
-                   ("SS", [16, 4, 4], bf), ("SR", [CW], bf), ("LS", [16, 4, 3], f32), ("LX", [6, CW], f16), ("FS", [16, 4, 4], f16), ("FT", [16, 16], bf),
+                   ("OB", [2, CW], bf), ("UN", [16, 28, 3], f32), ("IN", [16, 5, 3], f32), ("SI", [16, 6, 3], i32),
+                   ("SS", [16, 4, 4], bf), ("SR", [2, CW], bf), ("LS", [16, 4, 3], f32), ("LX", [6, CW], f16), ("FS", [16, 4, 4], f16), ("FT", [4, 8, 16], bf),
                    ("FL", [68, 4], f16), ("LL", [64], u16), ("GL", [1024], bf), ("FO", [20, 3, 4], f16), ("FP", [4, 2, 12], f32)):
     _sb(_n, _s, _d, NB)
 for _k in range(8):
@@ -52,11 +53,13 @@ for _k in range(8):
 DMAS = ["leaf", "tab"] + [x + str(b) + str(h) for x in ("fan", "req", "cel") for b in range(NB) for h in range(2)] + \
     [x + str(b) for x in ("oyl", "oyt", "oyc") for b in range(NB)]
 SEMAPHORES = ["sP", "sT", "sV", "sA", "sent"] + ["d" + x for x in DMAS] + ["arr%d%d" % (r, k) for r in range(NB * RO) for k in range(2)]
-CYC = 0.00083; PEC = 0.00042; LAG = 0.08; FIX = 0.045; AFIX = 0.02; GC = 1.56; WIRE = 6.0
-VG = ("A", "A", "A", "any")
-SLACK = 0.6; GAIN = 0.1; LEADS = (3, 5, 6, 7, 9); D1P = (0, 1); LOOK = 0.03; PASSES = 6
-XF = (0, 0, 1, 1)
-HS = (1, 1, 1, 1); AS = (2, 1, 1, 2); CS = (1, 1, 1, 2)
+CYC = 0.00083; PEC = 0.00042; LAG = 0.08; FIX = 0.045; AFIX = 0.02; GC = 1.6; WIRE = 6.0
+VG = ((7,), None, (7,), None)
+SLACK = 0.6; GAIN = 0.1; LEADS = (2, 3, 4, 5, 6, 7, 8); D1P = (0, 1); LOOK = 0.03; PASSES = 6; SHAKES = 40
+XF = (0, 0, 0, 1)
+PX = (0, 0, 0, 0); TE = 0; KP = (2, 0, 0, 0); CG = (0, 1); MA = 1; GWN = 2; GPS = (2, 4, 2, 2); PC = (1, 1, 0, 1); CP = (0, 1, 1, 0)
+OTHER = ((1.1, 1.0, 4.0), (2.0, 1.4, 9.0), (1.2, 1.3, 8.0), (1.9, 1.1, 5.0))
+HS = (1, 1, 1, 1); LS = (1, 1, 1, 1); AS = (2, 1, 1, 2); CS = (1, 1, 1, 2)
 PLAN = {}
 SAME = {"INI": "EI1", "INF": "AC1", "TI": "T50", "TJ": "T51", "ME1": "ME0", "GL1": "GL0", "HH1": "HH0", "HX1": "HX0", "IN1": "IN0", "LX1": "LX0", "LS1": "LS0",
         "RR1": "RR0", "OB1": "OB0", "SR1": "SR0", "FO1": "FO0", "FP1": "FP0"}
@@ -154,7 +157,7 @@ def rank_program(g, core, T, topo):
     def cp(o, a): op("V", lambda q: q.tensor_copy(x(o), x(a)), [a], [o], c1(o, a))
     def ms(o, c): op("V", lambda q: q.memset(x(o), c), [], [o], c1(o, o))
     def mf(o, c):
-        z = ap("CE0", sl(0, len(o[2])))
+        z = ap("RQ0", sl(0, len(o[2])))
         op("F", {"A": actf(o, z, F.Identity, c, 0.0), "V": lambda q: q.memset(x(o), c)}, [z], [o], {"A": vc(len(o[2])) + AFIX, "V": c1(o, o)})
     def red(o, a): op("V", lambda q: q.tensor_reduce(x(o), x(a), AxisListType.X, A.add), [a], [o], vc(len(a[2])))
     def scan(o, a, b, f0, f1):
@@ -164,6 +167,7 @@ def rank_program(g, core, T, topo):
     def either(o, a, fa, fv):
         op("F", {"A": actf(o, a, *fa), "V": tsf(o, a, *fv)}, [a] + cols(*fa, *fv), [o], {"A": vc(len(a[2])) + AFIX, "V": c1(o, a)})
     def lin(o, a, scale=1.0, bias=0.0): either(o, a, (F.Identity, bias, scale), (scale, A.mult, bias, A.add))
+    def step(o, a, at, steep): either(o, a, (F.Sigmoid, -at * steep, steep), (at, A.is_ge if steep > 0 else A.is_lt))
     def mm(o, l, r, start=False, stop=False):
         n = max(min(64, len(l[2])), len(r[2])) * (4 if dty(l) == f32 else 1)
         op("T", lambda q: q.matmul(x(o), x(l), x(r), start, stop), [l, r], [o], 0.02 + n * PEC)
@@ -183,10 +187,13 @@ def rank_program(g, core, T, topo):
     def gat(o, win, off, kind):
         w = lambda: x(win).indirect(x(off)); c = 0.07 + GC * len(o[2]) * CYC
         if kind == "any": op("F", {"V": lambda q: q.tensor_copy(x(o), w()), "A": lambda q: q.activation(x(o), w(), F.Copy)}, [win, off], [o], {"A": c, "V": c})
+        elif kind == "V": op("V", lambda q: q.tensor_copy(x(o), w()), [win, off], [o], c)
         elif kind == "A": op("A", lambda q: q.activation(x(o), w(), F.Copy), [win, off], [o], c)
         else: op("V", lambda q: q.tensor_scalar(x(o), w(), kind, None, A.min), [win, off], [o], c)
+        ops[-1]["gat"] = len(o[2])
     def dma(name, o, a, rd, wr, nbytes):
         op("S", lambda q: q.dma_start(o, a), rd, wr, 0.08, lat=2.0 + nbytes / 150e3, sem="d" + name, val=16)
+    def who(k): return "any" if VG[cur[0]] is None else "V" if k in VG[cur[0]] else "A"
     def also(k): ops[-1]["deps"] += [z for z in k if z not in ops[-1]["deps"]]
     def M(name, *idx):
         t, names = ("MH", MATH) if name in MATH else ("MT", MATS); k = names.index(name) * 8
@@ -206,7 +213,7 @@ def rank_program(g, core, T, topo):
             for h in range(2):
                 r = sl(64 * b, 64 * b + 64)
                 src = {"fan": T.fan[r, :], "req": T.req[r, CW * h:CW * (h + 1)], "cel": T.cells[r, :]}[name]
-                dma("%s%d%d" % (name, b, h), T[buf + str(b)][64 * h:64 * h + 64], src, [], [ap(buf + str(b))] if h else [], size * (b + 1))
+                dma("%s%d%d" % (name, b, h), T[buf + str(b)][64 * h:64 * h + 64], src, [], [ap(buf + str(b))] if h else [], size)
                 both[(buf, b, h)] = len(ops) - 1
             ops[-1]["deps"].append(both[(buf, b, 0)]); ops[-1]["pair"] = both[(buf, b, 0)]
 
@@ -240,14 +247,14 @@ def rank_program(g, core, T, topo):
     for q0, q1 in ((4, 0), (3, 5), (1, 2)):
         for s in "AB":
             z = "Z%s%d" % (s, q0); hi, lo = ROWS[q0][1:]
-            sel(M(z), Z3, G16, -15, 256.0 * HEIGHT[s][q0])
+            sel(M(z), Z3, G16, -15, 65536 * HEIGHT[s][q0] / CONST[ROWS[q0][0]])
             if hi == lo: part(z, s, 5, lo, 257.0)
             else: part(z, s, 5, hi, 256.0); part(z, s, 5, lo, 1.0)
-            sel(M("Z%s%d" % (s, q1)), M(z), G16, -15, 256.0 * HEIGHT[s][q1])
+            sel(M("Z%s%d" % (s, q1)), M(z), G16, -15, 65536 * HEIGHT[s][q1] / CONST[ROWS[q1][0]])
     for s in "AB":
         for q in (0, 3, 1, 5, 2):
             z = M("Z%s%d" % (s, q), *last(s))
-            if HEIGHT3[s][q] != HEIGHT[s][q]: sel(z, z, G4, -15, 256.0 * HEIGHT3[s][q] + (TRIV[q] / 256 if q in (2, 5) else 0.0))
+            if q in TRIV or HEIGHT3[s][q] != HEIGHT[s][q]: sel(z, z, G4, -15, (65536 * HEIGHT3[s][q] + TRIV.get(q, 0)) / CONST[ROWS[q][0]])
     ms(ap("CK"), -32.0 * KU)
     sel(M("RM"), ap("CK"), G16, 0, 0.0, A.is_ge); sel(M("RM"), M("RM"), [[16, 8], [0, 16]], 15, 0.0, A.is_ge, -1)
     lin(ap("BO"), M("RM", 0, 0), -1.0); lin(ap("BOF"), M("RM", 0, 0), -1.0 / (32 * KU))
@@ -327,24 +334,18 @@ def rank_program(g, core, T, topo):
     ts(bc(35), pp, 96.0, A.is_lt, 8191.0, A.mult); lin(bc(35), bc(35), 1.0, 1.0)
     ts(bc(16), pp, 96.0, A.is_ge); ts(bc(36), pp, 108.0, A.is_lt, bc(16), A.mult); lin(bc(36), bc(36), 1.0, -1.0)
     for name, w in [("U9", 9 / 16), ("U7", -7 / 16), ("X9", 9.0)] + [("D%d" % v, 65536.0 * v) for v in SIG]: lin(M(name), I, w)
-    ms(ap("TV", (0, 64)), 0.0); ms(ap("ON", (0, 64)), 1.0); del fills[:]
-    TVQ = [(s, 1) for s in "AB"]
-    for k, (s, q) in enumerate(TVQ):
-        for p, v in ((0, TRIV[q] & 0xFF00), (32, TRIV[q] & 0xFF)):
-            if v: fill(ap("TV", (p, p + 1), sl(8 * k, 8 * k + 8), *last(s)), float(v))
-    tvf = list(fills)
-    def tv(k, *idx): return ap("TV", (0, 33), sl(8 * k, 8 * k + 8), *idx)
+    ms(ap("TV", (0, 64)), 0.0); ms(ap("ON", (0, 64)), 1.0)
     base, base3 = [157.0 - THR - sum(m * o for m, o in zip(UW, off["A"])) / 16 for off in (OFF, OFF3)]
     base3 += 3 * muA
     for view, v in (((), base), (last("A"), base3), (last("B"), base + 3 * MUW), ((3, sl(3, 4)), base3 + 3 * MUW)):
-        for p, y in ((0, float(math.floor(v))), (32, v - math.floor(v))): ms(ap("TV", (p, p + 1), sl(16, 24), *view), y)
+        for p, y in ((0, float(math.floor(v))), (32, v - math.floor(v))): ms(ap("TV", (p, p + 1), ALL, *view), y)
     mf(ap("RS"), 0.0); mf(ap("RS", sl(0, CW, 16)), 2.0 ** 34); mf(ap("RZ"), KU); mf(ap("RZ", sl(15, CW, 16)), 2.0 ** 34)
     for b in range(NB):
         b = str(b)
         for h in range(2): lin(ap("L0" + b, half(h)), ap("FN" + b, half(h), sl(h, 4, 2)))
         for w in range(2): lin(ap("LW" + b, sl(32 * w, 32 * w + 32)), ap("L0" + b), 2.0, float(w))
-        mf(ap("SS" + b, ALL, 3, 3), 1.0); ms(ap("FT" + b), 0.0); ms(ap("FL" + b), 0.0)
-        mf(ap("D0" + b, sl(0, 4096, 2)), -1.0)
+        mf(ap("SS" + b), 1.0); ms(ap("FT" + b), 0.0); ms(ap("FT" + b, ALL, ALL, 15), CONST[0] - CONST[1]); ms(ap("FL" + b), 0.0)
+        ms(ap("D0" + b, sl(0, 4096, 2)), -1.0)
         lin(ap("FS" + b, ALL, 0, 3), ap("OWN", sl(16 * int(b), 16 * int(b) + 16)), U)
     mf(ap("FO0", sl(16, 20)), 0.0)
     for h in range(2): lin(ap("INF", (0, 120), h), ap("INI", (0, 120), h)); also([tabop])
@@ -356,27 +357,25 @@ def rank_program(g, core, T, topo):
         wn = str(RO * int(b) + rnd); w0, wb = "W0" + wn, "WB" + wn
         mu = ap("FS" + b, ALL, sl(1, 4), 3)
         tt(un(b, 20), un(b, 17), un(b, 18), A.add); tt(un(b, 20), un(b, 20), un(b, 19), A.add); tt(mu, un(b, 20), un(b, 21), A.mult)
-        bn = bank()
-        for d in range(2):
-            group([(ap(bn, half(d), sl(CW * h + 128 * vb, CW * h + 128 * vb + 128)), ap("FS" + b, sl(8 * vb + 4 * h, 8 * vb + 4 * h + 4)), I)
-                   for h in range(2) for vb in range(2)])
-        lin(ap(w0, sl(0, V)), ap(bn), bc(3))
+        for h in range(2):
+            bn = bank()
+            for d in range(2):
+                group([(ap(bn, half(d), sl(128 * vb, 128 * vb + 128)), ap("FS" + b, sl(8 * vb + 4 * h, 8 * vb + 4 * h + 4)), I) for vb in range(2)])
+            ts(ap(w0, sl(CW * h, CW * h + CW)), ap(bn, H0), bc(3), A.mult, 4096.0, A.min)
         ts(si(b, 1), si(b, 0), 255, A.bitwise_and); ts(si(b, 2), si(b, 0), 8, A.logical_shift_right, 255, A.bitwise_and)
         lin(un(b, 23), mu, 256.0); tt(ap("FL" + b, sl(3, 64, 4), sl(0, 3)), un(b, 23), si(b, 1), A.add)
-        ts(un(b, 22), mu, 0.0, A.is_equal); tt(ap("FT" + b, ALL, sl(ROWS[3][1], 15, 5)), si(b, 2), un(b, 22), A.mult)
+        either(un(b, 22), mu, (F.Relu, 1.0, -1.0), (0.0, A.is_equal))
+        for d in range(2): tt(ap("FT" + b, ALL, sl(4 * d, 4 * d + 4), sl(ROWS[3][1], 15, 5)), si(b, 2), un(b, 22), A.mult)
         bn = bank(); blocks = [(vb, hh) for vb in range(2) for hh in range(2)]
         group([(ap(bn, sl(0, 64)), ap("FL" + b, sl(31 * vb + 3 - 2 * hh, 31 * vb + 35 - 2 * hh)), ap("I0", sl(8 + hh, 136, 2))) for vb, hh in blocks])
         lin(ap("LL" + b), ap(bn, sl(0, 64)))
         gat(ap("GL" + b), ap("LUT"), ap("LL" + b), "any")
-        for w in range(2):
-            bn = bank()
-            it = [(ap(bn, sl(CW * h + 128 * vb, CW * h + 128 * vb + 128)), ap("JW", 2 * w + h, sl(16 + 5 * w - 5 * c, 144 + 5 * w - 5 * c)),
-                   ap("GL" + b, sl(4 * vb + c, 1024, 8))) for c in range(3) for h in range(2) for vb in range(2)]
-            if w == ROWS[3][0]:
-                it[4:4] = [(ap(bn, half(d), sl(CW * h + 128 * vb, CW * h + 128 * vb + 128)), ap("FT" + b, sl(8 * vb + 4 * h, 8 * vb + 4 * h + 4)), I)
-                       for d in range(2) for h in range(2) for vb in range(2)]
-            group(it)
-            lin(ap(wb, sl(w, 2 * V, 2)), ap(bn), 1.0, bc(4))
+        for h in range(2):
+            bn = bank(); at = lambda w, vb: ap(bn, sl(CW * vb + w, CW * vb + CW, 2))
+            it = [(at(w, vb), ap("JW", 2 * w + h, sl(16 + 5 * w - 5 * c, 144 + 5 * w - 5 * c)), ap("GL" + b, sl(4 * vb + c, 1024, 8)))
+                  for c in range(3) for w in range(2) for vb in range(2)]
+            group(it + [(at(ROWS[3][0], vb), ap("FT" + b, 2 * vb + h), I) for vb in range(2)])
+            lin(ap(wb, sl(V * h, V * h + V)), ap(bn), 1.0, bc(4))
         for kind, name, m in ((0, w0, 1), (1, wb, 2)):
             def send(q, kind=kind, name=name, m=m):
                 tr = []
@@ -390,8 +389,8 @@ def rank_program(g, core, T, topo):
             n = sum(bin(masks(T, topo, (rank - d) % NR)[d - 1]).count("1") for d in range(1, NR))
             op("X", None, [], [ap(name, sl(m * V, m * W))], 0.0, lat=WIRE, sem="arr%s%d" % (wn, kind), val=n)
             also([me])
-            if wn + str(kind) == "01":
-                for h in range(2): ops[both[("CE", 1, h)]]["deps"].append(len(ops) - 1)
+            if rnd == 0 and kind == CG[int(b)]:
+                for h in range(2): ops[both[("CE", int(b), h)]]["deps"].append(len(ops) - 1)
 
     for b in range(NB):
         kb = bank(); r120 = (0, 120); cur[0] = b
@@ -399,7 +398,7 @@ def rank_program(g, core, T, topo):
                 ap("SEL", r120, sl(4 * b, 4 * b + 4))) for vb in range(2) for h in range(2)])
         b = str(b); raw = ap("IN" + b, ALL, sl(0, 4))
         lin(ap("IN" + b), ap(kb, sl(0, 240)))
-        ts(un(b, 16, 4), raw, 0.0, A.is_lt); lin(un(b, 7, 4), raw, U); lin(si(b, 0), ap("IN" + b, ALL, sl(4, 5)))
+        either(un(b, 16, 4), raw, (F.Relu, 0.0, -1.0), (0.0, A.is_lt)); lin(un(b, 7, 4), raw, U); lin(si(b, 0), ap("IN" + b, ALL, sl(4, 5)))
         tt(fs(b, 0, 3), un(b, 7, 3), un(b, 16, 3), A.max)
         tt(un(b, 11, 2), un(b, 7, 2), un(b, 9, 2), A.max); tt(un(b, 11), un(b, 11), un(b, 12), A.max); tt(fs(b, 3), un(b, 11), un(b, 16), A.max)
         lin(un(b, 21), un(b, 16), -1.0, 1.0)
@@ -410,8 +409,8 @@ def rank_program(g, core, T, topo):
         fin = rnd == RO - 1
         for bi in range(NB):
             b = str(bi); wn = str(RO * bi + rnd); w0, wb = "W0" + wn, "WB" + wn; cur[0] = NB * rnd + bi; cur[1] = 1
-            gat(ap("G0" + b, 0), ap(w0), ap("L0" + b, sl(0, 16)), 4096.0); gat(ap("G0" + b, 1), ap(w0), ap("L0" + b, sl(16, 32)), 3072.0)
-            for w in range(2): gat(ap("GW" + b, sl(2 * w * CW, 2 * (w + 1) * CW)), ap(wb), ap("LW" + b, sl(32 * w, 32 * w + 32)), "any")
+            gat(ap("G0" + b, 0), ap(w0), ap("L0" + b, sl(0, 16)), "any"); gat(ap("G0" + b, 1), ap(w0), ap("L0" + b, sl(16, 32)), 3072.0)
+            for w in range(GWN): gat(ap("GW" + b, sl(4 * w * CW // GWN, 4 * (w + 1) * CW // GWN)), ap(wb), ap("LW" + b, sl(64 * w // GWN, 64 * (w + 1) // GWN)), "any")
 
             def head(cs):
                 m = cs.stop - cs.start; P0, P1, P2 = sl(0, m), sl(m, 2 * m), sl(0, 2 * m); PP = (P0, P1)
@@ -421,13 +420,17 @@ def rank_program(g, core, T, topo):
                 for t, bias in ((0, 8), (2, 9), (4, 10), (6, 10)):
                     bn = bank(); it = []
                     for u, (k, l) in enumerate(CL[t:t + 2]): it += [(ap(bn, PP[u]), M("A%d" % k), ga), (ap(bn, PP[u]), M("B%d" % l), gb)]
-                    group(it); act(hh(t, 2), ap(bn, P2), F.Sigmoid, bc(bias), 256.0)
+                    got = group(it); act(hh(t, 2), ap(bn, P2), F.Sigmoid, bc(bias), 256.0)
                 bn = bank(); group([(ap(bn, P0), M("A0"), ga), (ap(bn, P0), M("B0"), gb)]); act(hh(8), ap(bn, P0), F.Sigmoid, bc(7), 256.0)
                 for k in range(3):
                     bn = bank(); it = [(ap(bn, PP[s]), M("T%s%d" % ("AB"[s], k)), (ga, gb)[s]) for s in range(2) if FOLD["AB"[s]][k]]
                     for l in range(3): it += [(ap(bn, P0), I, hh(CL.index((k, l)))), (ap(bn, P1), I, hh(CL.index((l, k))))]
-                    group(it)
+                    group(it, early=got if TE else None)
                     for s in range(2): lin(fe(s, k), ap(bn, PP[s]), 16.0, bc(24 + 3 * s + k))
+
+            def lines(cs):
+                m = cs.stop - cs.start; P0, P1, P2 = sl(0, m), sl(m, 2 * m), sl(0, 2 * m); PP = (P0, P1)
+                fe = lambda s, k: ap("FE" + b, 3 * s + k, cs)
                 prev = None; ac = ap("AC" + b, ALL, cs); ei = ap("EI" + b, ALL, cs)
                 for q in LINES:
                     bn = bank(); it = []
@@ -436,103 +439,121 @@ def rank_program(g, core, T, topo):
                         it += [(o, M("D%d" % v), fe(s, k)) for k, v in enumerate(SLOPE[S][q]) if v]
                         at = (2 * ROWS[q][0] + s) * CW
                         it += [(o, M("Z%s%d" % (S, q)), ap("GW" + b, sl(at + cs.start, at + cs.stop)))]
-                        if (S, q) in TVQ: it += [(o, tv(TVQ.index((S, q))), ap("ON", (0, 33), P0))]
-                    prev = group(it, prev); ops[prev]["deps"] += [z for z in tvf if z not in ops[prev]["deps"]]
+                    prev = group(it, prev)
                     if q == LINES[0]:
                         for s in range(2): lin(ap("AC" + b, s, cs), ap(bn, PP[s]), 1.0, bc(14 + s))
                     else: tt(ei if q == LINES[-1] else ac, ap(bn, P2), ac, A.max)
 
             def codes(cs):
                 m = cs.stop - cs.start; P0 = sl(0, m); ei = ap("EI" + b, ALL, cs)
-                for e, mk in ((0, 0x5555), (1, 0xAAAA)): ts(ap("ME" + b, sl(2 * e, 2 * e + 2), cs), ei, mk, A.bitwise_and)
+                for e, mk in ((0, 0x5555), (1, 0xAAAA)): ts(ap("ME" + b, sl(e, e + 3, 2), cs), ei, mk, A.bitwise_and)
+                def near(a):
+                    if not PX[cur[0]]: return a
+                    o = ap(bank(), P0); act(o, a, F.Identity)
+                    return o
+                if m == CW: tt(ei, ap("ME" + b, sl(0, 2)), ap("ME" + b, sl(2, 4)), A.add)
                 for e, mk in ((0, 0x5555), (1, 0xAAAA)):
                     o = ap("EI" + b, e, cs)
-                    tt(o, ap("ME" + b, 2 * e, cs), ap("ME" + b, 2 * e + 1, cs), A.add); ts(o, o, 1, A.logical_shift_right, mk, A.bitwise_and)
+                    if m < CW: tt(o, near(ap("ME" + b, e, cs)), ap("ME" + b, 2 + e, cs), A.add)
+                    ts(o, o, 1, A.logical_shift_right, mk, A.bitwise_and)
                 nf = ap("NF" + b, cs); t5 = ap("T5" + b, cs)
-                tt(nf, ap("EI" + b, 0, cs), ap("EI" + b, 1, cs), A.add)
+                tt(nf, near(ap("EI" + b, 0, cs)), ap("EI" + b, 1, cs), A.add)
                 lin(ap("C2" + b, cs), nf, -0.125, 65531.5 / 8); lin(t5, nf, -1.0 / 32, 65519.5 / 32)
                 bn = bank(); lin(ap(bn, P0), t5, 29.0, 65535.0)
-                tt(t5, ap(bn, P0), nf, A.subtract); ts(t5, t5, 8191, A.bitwise_and); lin(ap("C1" + b, cs), t5)
-            n = HS[NB * rnd + bi]
-            for u in range(n): head(sl(u * CW // n, (u + 1) * CW // n))
-            n = AS[NB * rnd + bi]
-            for u in range(n): codes(sl(u * CW // n, (u + 1) * CW // n))
+                tt(t5, ap(bn, P0), nf, A.subtract); ts(t5, t5, 8191, A.bitwise_and)
+                if CP[cur[0]]: sel(ap("C1" + b, cs), t5, [[0, m]], 1, 0.0, A.is_ge, 0)
+                else: lin(ap("C1" + b, cs), t5)
+            for stage, pieces in ((head, HS), (lines, LS), (codes, AS)):
+                n = pieces[cur[0]]
+                for u in range(n): stage(sl(u * CW // n, (u + 1) * CW // n))
             cur[1] = 0; nf = ap("NF" + b)
             bn = bank(); ga, gb = ap("G0" + b, 0), ap("G0" + b, 1); hx = (ap("HX" + b, 0), ap("HX" + b, 1))
             group([(ap(bn, H0), M("AL"), ga), (ap(bn, H0), M("BK"), gb), (ap(bn, H1), M("AK"), ga), (ap(bn, H1), M("BL"), gb)])
             act(hx[0], ap(bn, H0), F.Sigmoid, bc(11), 256.0); act(hx[1], ap(bn, H1), F.Sigmoid, bc(8), 256.0)
             bn = bank(); o = ap(bn, H0)
-            it = [(o, M("UA"), ga), (o, M("UB"), gb), (o, M("X9"), hx[0]), (o, M("X9"), hx[1]), (o, tv(len(TVQ)), ap("ON", (0, 33)))]
+            it = [(o, M("UA"), ga), (o, M("UB"), gb), (o, M("X9"), hx[0]), (o, M("X9"), hx[1]), (o, ap("TV", (0, 33)), ap("ON", (0, 33)))]
             group(it + [(o, M("U%d" % abs(m)), ap("FE" + b, k)) for k, m in enumerate(UW)])
             lin(ap("RR" + b), o); tt(ap("VD" + b), o, ap("RR" + b), A.is_lt)
             blk = lambda name, vb, *s: ap(name, *s, sl(vb * 128, vb * 128 + 128))
             n = CS[NB * rnd + bi]
             for vb in range(2):
-                r = str(vb); o = 32 * 128 * vb; m = 128 // GP
+                r = str(vb); o = 32 * 128 * vb; GP = GPS[cur[0]]; m = 128 // GP
                 for h in range(GP):
                     c = sl(vb * 128 + h * m, vb * 128 + (h + 1) * m); lo, hi = 32 * h * m, 32 * (h + 1) * m
-                    gat(ap("D0" + r, sl(lo + 1, hi, 2)), ap("CE" + b), ap("C2" + b, c), VG[cur[0]])
-                    gat(ap("D1" + b, sl(o + lo, o + hi, 2)), ap("CE" + b), ap("C1" + b, c), VG[cur[0]])
+                    gat(ap("D0" + r, sl(lo + 1, hi, 2)), ap("CE" + b), ap("C2" + b, c), who(2 * (vb * GP + h)))
+                    gat(ap("D1" + b, sl(o + lo, o + hi, 2)), ap("CE" + b), ap("C1" + b, c), who(2 * (vb * GP + h) + 1))
                     scan(ap("MX" + r, sl(lo, hi)), ap("D0" + r, sl(lo, hi)), ap("D1" + b, sl(o + lo, o + hi)), A.min, A.max)
                 if n == 2 or vb == 0:
-                    kb = bank(); vs = [vb] if n == 2 else [0, 1]; gate = len(ops) - 1
-                    it = [(blk(kb, v), blk("VD" + b, v), I) for v in vs]
-                    if fin: it += [(blk(kb, v), blk("RQ" + b, v), M("RM")) for v in vs]
-                    for k, t in enumerate(it):
-                        mm(t[0], t[1], t[2], k == 0, False)
-                        if k == 0: also([gate])
-                for p in range(16):
-                    mm(ap(kb, sl(vb * 128 + p, vb * 128 + 128, 16)), ap("MX" + r, sl(2 * p + 1, 4096, 32)), ap("BO"), False, p == 15 and vb == vs[-1])
+                    kbs = [bank() for _ in range(1 + KP[cur[0]])]; vs = [vb] if n == 2 else [0, 1]; gate = len(ops) - 1
+                    for kb in kbs:
+                        it = [(blk(kb, v), blk("VD" + b, v), I) for v in vs]
+                        if fin: it += [(blk(kb, v), blk("RQ" + b, v), M("RM")) for v in vs]
+                        for k, t in enumerate(it):
+                            mm(t[0], t[1], t[2], k == 0, False)
+                            if k == 0: also([gate])
+                for kb in kbs:
+                    for p in range(16):
+                        mm(ap(kb, sl(vb * 128 + p, vb * 128 + 128, 16)), ap("MX" + r, sl(2 * p + 1, 4096, 32)), ap("BO"), False,
+                           p == 15 and vb == vs[-1] and kb == kbs[0])
                 if vb < vs[-1]: continue
-                c0, c9 = 128 * vs[0], 128 * vb + 128; cs = sl(c0, c9); rv = sl(c9 - 1, c0 - 1 if c0 else None, -1); key = ap(kb, cs)
+                c0, c9 = 128 * vs[0], 128 * vb + 128; cs = sl(c0, c9); rv = sl(c9 - 1, c0 - 1 if c0 else None, -1); kb = kbs[0]
                 for c in range(3):
                     scan(ap("S1" + b, rv, c), ap("RZ", rv), ap(kb, rv), A.add, A.min)
                     if c < 2:
-                        scan(ap("KB" + b, cs), ap("RS", cs), ap("S1" + b, cs, c), A.add, A.min)
-                        tt(ap("OB" + b, cs), key, ap("KB" + b, cs), A.is_le); tt(key, key, ap("OB" + b, cs), A.max)
+                        key = ap(kb, cs); ob = ap("OB" + b, c, cs)
+                        scan(ap("KB" + b, cs), ap("RS", cs), ap("S1" + b, cs, c), A.add, A.min); tt(ob, key, ap("KB" + b, cs), A.is_le)
+                        if c < KP[cur[0]]:
+                            kb = kbs[c + 1]
+                            for k in kbs[c + 1:]: mm(ap(k, cs), I, ob, False, k == kb)
+                        else: tt(key, key, ob, A.max)
                     ksel = len(ops) - 1
             keys = ap("S1" + b, sl(0, CW, 16))
-            lin(si(b, 3), keys, 1 / KU)
-            ts(si(b, 4), si(b, 3), 2, A.logical_shift_right, 3, A.bitwise_and); ts(si(b, 5), si(b, 3), 3, A.bitwise_and)
-            ss = lambda t: ap("SS" + b, ALL, sl(t, t + 2), sl(0, 3))
-            lin(ss(0), si(b, 4, 2)); act(ss(2), si(b, 4, 2), F.Square); ts(ap("SS" + b, ALL, sl(0, 3), 3), keys, 0.5, A.is_ge)
-            bn = bank(); prev = None
-            group([(blk(bn, vb), ap("SS" + b, sl(vb * 8, vb * 8 + 8)), I) for vb in range(2)])
-            lin(ap("SR" + b), ap(bn, H0))
-            xn = [("AC" + b, 0), ("AC" + b, 1), ("KB" + b,)]
-            for c in range(3):
-                bn = bank(); o = ap(bn, H0)
-                if XF[cur[0]]:
-                    group([(o, ap("I32"), nf), (o, M("PN%d" % c), ap("SR" + b))]); either(ap(*xn[c]), o, (F.Relu, -65536.0, 1.0), (-65536.0, A.add, 0.0, A.max))
-                else: group([(o, M("PN%d" % c), ap("SR" + b))]); tt(ap(*xn[c]), o, nf, A.min)
+            xn = [("AC" + b, 0), ("AC" + b, 1), ("KB" + b,)]; lx = []
+            for u, cc in enumerate((sl(0, 2), sl(2, 3)) if PC[cur[0]] else (sl(0, 3),)):
+                sc = lambda k, n=1: ap("SI" + b, ALL, sl(k, k + n), cc); ss = lambda t: ap("SS" + b, ALL, sl(t, t + 2), cc)
+                kc = ap("S1" + b, sl(0, CW, 16), cc); sr = ap("SR" + b, u)
+                lin(sc(3), kc, 1 / KU); soon = len(ops) - 1 if PC[cur[0]] else ksel
+                ts(sc(4), sc(3), 2, A.logical_shift_right, 3, A.bitwise_and); ts(sc(5), sc(3), 3, A.bitwise_and)
+                lin(ss(0), sc(4, 2)); act(ss(2), sc(4, 2), F.Square); step(ap("SS" + b, ALL, cc, 3), kc, 0.75, 256.0)
+                bn = bank()
+                group([(blk(bn, vb), ap("SS" + b, sl(vb * 8, vb * 8 + 8)), I) for vb in range(2)])
+                lin(sr, ap(bn, H0))
+                for c in range(cc.start, cc.stop):
+                    bn = bank()
+                    group([(ap(bn, (H0, H1)[s]), M("IM"), ap("G0" + b, s)) for s in range(2)] +
+                          [(ap(bn, (H0, H1)[s]), M("PL%d" % (2 * c + s)), sr) for s in range(2)], early=soon)
+                    either(ap("LX" + b, sl(2 * c, 2 * c + 2)), ap(bn), (F.Relu, 0.0, 1.0), (0.0, A.max)); lx.append(len(ops) - 1)
+                    bn = bank(); o = ap(bn, H0)
+                    if XF[cur[0]]:
+                        group([(o, ap("I32"), nf), (o, M("PN%d" % c), sr)], early=soon)
+                        either(ap(*xn[c]), o, (F.Relu, -65536.0, 1.0), (-65536.0, A.add, 0.0, A.max))
+                    else: group([(o, M("PN%d" % c), sr)]); tt(ap(*xn[c]), o, nf, A.min)
+            if fin: ts(si(b, 2), si(b, 3), 5, A.logical_shift_right)
             bn = bank()
             group([(ap(bn, sl(vb * 24 + c, vb * 24 + 24, 3)), blk(xn[c][0], vb, *xn[c][1:]), ap("BOF")) for c in range(3) for vb in range(2)])
             lin(si(b, 0), ap(bn, sl(0, 48)), -1.0, 65535.0)
-            for c in range(3):
-                bn = bank()
-                group([(ap(bn, (H0, H1)[s]), M("IM"), ap("G0" + b, s)) for s in range(2)] +
-                      [(ap(bn, (H0, H1)[s]), M("PL%d" % (2 * c + s)), ap("SR" + b)) for s in range(2)], early=ksel)
-                either(ap("LX" + b, sl(2 * c, 2 * c + 2)), ap(bn), (F.Relu, 0.0, 1.0), (0.0, A.max))
-            bn = bank()
-            group([(ap(bn, sl(96 * (2 * s + vb) + c, 96 * (2 * s + vb + 1), 3)), blk("LX" + b, vb, 2 * c + s), ap("TM"))
-                   for c in range(3) for s in range(2) for vb in range(2)])
-            sa = sl(0, 16); lin(ap("LS" + b), ap(bn, sl(0, 192)))
-            tt(un(b, 0, 4), ap(bn, sl(192, 384)), ap("LS" + b), A.min); tt(un(b, 24, 4), ap(bn, sl(192, 384)), ap("LS" + b), A.max)
+            for s in range(2):
+                bn = bank(); o = ap(bn, sl(0, 192))
+                group([(ap(bn, sl(96 * vb + c, 96 * (vb + 1), 3)), blk("LX" + b, vb, 2 * c + s), ap("TM")) for c in range(3) for vb in range(2)],
+                      early=lx[1] if PC[cur[0]] else None)
+                if s == 0: lin(ap("LS" + b), o)
+            sa = sl(0, 16); tt(un(b, 0, 4), o, ap("LS" + b), A.min); tt(un(b, 24, 4), o, ap("LS" + b), A.max)
             def above(o, a, u): tt(o, a, u, A.is_le); tt(o, o, a, A.max)
             above(un(b, 11), un(b, 24), un(b, 0)); tt(un(b, 8), un(b, 11), un(b, 1), A.min); tt(un(b, 12), un(b, 11), un(b, 1), A.max)
             above(un(b, 13), un(b, 12), un(b, 8)); above(un(b, 14), un(b, 25), un(b, 8))
             tt(un(b, 15), un(b, 14), un(b, 2), A.min); tt(un(b, 9), un(b, 15), un(b, 13), A.min)
             if not fin:
-                lin(fs(b, 0, 2, 3), un(b, 0, 2, 27)); ts(un(b, 21), keys, 0.5, A.is_lt)
-                ts(un(b, 17, 2), un(b, 8, 2), 0.3, A.is_ge); tt(fs(b, 1, 2), un(b, 8, 2), un(b, 17, 2), A.max); tt(un(b, 19), un(b, 27), un(b, 9), A.is_le)
+                lin(fs(b, 0, 2, 3), un(b, 0, 2, 27)); step(un(b, 21), keys, 0.75, -256.0)
+                step(un(b, 17, 2), un(b, 8, 2), 0.3125, 1024.0); tt(fs(b, 1, 2), un(b, 8, 2), un(b, 17, 2), A.max); tt(un(b, 19), un(b, 27), un(b, 9), A.is_le)
                 cur[1] = 1; prep(rnd + 1, b)
             else:
-                lin(un(b, 7), un(b, 0)); above(un(b, 10), un(b, 27), un(b, 9))
-                ts(un(b, 16, 4), un(b, 7, 4), 0.3, A.is_ge, -4.0, A.mult)
-                for c in range(3): tt(ap("FO" + b, sa, c), ap("UN" + b, ALL, sl(7, 11), c), ap("UN" + b, ALL, sl(16, 20), c), A.add)
-                ts(un(b, 21), keys, 0.5, A.is_ge, -2.0 ** 22, A.mult)
-                ts(si(b, 1), si(b, 0), 65535, A.bitwise_and); ts(si(b, 2), si(b, 3), 5, A.logical_shift_right)
-                for u in range(2): tt(ap("FP" + b, ALL, u), si(b, 1 + u), un(b, 21), A.add)
+                for k, u in enumerate((0, 8, 9, 27)):
+                    if k < 3: either(un(b, 16 + k), un(b, u), (F.Relu, -80.0, 256.0), (0.3125, A.is_ge, 16.0, A.mult))
+                    else: tt(un(b, 19), un(b, 27), un(b, 9), A.is_le); tt(un(b, 19), un(b, 19), un(b, 16), A.max)
+                    tt(ap("FO" + b, sa, ALL, k), un(b, u), un(b, 16 + k), A.subtract)
+                either(un(b, 21), keys, (F.Relu, -2.0 ** 23, 2.0 ** 24), (0.5, A.is_ge, 2.0 ** 23, A.mult))
+                ts(si(b, 1), si(b, 0), 65535, A.bitwise_and)
+                for u in range(2): tt(ap("FP" + b, ALL, u), si(b, 1 + u), un(b, 21), A.subtract)
                 bn = bank(); at = lambda k: sl(CW * (k % 2) + 128 * (k // 2), CW * (k % 2) + 128 * (k // 2) + 128)
                 group([(ap(bn, (96, 120), at(k)), ap("FP" + b, k), ap("I32")) for k in range(4)])
                 group([(ap(bn, (0, 96), at(k)), ap("FO" + b, sl(4 * k, 4 * k + 8)), I) for k in range(4)])
@@ -592,15 +613,25 @@ def rank_program(g, core, T, topo):
                 if not left[s]: pool[eng[s]].append(s)
         return end, order, start, eng, at, extra
 
+    def replay(w, gc, slow, wire):
+        more = {}; done = [0.0] * n; free = dict.fromkeys("PTVASX", 0.0)
+        for d, k in w[5]: more.setdefault(k, []).append(d)
+        for k in w[1]:
+            e = w[3][k]; t = max([free[e]] + [done[d] + (wire if kind[d] == "X" else lag(d, k)) for d in pred[k] + more.get(k, [])])
+            free[e] = done[k] = t + slow * (cost(k, e) + (gc - GC) * CYC * ops[k].get("gat", 0))
+        return max(t + lat[k] for k, t in enumerate(done))
+
     if "plan" not in PLAN:
         pri = [0.0] * n
         for k in range(n - 1, -1, -1): pri[k] = cost(k, "A") + max([lag(k, s) + pri[s] for s in succ[k]] + [lat[k]])
-        path = pri
-        for lead in LEADS:
-            pri = [p - lead * (o["ch"] % NB) for p, o in zip(path, ops)]
-            for k in range(PASSES):
+        path = pri; shake = np.random.RandomState(0)
+        for lead in LEADS + (None,) * SHAKES:
+            if lead is None: pri = list(np.array(PLAN["pri"]) + np.repeat(shake.normal(0, 0.4, n // 8 + 1), 8)[:n])
+            else: pri = [p - lead * (o["ch"] % NB) for p, o in zip(path, ops)]
+            for k in range(PASSES if lead else 2):
                 w = walk(pri, kind, False)
-                if "plan" not in PLAN or w[0] < PLAN["plan"][0]: PLAN["plan"] = w
+                score = w[0] + sum(replay(w, *c) / c[1] for c in OTHER) / len(OTHER)
+                if "plan" not in PLAN or score < PLAN["score"]: PLAN["plan"], PLAN["score"], PLAN["pri"] = w, score, pri
                 PLAN.setdefault("log", []).append(round(w[0], 1))
                 b = walk([t + cost(k, e) for k, (t, e) in enumerate(zip(w[2], w[3]))], w[3], True)
                 pri = [t + cost(k, e) for k, (t, e) in enumerate(zip(b[2], b[3]))]

import math
import numpy as np
from concourse.bass import DstId, RemoteDMATransfer
from concourse.mybir import AluOpType as A, AxisListType, ActivationFunctionType as F

V, G, NR, RO, NB = 512, 192, 4, 2, 2
W = V + (NR - 1) * G
CW = 256; GP = 2; U = 2.0 ** -13; KU = 2.0 ** -25
SLOTS = {1: [(0,), (0,), (2,), (2,), (1,), (3,)], 2: [(0, 1), (0, 2), (1, 2), (0, 3), (1, 3), (2, 3)],
         3: [(0, 1, 3), (0, 1, 2), None, (0, 2, 3), None, (1, 2, 3)], 4: [None, None, None, (0, 1, 2, 3), None, None]}
ROWS = {0: (0, 0, 1), 3: (0, 2, 3), 1: (0, 4, 4), 4: (1, 0, 1), 5: (1, 2, 3), 2: (1, 4, 4)}
LINES = (4, 0, 3, 1, 5, 2)
TRIV = {1: 0xAAAA, 4: 0xCCCC, 2: 0xF0F0, 5: 0xFF00}
SLOPE = {"A": ((0, -11, 5), (-12, 0, 0), (12, -9, 4), (-30, 10, 0), (0, 0, 0), (15, -9, 5)),
         "B": ((7, 0, 0), (15, -7, 3), (-9, 4, 0), (26, -18, 9), (0, 0, 0), (-19, 9, 0))}
FOLD = {"A": (-2, -26, -55), "B": (0, -16, -48)}
OFF = {"A": (4, 29, -6), "B": (-52, -59, -45)}
HEIGHT = {"A": (170, -85, -75, -170, -235, -83), "B": (0, 0, -12, 0, -117, 49)}
OFF3 = {"A": (-2, 27, 17), "B": (-39, -28, -38)}
HEIGHT3 = {"A": (170, 0, -1, -1020, -95, -1), "B": (-1020, 0, -1, -1020, -113, -1)}
CONST = (170.0, 256.0)
UW = (9, 9, -7); MUW = 5 / 64; THR = 4.125 / 16
SIG = sorted(set(x for s in SLOPE.values() for r in s for x in r if x))
ZEROED = ["A1", "A2", "B1", "B2", "TA0", "TA1", "TA2", "TB1", "TB2", "UA", "UB", "PN"]
MATS = ZEROED + ["A0", "B0", "AL", "AK", "BL", "BK", "U9", "U7", "X9", "RM", "PB", "PN0", "PN1", "PN2", "IM", "PL", "E3", "LA", "LB"] + \
    ["PL%d" % k for k in range(6)] + \
    ["Z%s%d" % (s, q) for s in "AB" for q in (0, 3, 4, 5)] + ["D%d" % x for x in SIG]
MATH = ["Z%s%d" % (s, q) for s in "AB" for q in (1, 2)]
f32, bf, i32, u16, f16 = "float32", "bfloat16", "int32", "uint16", "float16"
SCRATCH = {}
def _sb(name, shape, dt, per=1):
    for k in range(per):
        SCRATCH[name + (str(k) if per > 1 else "")] = ("sbuf", [128] + list(shape), dt)
for _n, _s, _d in (("MT", [len(MATS) * 8, 4, 4], bf), ("MH", [len(MATH) * 8, 4, 4], f16), ("TM", [8, 4], bf), ("Z3", [8, 4, 4], bf),
                   ("Z2", [160], bf), ("ZF", [128], f32), ("SEL", [8, 5, 3], f32), ("I0", [136], bf), ("I32", [128], f32),
                   ("CK", [8, 4, 4], bf), ("QI", [3, 128], bf), ("J0", [160], bf), ("JW", [4, 160], bf),
                   ("TV", [8, 4, 4], bf), ("ON", [CW], bf), ("BO", [8], bf), ("BOF", [8], f32), ("BC", [48], f32), ("PC", [4], i32),
                   ("OWN", [32], f32), ("PL", [64], i32), ("PF", [64], f32), ("WL", [4, 8, 16], bf), ("TI", [256], i32), ("TJ", [256], i32), ("BT", [256], bf), ("LUT", [1024], bf),
                   ("RS", [CW], f32), ("RZ", [CW], f32), ("INI", [V], i32), ("INF", [V], f32)):
    _sb(_n, _s, _d)
for _n, _s, _d in (("W0", [W], f32), ("WB", [2 * W], bf)):
    _sb(_n, _s, _d, NB * RO)
for _n, _s, _d in (("CE", [8192], bf), ("RQ", [CW], bf), ("FN", [4, 16], i32), ("L0", [32], u16), ("LW", [64], u16), ("D1", [32 * CW], bf),
                   ("G0", [2, CW], f16), ("GW", [4 * CW], bf), ("HH", [9, CW], bf), ("HX", [2, CW], bf), ("FE", [6, CW], bf), ("RR", [CW], bf),
                   ("VD", [CW], bf), ("AC", [2, CW], f32), ("EI", [2, CW], i32), ("ME", [4, CW], i32), ("NF", [CW], f32), ("T5", [CW], i32),
                   ("C1", [CW], u16), ("C2", [CW], u16), ("D0", [4096], bf), ("MX", [4096], bf), ("S1", [CW, 3], f32), ("KB", [CW], f32),
                   ("OB", [2, CW], bf), ("UN", [16, 28, 3], f32), ("IN", [16, 5, 3], f32), ("SI", [16, 6, 3], i32),
                   ("SS", [16, 4, 4], bf), ("SR", [2, CW], bf), ("LS", [16, 4, 3], f32), ("LX", [6, CW], f16), ("FS", [16, 4, 4], f16), ("FT", [4, 8, 16], bf),
                   ("FL", [68, 4], f16), ("LL", [64], u16), ("GL", [1024], bf), ("FO", [20, 3, 4], f16), ("FP", [4, 2, 12], f32)):
    _sb(_n, _s, _d, NB)
for _k in range(8):
    SCRATCH["B%d" % _k] = ("psum", [128, 512], f32)
DMAS = ["leaf", "tab"] + [x + str(b) + str(h) for x in ("fan", "req", "cel") for b in range(NB) for h in range(2)] + \
    [x + str(b) for x in ("oyl", "oyt", "oyc") for b in range(NB)]
SEMAPHORES = ["sP", "sT", "sV", "sA", "sent"] + ["d" + x for x in DMAS] + ["arr%d%d" % (r, k) for r in range(NB * RO) for k in range(2)]
CYC = 0.00083; PEC = 0.00042; LAG = 0.08; FIX = 0.045; AFIX = 0.02; GC = 1.6; WIRE = 6.0
VG = ((7,), None, (7,), None)
SLACK = 0.6; GAIN = 0.1; LEADS = (2, 3, 4, 5, 6, 7, 8); D1P = (0, 1); LOOK = 0.03; PASSES = 6; SHAKES = 40
XF = (0, 0, 0, 1)
PX = (0, 0, 0, 0); TE = 0; KP = (2, 0, 0, 0); CG = (0, 1); MA = 1; GWN = 2; GPS = (2, 4, 2, 2); PC = (1, 1, 0, 1); CP = (0, 1, 1, 0)
OTHER = ((1.1, 1.0, 4.0), (2.0, 1.4, 9.0), (1.2, 1.3, 8.0), (1.9, 1.1, 5.0))
HS = (1, 1, 1, 1); LS = (1, 1, 1, 1); AS = (2, 1, 1, 2); CS = (1, 1, 1, 2)
PLAN = {}
SAME = {"INI": "EI1", "INF": "AC1", "TI": "T50", "TJ": "T51", "ME1": "ME0", "GL1": "GL0", "HH1": "HH0", "HX1": "HX0", "IN1": "IN0", "LX1": "LX0", "LS1": "LS0",
        "RR1": "RR0", "OB1": "OB0", "SR1": "SR0", "FO1": "FO0", "FP1": "FP0"}
for _n in SAME: del SCRATCH[_n]


def lut_columns():
    out = {}
    for n, held in SLOTS.items():
        for q, pl in enumerate(held):
            if pl is None: continue
            w, hi, lo = ROWS[q]
            for row, half in ((hi, 1), (lo, 0)):
                wt = [0] * 9
                for m in range(8):
                    o = sum((((m + 8 * half) >> p) & 1) << k for k, p in enumerate(pl))
                    if o < 8: wt[o] += 1 << m
                out[(4 - n, 5 * w + row)] = wt
    return out


def masks(T, topo, r):
    src = T.cores[r]; dst = [T.cores[(r + d) % NR] for d in range(1, NR)]
    eng = [topo.engines(src, x) for x in dst]; used = []; out = [0] * len(dst)
    for size in sorted(set(len(e) for e in eng)):
        who = [k for k in range(len(dst)) if len(eng[k]) == size]
        free = [e for e in eng[who[0]] if e not in used]
        n = 1
        while 2 * n * len(who) <= len(free): n *= 2
        for t, k in enumerate(who):
            mine = free[t * n:(t + 1) * n]; used += mine; out[k] = sum(1 << e for e in mine)
    return out


def rank_program(g, core, T, topo):
    rank = T.rank_of(core)
    if rank is None:
        return
    Q = {"P": g, "T": g.tensor, "V": g.vector, "A": g.scalar, "S": g.sync}
    ops = []; track = {}; runs = {}; grid = {}; sess = {}; place = {}; nb = [0]; cur = [0, 0]
    sl = slice; ALL = slice(None)

    def ap(name, *idx):
        name = SAME.get(name, name)
        shape = SCRATCH[name][1] if name[0] != "@" else [128, 512]
        if name not in grid: grid[name] = np.arange(int(np.prod(shape[1:]))).reshape(shape[1:])
        if not idx or not isinstance(idx[0], tuple): idx = ((0, 128),) + idx
        cols = grid[name][idx[1:]].ravel() if len(idx) > 1 else grid[name].ravel()
        return ((slice(idx[0][0], idx[0][1]),) + idx[1:], name, cols)

    def op(eng, fn, reads, writes, cost, lat=0.0, sem=None, val=None):
        me = len(ops); deps = {}
        for acc, wr in ((reads, False), (writes, True)):
            for a in acc:
                name, cols = a[1], a[2]
                if name not in track: track[name] = (np.full(grid[name].size, -1), [])
                lastw, rd = track[name]
                for d in np.unique(lastw[cols]): deps[int(d)] = 1
                if wr:
                    m = np.zeros(lastw.size, bool); m[cols] = True; keep = []
                    for d, c in rd:
                        hit = m[c]
                        if hit.any(): deps[d] = 1
                        if not hit.all(): keep.append((d, c))
                    rd[:] = keep
                if ps(a):
                    if name[0] == "@" and me not in sess.setdefault(name, []): sess[name].append(me)
                    st = runs.setdefault(name, [None, [], []]); lab = eng if eng != "F" else me
                    if st[0] != lab: st[0], st[2], st[1] = lab, st[1], []
                    for d in st[2]: deps[d] = 1
                    if eng == "T" and st[1]: deps[st[1][-1]] = 1
                    if me not in st[1]: st[1].append(me)
        for a in reads: track[a[1]][1].append((me, a[2]))
        for a in writes: track[a[1]][0][a[2]] = me
        deps.pop(-1, None); deps.pop(me, None)
        ops.append(dict(eng=eng, ch=cur[0], up=cur[1], fn=fn, deps=list(deps), cost=cost, lat=lat, sem=sem, val=val))
        return me

    def ps(a): return a[1][0] == "@" or SCRATCH[a[1]][0] == "psum"
    def dty(a): return f32 if ps(a) else SCRATCH[a[1]][2]
    def two(*a): return all(dty(z) in (bf, u16, f16) for z in a)
    def vc(n): return FIX + max(64, n) * CYC
    def x(a): return T[place.get(a[1], a[1])][a[0]] if isinstance(a, tuple) else a
    def cols(*a): return [b for b in a if isinstance(b, tuple)]
    def bank():
        nb[0] += 1
        return "@%d" % nb[0]
    def tsf(o, a, s1, op0, s2=None, op1=None):
        if op1 is None: return lambda q: q.tensor_scalar(x(o), x(a), x(s1), None, op0)
        return lambda q: q.tensor_scalar(x(o), x(a), x(s1), x(s2), op0, op1)
    def c1(o, a): return vc(len(a[2]) * (0.5 if two(o, a) else 1))
    def ts(o, a, s1, op0, s2=None, op1=None): op("V", tsf(o, a, s1, op0, s2, op1), [a] + cols(s1, s2), [o], c1(o, a))
    def tt(o, a, b, f):
        op("V", lambda q: q.tensor_tensor(x(o), x(a), x(b), f), [a, b], [o], vc(len(a[2]) * (1 if ps(a) or ps(b) else 2)))
    def cp(o, a): op("V", lambda q: q.tensor_copy(x(o), x(a)), [a], [o], c1(o, a))
    def ms(o, c): op("V", lambda q: q.memset(x(o), c), [], [o], c1(o, o))
    def mf(o, c):
        z = ap("RQ0", sl(0, len(o[2])))
        op("F", {"A": actf(o, z, F.Identity, c, 0.0), "V": lambda q: q.memset(x(o), c)}, [z], [o], {"A": vc(len(o[2])) + AFIX, "V": c1(o, o)})
    def red(o, a): op("V", lambda q: q.tensor_reduce(x(o), x(a), AxisListType.X, A.add), [a], [o], vc(len(a[2])))
    def scan(o, a, b, f0, f1):
        op("V", lambda q: q.tensor_tensor_scan(x(o), x(a), x(b), 0.0, f0, f1), [a, b], [o], vc(len(a[2]) * (0.5 if two(o, a, b) else 1)))
    def actf(o, a, f, bias, scale): return lambda q: q.activation(x(o), x(a), f, bias=x(bias), scale=x(scale))
    def act(o, a, f, bias=0.0, scale=1.0): op("A", actf(o, a, f, bias, scale), [a] + cols(bias, scale), [o], vc(len(a[2])) + AFIX)
    def either(o, a, fa, fv):
        op("F", {"A": actf(o, a, *fa), "V": tsf(o, a, *fv)}, [a] + cols(*fa, *fv), [o], {"A": vc(len(a[2])) + AFIX, "V": c1(o, a)})
    def lin(o, a, scale=1.0, bias=0.0): either(o, a, (F.Identity, bias, scale), (scale, A.mult, bias, A.add))
    def step(o, a, at, steep): either(o, a, (F.Sigmoid, -at * steep, steep), (at, A.is_ge if steep > 0 else A.is_lt))
    def mm(o, l, r, start=False, stop=False):
        n = max(min(64, len(l[2])), len(r[2])) * (4 if dty(l) == f32 else 1)
        op("T", lambda q: q.matmul(x(o), x(l), x(r), start, stop), [l, r], [o], 0.02 + n * PEC)
    def group(items, after=None, early=None, close=True):
        first = len(ops)
        for k, it in enumerate(items): mm(it[0], it[1], it[2], k == 0, close and k == len(items) - 1)
        d = ops[first]["deps"]
        more = [early] if early is not None else [z for o in ops[first + 1:] for z in o["deps"]]
        for z in more + [first if after is None else after]:
            if z < first and z not in d: d.append(z)
        return first
    def sel(o, a, pat, base, fill, cmp=None, cm=1):
        op("P", lambda q: q.affine_select(x(o), x(a), pat, A.not_equal if cmp is None else cmp, fill, base, cm), [a], [o], 0.2 + 2 * len(o[2]) * CYC)
    def iota(o, pat, base, cm, fl=False):
        fn = (lambda q: q.iota(x(o), pat, base, cm, allow_small_or_imprecise_dtypes=True)) if fl else (lambda q: q.iota(x(o), pat, base, cm))
        op("P", fn, [], [o], 0.15 + 2 * len(o[2]) * CYC)
    def gat(o, win, off, kind):
        w = lambda: x(win).indirect(x(off)); c = 0.07 + GC * len(o[2]) * CYC
        if kind == "any": op("F", {"V": lambda q: q.tensor_copy(x(o), w()), "A": lambda q: q.activation(x(o), w(), F.Copy)}, [win, off], [o], {"A": c, "V": c})
        elif kind == "V": op("V", lambda q: q.tensor_copy(x(o), w()), [win, off], [o], c)
        elif kind == "A": op("A", lambda q: q.activation(x(o), w(), F.Copy), [win, off], [o], c)
        else: op("V", lambda q: q.tensor_scalar(x(o), w(), kind, None, A.min), [win, off], [o], c)
        ops[-1]["gat"] = len(o[2])
    def dma(name, o, a, rd, wr, nbytes):
        op("S", lambda q: q.dma_start(o, a), rd, wr, 0.08, lat=2.0 + nbytes / 150e3, sem="d" + name, val=16)
    def who(k): return "any" if VG[cur[0]] is None else "V" if k in VG[cur[0]] else "A"
    def also(k): ops[-1]["deps"] += [z for z in k if z not in ops[-1]["deps"]]
    def M(name, *idx):
        t, names = ("MH", MATH) if name in MATH else ("MT", MATS); k = names.index(name) * 8
        return ap(t, sl(k, k + 8), *idx)
    def bc(k): return ap("BC", sl(k, k + 1))
    def half(h): return (64 * h, 64 * h + 64)
    def shift(k): return ap("I0", sl(8 - k, 136 - k))
    I = shift(0); Z3 = ap("Z3")
    H0, H1, H2 = sl(0, CW), sl(CW, 2 * CW), sl(0, 2 * CW)

    INI, INF = T[SAME["INI"]], T[SAME["INF"]]
    dma("leaf", INI[0:96, :], T.leaf0[:, :], [], [ap("INI")], 2e5)
    dma("tab", INI[96:120, :], T.tab0[:, :], [], [], 5e4); tabop = len(ops) - 1
    both = {}
    for name, buf, size in (("fan", "FN", 3e4), ("req", "RQ", 5e4), ("cel", "CE", 2e6)):
        for b in range(NB):
            for h in range(2):
                r = sl(64 * b, 64 * b + 64)
                src = {"fan": T.fan[r, :], "req": T.req[r, CW * h:CW * (h + 1)], "cel": T.cells[r, :]}[name]
                dma("%s%d%d" % (name, b, h), T[buf + str(b)][64 * h:64 * h + 64], src, [], [ap(buf + str(b))] if h else [], size)
                both[(buf, b, h)] = len(ops) - 1
            ops[-1]["deps"].append(both[(buf, b, 0)]); ops[-1]["pair"] = both[(buf, b, 0)]

    ms(ap("ZF"), 0.0); ms(ap("Z2"), 0.0); ms(Z3, 0.0); ms(ap("PF"), 0.0)
    iota(ap("PC", sl(0, 1)), [[0, 1]], 0, 1)
    sel(ap("I32"), ap("ZF"), [[-1, 128]], 0, 1.0); iota(ap("TI"), [[1, 256]], 0, 0)
    ms(ap("SEL"), 0.0)
    sel(ap("SEL", ALL, sl(0, 4)), ap("SEL", ALL, sl(0, 4)), [[-12, 8], [-1, 4], [-4, 3]], 0, 1.0)
    sel(ap("SEL", ALL, 4), ap("SEL", ALL, 4), [[-3, 8], [-1, 3]], -96, 1.0)
    for b in range(NB): iota(ap("OWN", sl(16 * b, 16 * b + 16)), [[128, 2], [CW, 2], [0, 4]], V * rank, 1, True)
    sel(ap("I0"), ap("Z2", sl(0, 136)), [[-1, 136]], 8, 1.0)
    sel(ap("J0"), ap("Z2"), [[-1, 160]], 16, 1.0)
    sel(ap("J0", sl(80, 144)), ap("J0", sl(80, 144)), [[-1, 64]], 0, 1.0); sel(ap("J0", sl(16, 80)), ap("J0", sl(16, 80)), [[-1, 64]], -64, 1.0)
    ms(ap("MT", sl(0, 8 * len(ZEROED))), 0.0)
    G4 = [[-16, 8], [0, 4]]; G16 = [[-16, 8], [0, 16]]
    def real(s): return (sl(0, 3), ALL) if s == "A" else (ALL, sl(0, 3))
    def last(s): return (3, ALL) if s == "A" else (ALL, 3)
    def pat(s, st, n=4): return [[-16, 8], [-st, n], [0, 4]] if s == "A" else [[-16, 8], [0, 4], [-st, n]]
    def part(name, s, st, row, w): sel(M(name, *real(s)), M(name, *real(s)), pat(s, st, 3), -row, w)
    for s, w in (("A", 1.0), ("B", -1.0)):
        sel(M(s + "0"), Z3, pat(s, 1), 0, w)
        for k in (1, 2): part(s + str(k), s, 1, 4 * k, w)
    for s, w in (("A", 1.0), ("B", -1.0)):
        sel(M(s + "L"), Z3, pat(s, 1), -12, w); sel(M(s + "L", *last(s)), ap("Z3", ALL, *last(s)), G4, -3, w)
        sel(M(s + "K"), M(s + "L"), pat(s, 4), -7, 2048.0 * w)
    for s in "AB":
        for k in range(3):
            if FOLD[s][k]: part("T%s%d" % (s, k), s, 4, 7, FOLD[s][k] / 16)
    muA = 5 + MUW - sum(m * t for m, t in zip(UW, FOLD["A"])) / 16
    part("UA", "A", 4, 7, muA); part("UB", "B", 4, 7, MUW)
    for q0, q1 in ((4, 0), (3, 5), (1, 2)):
        for s in "AB":
            z = "Z%s%d" % (s, q0); hi, lo = ROWS[q0][1:]
            sel(M(z), Z3, G16, -15, 65536 * HEIGHT[s][q0] / CONST[ROWS[q0][0]])
            if hi == lo: part(z, s, 5, lo, 257.0)
            else: part(z, s, 5, hi, 256.0); part(z, s, 5, lo, 1.0)
            sel(M("Z%s%d" % (s, q1)), M(z), G16, -15, 65536 * HEIGHT[s][q1] / CONST[ROWS[q1][0]])
    for s in "AB":
        for q in (0, 3, 1, 5, 2):
            z = M("Z%s%d" % (s, q), *last(s))
            if q in TRIV or HEIGHT3[s][q] != HEIGHT[s][q]: sel(z, z, G4, -15, (65536 * HEIGHT3[s][q] + TRIV.get(q, 0)) / CONST[ROWS[q][0]])
    ms(ap("CK"), -32.0 * KU)
    sel(M("RM"), ap("CK"), G16, 0, 0.0, A.is_ge); sel(M("RM"), M("RM"), [[16, 8], [0, 16]], 15, 0.0, A.is_ge, -1)
    lin(ap("BO"), M("RM", 0, 0), -1.0); lin(ap("BOF"), M("RM", 0, 0), -1.0 / (32 * KU))
    for b in range(NB):
        for p in range(16):
            o = ap("D1%d" % b, sl(2 * p + 1, 32 * CW, 32))
            if D1P[b]: sel(o, ap("RQ%d" % b), [[0, CW]], 1, 0.0, A.is_ge, 0)
            else: lin(o, ap("RQ%d" % b))
        if b == 0:
            TM = ap("TM"); ms(TM, U); KL = 8192.0
            sel(TM, TM, [[-16, 8], [-4, 4]], 0, 0.0, A.is_ge); sel(TM, TM, [[16, 8], [4, 4]], 3, 0.0, A.is_ge, -1)
            sel(ap("TM", ALL, 3), ap("TM", ALL, 3), [[-16, 8]], -3, U)
            sel(M("PL"), Z3, G16, -8, -KL); sel(M("E3"), Z3, G16, -3, 2 * KL); sel(M("LA"), Z3, G16, -15, -16 * KL)
            for i in (1, 2, 3): sel(M("PL", ALL, i), M("PL", ALL, i), G4, 0, 2 * KL * i)
            for i in (0, 1, 2): sel(M("LA", ALL, i), M("LA", ALL, i), G4, -15, -KL * i * i)
            sel(M("LA", 0, sl(3, 4)), M("LA", 0, sl(3, 4)), [[-16, 8]], -15, -9 * KL); lin(M("LB"), M("LA"))
            for s, none in (("A", 4096.0), ("B", 3072.0)): sel(M("L" + s, sl(1, 3), 3), M("L" + s, sl(1, 3), 3), [[-16, 8], [0, 2]], -15, none - 9 * KL)
            for u in range(2):
                bn = bank(); it = []
                for k in range(3 * u, 3 * u + 3):
                    o = ap(bn, sl(128 * (k % 3), 128 * (k % 3) + 128)); c, s = k // 2, k % 2
                    it += [(o, shift(c + 4 * s), M("PL")), (o, shift(4 * c), M("E3")), (o, I, M("L" + "AB"[s]))]
                group(it); k = 8 * MATS.index("PL%d" % (3 * u)); lin(ap("MT", sl(k, k + 24)), ap(bn, sl(0, 384)))
            iota(ap("QI", 0), [[0, 8], [1, 4], [0, 4]], 0, 0, True); iota(ap("QI", 1), [[0, 32], [1, 4]], 0, 0, True)
            tt(ap("QI", sl(0, 2)), ap("QI", sl(0, 2)), ap("QI", sl(0, 2)), A.mult); tt(ap("QI", 2), ap("QI", 0), ap("QI", 1), A.add)
            lin(ap("QI", 2), ap("QI", 2), -65536.0, 65536.0)
            sel(M("PB"), ap("QI", 2), G16, -15, 0.0, A.is_equal)
            sel(M("PN"), M("PN"), G16, -8, -65536.0); sel(M("PN"), M("PN"), G16, -12, -65536.0)
            for i in (1, 2, 3):
                for row, view in ((0, (i, ALL)), (4, (ALL, i))): sel(M("PN", *view), M("PN", *view), G4, -row, 131072.0 * i)
            bn = bank(); it = []
            for c in range(3):
                o = ap(bn, sl(128 * c, 128 * c + 128)); it += [(o, shift(c), M("PN")), (o, I, M("PB"))]
            group(it); k = 8 * MATS.index("PN0"); lin(ap("MT", sl(k, k + 24)), ap(bn, sl(0, 384)))
    ts(ap("PC", sl(1, 2)), ap("PC", sl(0, 1)), 15, A.bitwise_and); ts(ap("PC", sl(2, 3)), ap("PC", sl(0, 1)), 3, A.bitwise_and)
    p16 = ap("PC", sl(1, 2)); ta, tb, t15 = bc(0), bc(1), bc(2)
    ts(ta, p16, 12.0, A.is_ge); ts(tb, ap("PC", sl(2, 3)), 3.0, A.is_equal); ts(t15, p16, 15.0, A.is_equal)
    ts(bc(16), p16, 7.0, A.is_ge, tb, A.mult); lin(bc(3), bc(16), -8191.0, 8192.0); lin(bc(4), t15, 256.0)
    lin(bc(39), bc(16), -1.0, 1.0); lin(M("IM"), I, bc(39))
    for w in range(2):
        ts(bc(16), p16, 5.0 * w, A.is_ge); ts(bc(5 + w), p16, 5.0 * w + 5, A.is_lt, bc(16), A.mult)
        ts(bc(37 + w), ap("PC", sl(0, 1)), 64.0, A.is_ge, bc(5 + w), A.mult); tt(bc(5 + w), bc(5 + w), bc(37 + w), A.subtract)
        lin(ap("JW", 2 * w), ap("J0"), bc(5 + w)); lin(ap("JW", 2 * w + 1), ap("J0"), bc(37 + w))
    lc = lut_columns(); seen = {}; fills = []
    for (n, row), w in sorted(lc.items()):
        for j in range(4):
            val = w[2 * j] + (w[2 * j + 1] << 8)
            if val: seen.setdefault((j, val), []).append(16 * n + row)
    def fill(o, v):
        z = ap("ZF", (o[0][0].start, o[0][0].stop), sl(0, len(o[2])))
        op("F", {"A": actf(o, z, F.Identity, v, 1.0), "V": lambda q: q.memset(x(o), v)}, [z, o], [], {"A": vc(1) + AFIX, "V": vc(1)})
        fills.append(len(ops) - 1)
    for (j, val), cs in sorted(seen.items()):
        while cs:
            st = cs[1] - cs[0] if len(cs) > 1 else 1; k = 1
            while k < len(cs) and cs[k] - cs[k - 1] == st: k += 1
            fill(ap("PF", (32 * j, 32 * j + 32), sl(cs[0], cs[k - 1] + 1, st)), float(val))
            cs = cs[k:]
    p32 = ap("PC", sl(3, 4)); ts(p32, ap("PC", sl(0, 1)), 31, A.bitwise_and); FLOOR = -0.5 + 2.0 ** -9
    ts(bc(20), p32, 1.0, A.is_equal); lin(bc(21), bc(20), 2.0 ** -8 - 1, 1.0); lin(bc(22), bc(20), FLOOR)
    lin(ap("PL"), ap("PF"), bc(21), bc(22)); also(fills); ts(ap("PL"), ap("PL"), 255, A.bitwise_and)
    lin(ap("WL", ALL, 0), ap("PL"))
    for k in (1, 2, 4): lin(ap("WL", ALL, sl(k, 2 * k)), ap("WL", ALL, sl(0, k)))
    for j in range(4): ms(ap("BC", (32 * j, 32 * j + 32), sl(18, 19)), 4.0 ** -j)
    ts(bc(19), p32, -0.5, A.mult, 1.0, A.add); ts(bc(19), bc(19), 0.0, A.max, bc(18), A.mult)
    lin(ap("TJ"), ap("TI"), bc(19), FLOOR); ts(ap("TJ"), ap("TJ"), 1, A.bitwise_and); lin(ap("BT"), ap("TJ"))
    for n0 in (0, 2):
        bn = bank()
        group([(ap(bn, (H0, H1)[u]), ap("WL", n0 + u), ap("BT")) for u in range(2)])
        lin(ap("LUT", sl(256 * n0, 256 * n0 + 512)), ap(bn))
    LN = math.log(9 / 7)
    ms(bc(7), LN); lin(bc(8), ta, 4096.0 * 256, LN); lin(bc(9), tb, -3072.0 * 256, LN); lin(bc(10), ta, 4096.0 * 256, bc(9)); lin(bc(11), tb, -2.0 ** 24, LN)
    for u, s in enumerate("AB"):
        for k in range(3): lin(bc(24 + 3 * u + k), (ta, tb)[u], 3.0 * FOLD[s][k] + OFF3[s][k] - OFF[s][k], float(OFF[s][k]))
        lin(bc(14 + u), (ta, tb)[u], TRIV[4] + 65536.0 * (HEIGHT3[s][4] - HEIGHT[s][4]))
    pp = ap("PC", sl(0, 1))
    ts(bc(35), pp, 96.0, A.is_lt, 8191.0, A.mult); lin(bc(35), bc(35), 1.0, 1.0)
    ts(bc(16), pp, 96.0, A.is_ge); ts(bc(36), pp, 108.0, A.is_lt, bc(16), A.mult); lin(bc(36), bc(36), 1.0, -1.0)
    for name, w in [("U9", 9 / 16), ("U7", -7 / 16), ("X9", 9.0)] + [("D%d" % v, 65536.0 * v) for v in SIG]: lin(M(name), I, w)
    ms(ap("TV", (0, 64)), 0.0); ms(ap("ON", (0, 64)), 1.0)
    base, base3 = [157.0 - THR - sum(m * o for m, o in zip(UW, off["A"])) / 16 for off in (OFF, OFF3)]
    base3 += 3 * muA
    for view, v in (((), base), (last("A"), base3), (last("B"), base + 3 * MUW), ((3, sl(3, 4)), base3 + 3 * MUW)):
        for p, y in ((0, float(math.floor(v))), (32, v - math.floor(v))): ms(ap("TV", (p, p + 1), ALL, *view), y)
    mf(ap("RS"), 0.0); mf(ap("RS", sl(0, CW, 16)), 2.0 ** 34); mf(ap("RZ"), KU); mf(ap("RZ", sl(15, CW, 16)), 2.0 ** 34)
    for b in range(NB):
        b = str(b)
        for h in range(2): lin(ap("L0" + b, half(h)), ap("FN" + b, half(h), sl(h, 4, 2)))
        for w in range(2): lin(ap("LW" + b, sl(32 * w, 32 * w + 32)), ap("L0" + b), 2.0, float(w))
        mf(ap("SS" + b), 1.0); ms(ap("FT" + b), 0.0); ms(ap("FT" + b, ALL, ALL, 15), CONST[0] - CONST[1]); ms(ap("FL" + b), 0.0)
        ms(ap("D0" + b, sl(0, 4096, 2)), -1.0)
        lin(ap("FS" + b, ALL, 0, 3), ap("OWN", sl(16 * int(b), 16 * int(b) + 16)), U)
    mf(ap("FO0", sl(16, 20)), 0.0)
    for h in range(2): lin(ap("INF", (0, 120), h), ap("INI", (0, 120), h)); also([tabop])

    def un(b, k, n=1, st=1): return ap("UN" + b, ALL, sl(k, k + (n - 1) * st + 1, st))
    def si(b, k, n=1): return ap("SI" + b, ALL, sl(k, k + n))
    def fs(b, k, n=1, st=1): return ap("FS" + b, ALL, sl(k, k + (n - 1) * st + 1, st), sl(0, 3))
    def prep(rnd, b):
        wn = str(RO * int(b) + rnd); w0, wb = "W0" + wn, "WB" + wn
        mu = ap("FS" + b, ALL, sl(1, 4), 3)
        tt(un(b, 20), un(b, 17), un(b, 18), A.add); tt(un(b, 20), un(b, 20), un(b, 19), A.add); tt(mu, un(b, 20), un(b, 21), A.mult)
        for h in range(2):
            bn = bank()
            for d in range(2):
                group([(ap(bn, half(d), sl(128 * vb, 128 * vb + 128)), ap("FS" + b, sl(8 * vb + 4 * h, 8 * vb + 4 * h + 4)), I) for vb in range(2)])
            ts(ap(w0, sl(CW * h, CW * h + CW)), ap(bn, H0), bc(3), A.mult, 4096.0, A.min)
        ts(si(b, 1), si(b, 0), 255, A.bitwise_and); ts(si(b, 2), si(b, 0), 8, A.logical_shift_right, 255, A.bitwise_and)
        lin(un(b, 23), mu, 256.0); tt(ap("FL" + b, sl(3, 64, 4), sl(0, 3)), un(b, 23), si(b, 1), A.add)
        either(un(b, 22), mu, (F.Relu, 1.0, -1.0), (0.0, A.is_equal))
        for d in range(2): tt(ap("FT" + b, ALL, sl(4 * d, 4 * d + 4), sl(ROWS[3][1], 15, 5)), si(b, 2), un(b, 22), A.mult)
        bn = bank(); blocks = [(vb, hh) for vb in range(2) for hh in range(2)]
        group([(ap(bn, sl(0, 64)), ap("FL" + b, sl(31 * vb + 3 - 2 * hh, 31 * vb + 35 - 2 * hh)), ap("I0", sl(8 + hh, 136, 2))) for vb, hh in blocks])
        lin(ap("LL" + b), ap(bn, sl(0, 64)))
        gat(ap("GL" + b), ap("LUT"), ap("LL" + b), "any")
        for h in range(2):
            bn = bank(); at = lambda w, vb: ap(bn, sl(CW * vb + w, CW * vb + CW, 2))
            it = [(at(w, vb), ap("JW", 2 * w + h, sl(16 + 5 * w - 5 * c, 144 + 5 * w - 5 * c)), ap("GL" + b, sl(4 * vb + c, 1024, 8)))
                  for c in range(3) for w in range(2) for vb in range(2)]
            group(it + [(at(ROWS[3][0], vb), ap("FT" + b, 2 * vb + h), I) for vb in range(2)])
            lin(ap(wb, sl(V * h, V * h + V)), ap(bn), 1.0, bc(4))
        for kind, name, m in ((0, w0, 1), (1, wb, 2)):
            def send(q, kind=kind, name=name, m=m):
                tr = []
                for d in range(1, NR):
                    rid, pid, se = topo.addr(T.cores[(rank + d) % NR]); o = m * (V + (d - 1) * G)
                    tr.append(RemoteDMATransfer(dst_ids=[DstId(rid=rid, pnc=pid)], dma_engine_mask=masks(T, topo, rank)[d - 1],
                                                remote_sem=T.sem["arr%s%d" % (wn, kind)], src=T[name][:, 0:m * G], dst=T[name][:, o:o + m * G]))
                q.remote_dma_fused(tr, local_sem=T.sem.sent)
            op("P", send, [ap(name, sl(0, m * G))], [], 1.0, sem="none")
            me = len(ops) - 1
            n = sum(bin(masks(T, topo, (rank - d) % NR)[d - 1]).count("1") for d in range(1, NR))
            op("X", None, [], [ap(name, sl(m * V, m * W))], 0.0, lat=WIRE, sem="arr%s%d" % (wn, kind), val=n)
            also([me])
            if rnd == 0 and kind == CG[int(b)]:
                for h in range(2): ops[both[("CE", int(b), h)]]["deps"].append(len(ops) - 1)

    for b in range(NB):
        kb = bank(); r120 = (0, 120); cur[0] = b
        group([(ap(kb, sl(60 * (2 * vb + h), 60 * (2 * vb + h + 1))), ap("INF", r120, h, sl(128 * vb, 128 * vb + 128)),
                ap("SEL", r120, sl(4 * b, 4 * b + 4))) for vb in range(2) for h in range(2)])
        b = str(b); raw = ap("IN" + b, ALL, sl(0, 4))
        lin(ap("IN" + b), ap(kb, sl(0, 240)))
        either(un(b, 16, 4), raw, (F.Relu, 0.0, -1.0), (0.0, A.is_lt)); lin(un(b, 7, 4), raw, U); lin(si(b, 0), ap("IN" + b, ALL, sl(4, 5)))
        tt(fs(b, 0, 3), un(b, 7, 3), un(b, 16, 3), A.max)
        tt(un(b, 11, 2), un(b, 7, 2), un(b, 9, 2), A.max); tt(un(b, 11), un(b, 11), un(b, 12), A.max); tt(fs(b, 3), un(b, 11), un(b, 16), A.max)
        lin(un(b, 21), un(b, 16), -1.0, 1.0)
        prep(0, b)

    CL = [(1, 0), (2, 0), (0, 1), (0, 2), (1, 1), (1, 2), (2, 1), (2, 2), (0, 0)]
    for rnd in range(RO):
        fin = rnd == RO - 1
        for bi in range(NB):
            b = str(bi); wn = str(RO * bi + rnd); w0, wb = "W0" + wn, "WB" + wn; cur[0] = NB * rnd + bi; cur[1] = 1
            gat(ap("G0" + b, 0), ap(w0), ap("L0" + b, sl(0, 16)), "any"); gat(ap("G0" + b, 1), ap(w0), ap("L0" + b, sl(16, 32)), 3072.0)
            for w in range(GWN): gat(ap("GW" + b, sl(4 * w * CW // GWN, 4 * (w + 1) * CW // GWN)), ap(wb), ap("LW" + b, sl(64 * w // GWN, 64 * (w + 1) // GWN)), "any")

            def head(cs):
                m = cs.stop - cs.start; P0, P1, P2 = sl(0, m), sl(m, 2 * m), sl(0, 2 * m); PP = (P0, P1)
                ga, gb = ap("G0" + b, 0, cs), ap("G0" + b, 1, cs)
                hh = lambda t, n=1: ap("HH" + b, sl(t, t + n), cs)
                fe = lambda s, k: ap("FE" + b, 3 * s + k, cs)
                for t, bias in ((0, 8), (2, 9), (4, 10), (6, 10)):
                    bn = bank(); it = []
                    for u, (k, l) in enumerate(CL[t:t + 2]): it += [(ap(bn, PP[u]), M("A%d" % k), ga), (ap(bn, PP[u]), M("B%d" % l), gb)]
                    got = group(it); act(hh(t, 2), ap(bn, P2), F.Sigmoid, bc(bias), 256.0)
                bn = bank(); group([(ap(bn, P0), M("A0"), ga), (ap(bn, P0), M("B0"), gb)]); act(hh(8), ap(bn, P0), F.Sigmoid, bc(7), 256.0)
                for k in range(3):
                    bn = bank(); it = [(ap(bn, PP[s]), M("T%s%d" % ("AB"[s], k)), (ga, gb)[s]) for s in range(2) if FOLD["AB"[s]][k]]
                    for l in range(3): it += [(ap(bn, P0), I, hh(CL.index((k, l)))), (ap(bn, P1), I, hh(CL.index((l, k))))]
                    group(it, early=got if TE else None)
                    for s in range(2): lin(fe(s, k), ap(bn, PP[s]), 16.0, bc(24 + 3 * s + k))

            def lines(cs):
                m = cs.stop - cs.start; P0, P1, P2 = sl(0, m), sl(m, 2 * m), sl(0, 2 * m); PP = (P0, P1)
                fe = lambda s, k: ap("FE" + b, 3 * s + k, cs)
                prev = None; ac = ap("AC" + b, ALL, cs); ei = ap("EI" + b, ALL, cs)
                for q in LINES:
                    bn = bank(); it = []
                    for s in range(2):
                        S = "AB"[s]; o = ap(bn, PP[s])
                        it += [(o, M("D%d" % v), fe(s, k)) for k, v in enumerate(SLOPE[S][q]) if v]
                        at = (2 * ROWS[q][0] + s) * CW
                        it += [(o, M("Z%s%d" % (S, q)), ap("GW" + b, sl(at + cs.start, at + cs.stop)))]
                    prev = group(it, prev)
                    if q == LINES[0]:
                        for s in range(2): lin(ap("AC" + b, s, cs), ap(bn, PP[s]), 1.0, bc(14 + s))
                    else: tt(ei if q == LINES[-1] else ac, ap(bn, P2), ac, A.max)

            def codes(cs):
                m = cs.stop - cs.start; P0 = sl(0, m); ei = ap("EI" + b, ALL, cs)
                for e, mk in ((0, 0x5555), (1, 0xAAAA)): ts(ap("ME" + b, sl(e, e + 3, 2), cs), ei, mk, A.bitwise_and)
                def near(a):
                    if not PX[cur[0]]: return a
                    o = ap(bank(), P0); act(o, a, F.Identity)
                    return o
                if m == CW: tt(ei, ap("ME" + b, sl(0, 2)), ap("ME" + b, sl(2, 4)), A.add)
                for e, mk in ((0, 0x5555), (1, 0xAAAA)):
                    o = ap("EI" + b, e, cs)
                    if m < CW: tt(o, near(ap("ME" + b, e, cs)), ap("ME" + b, 2 + e, cs), A.add)
                    ts(o, o, 1, A.logical_shift_right, mk, A.bitwise_and)
                nf = ap("NF" + b, cs); t5 = ap("T5" + b, cs)
                tt(nf, near(ap("EI" + b, 0, cs)), ap("EI" + b, 1, cs), A.add)
                lin(ap("C2" + b, cs), nf, -0.125, 65531.5 / 8); lin(t5, nf, -1.0 / 32, 65519.5 / 32)
                bn = bank(); lin(ap(bn, P0), t5, 29.0, 65535.0)
                tt(t5, ap(bn, P0), nf, A.subtract); ts(t5, t5, 8191, A.bitwise_and)
                if CP[cur[0]]: sel(ap("C1" + b, cs), t5, [[0, m]], 1, 0.0, A.is_ge, 0)
                else: lin(ap("C1" + b, cs), t5)
            for stage, pieces in ((head, HS), (lines, LS), (codes, AS)):
                n = pieces[cur[0]]
                for u in range(n): stage(sl(u * CW // n, (u + 1) * CW // n))
            cur[1] = 0; nf = ap("NF" + b)
            bn = bank(); ga, gb = ap("G0" + b, 0), ap("G0" + b, 1); hx = (ap("HX" + b, 0), ap("HX" + b, 1))
            group([(ap(bn, H0), M("AL"), ga), (ap(bn, H0), M("BK"), gb), (ap(bn, H1), M("AK"), ga), (ap(bn, H1), M("BL"), gb)])
            act(hx[0], ap(bn, H0), F.Sigmoid, bc(11), 256.0); act(hx[1], ap(bn, H1), F.Sigmoid, bc(8), 256.0)
            bn = bank(); o = ap(bn, H0)
            it = [(o, M("UA"), ga), (o, M("UB"), gb), (o, M("X9"), hx[0]), (o, M("X9"), hx[1]), (o, ap("TV", (0, 33)), ap("ON", (0, 33)))]
            group(it + [(o, M("U%d" % abs(m)), ap("FE" + b, k)) for k, m in enumerate(UW)])
            lin(ap("RR" + b), o); tt(ap("VD" + b), o, ap("RR" + b), A.is_lt)
            blk = lambda name, vb, *s: ap(name, *s, sl(vb * 128, vb * 128 + 128))
            n = CS[NB * rnd + bi]
            for vb in range(2):
                r = str(vb); o = 32 * 128 * vb; GP = GPS[cur[0]]; m = 128 // GP
                for h in range(GP):
                    c = sl(vb * 128 + h * m, vb * 128 + (h + 1) * m); lo, hi = 32 * h * m, 32 * (h + 1) * m
                    gat(ap("D0" + r, sl(lo + 1, hi, 2)), ap("CE" + b), ap("C2" + b, c), who(2 * (vb * GP + h)))
                    gat(ap("D1" + b, sl(o + lo, o + hi, 2)), ap("CE" + b), ap("C1" + b, c), who(2 * (vb * GP + h) + 1))
                    scan(ap("MX" + r, sl(lo, hi)), ap("D0" + r, sl(lo, hi)), ap("D1" + b, sl(o + lo, o + hi)), A.min, A.max)
                if n == 2 or vb == 0:
                    kbs = [bank() for _ in range(1 + KP[cur[0]])]; vs = [vb] if n == 2 else [0, 1]; gate = len(ops) - 1
                    for kb in kbs:
                        it = [(blk(kb, v), blk("VD" + b, v), I) for v in vs]
                        if fin: it += [(blk(kb, v), blk("RQ" + b, v), M("RM")) for v in vs]
                        for k, t in enumerate(it):
                            mm(t[0], t[1], t[2], k == 0, False)
                            if k == 0: also([gate])
                for kb in kbs:
                    for p in range(16):
                        mm(ap(kb, sl(vb * 128 + p, vb * 128 + 128, 16)), ap("MX" + r, sl(2 * p + 1, 4096, 32)), ap("BO"), False,
                           p == 15 and vb == vs[-1] and kb == kbs[0])
                if vb < vs[-1]: continue
                c0, c9 = 128 * vs[0], 128 * vb + 128; cs = sl(c0, c9); rv = sl(c9 - 1, c0 - 1 if c0 else None, -1); kb = kbs[0]
                for c in range(3):
                    scan(ap("S1" + b, rv, c), ap("RZ", rv), ap(kb, rv), A.add, A.min)
                    if c < 2:
                        key = ap(kb, cs); ob = ap("OB" + b, c, cs)
                        scan(ap("KB" + b, cs), ap("RS", cs), ap("S1" + b, cs, c), A.add, A.min); tt(ob, key, ap("KB" + b, cs), A.is_le)
                        if c < KP[cur[0]]:
                            kb = kbs[c + 1]
                            for k in kbs[c + 1:]: mm(ap(k, cs), I, ob, False, k == kb)
                        else: tt(key, key, ob, A.max)
                    ksel = len(ops) - 1
            keys = ap("S1" + b, sl(0, CW, 16))
            xn = [("AC" + b, 0), ("AC" + b, 1), ("KB" + b,)]; lx = []
            for u, cc in enumerate((sl(0, 2), sl(2, 3)) if PC[cur[0]] else (sl(0, 3),)):
                sc = lambda k, n=1: ap("SI" + b, ALL, sl(k, k + n), cc); ss = lambda t: ap("SS" + b, ALL, sl(t, t + 2), cc)
                kc = ap("S1" + b, sl(0, CW, 16), cc); sr = ap("SR" + b, u)
                lin(sc(3), kc, 1 / KU); soon = len(ops) - 1 if PC[cur[0]] else ksel
                ts(sc(4), sc(3), 2, A.logical_shift_right, 3, A.bitwise_and); ts(sc(5), sc(3), 3, A.bitwise_and)
                lin(ss(0), sc(4, 2)); act(ss(2), sc(4, 2), F.Square); step(ap("SS" + b, ALL, cc, 3), kc, 0.75, 256.0)
                bn = bank()
                group([(blk(bn, vb), ap("SS" + b, sl(vb * 8, vb * 8 + 8)), I) for vb in range(2)])
                lin(sr, ap(bn, H0))
                for c in range(cc.start, cc.stop):
                    bn = bank()
                    group([(ap(bn, (H0, H1)[s]), M("IM"), ap("G0" + b, s)) for s in range(2)] +
                          [(ap(bn, (H0, H1)[s]), M("PL%d" % (2 * c + s)), sr) for s in range(2)], early=soon)
                    either(ap("LX" + b, sl(2 * c, 2 * c + 2)), ap(bn), (F.Relu, 0.0, 1.0), (0.0, A.max)); lx.append(len(ops) - 1)
                    bn = bank(); o = ap(bn, H0)
                    if XF[cur[0]]:
                        group([(o, ap("I32"), nf), (o, M("PN%d" % c), sr)], early=soon)
                        either(ap(*xn[c]), o, (F.Relu, -65536.0, 1.0), (-65536.0, A.add, 0.0, A.max))
                    else: group([(o, M("PN%d" % c), sr)]); tt(ap(*xn[c]), o, nf, A.min)
            if fin: ts(si(b, 2), si(b, 3), 5, A.logical_shift_right)
            bn = bank()
            group([(ap(bn, sl(vb * 24 + c, vb * 24 + 24, 3)), blk(xn[c][0], vb, *xn[c][1:]), ap("BOF")) for c in range(3) for vb in range(2)])
            lin(si(b, 0), ap(bn, sl(0, 48)), -1.0, 65535.0)
            for s in range(2):
                bn = bank(); o = ap(bn, sl(0, 192))
                group([(ap(bn, sl(96 * vb + c, 96 * (vb + 1), 3)), blk("LX" + b, vb, 2 * c + s), ap("TM")) for c in range(3) for vb in range(2)],
                      early=lx[1] if PC[cur[0]] else None)
                if s == 0: lin(ap("LS" + b), o)
            sa = sl(0, 16); tt(un(b, 0, 4), o, ap("LS" + b), A.min); tt(un(b, 24, 4), o, ap("LS" + b), A.max)
            def above(o, a, u): tt(o, a, u, A.is_le); tt(o, o, a, A.max)
            above(un(b, 11), un(b, 24), un(b, 0)); tt(un(b, 8), un(b, 11), un(b, 1), A.min); tt(un(b, 12), un(b, 11), un(b, 1), A.max)
            above(un(b, 13), un(b, 12), un(b, 8)); above(un(b, 14), un(b, 25), un(b, 8))
            tt(un(b, 15), un(b, 14), un(b, 2), A.min); tt(un(b, 9), un(b, 15), un(b, 13), A.min)
            if not fin:
                lin(fs(b, 0, 2, 3), un(b, 0, 2, 27)); step(un(b, 21), keys, 0.75, -256.0)
                step(un(b, 17, 2), un(b, 8, 2), 0.3125, 1024.0); tt(fs(b, 1, 2), un(b, 8, 2), un(b, 17, 2), A.max); tt(un(b, 19), un(b, 27), un(b, 9), A.is_le)
                cur[1] = 1; prep(rnd + 1, b)
            else:
                for k, u in enumerate((0, 8, 9, 27)):
                    if k < 3: either(un(b, 16 + k), un(b, u), (F.Relu, -80.0, 256.0), (0.3125, A.is_ge, 16.0, A.mult))
                    else: tt(un(b, 19), un(b, 27), un(b, 9), A.is_le); tt(un(b, 19), un(b, 19), un(b, 16), A.max)
                    tt(ap("FO" + b, sa, ALL, k), un(b, u), un(b, 16 + k), A.subtract)
                either(un(b, 21), keys, (F.Relu, -2.0 ** 23, 2.0 ** 24), (0.5, A.is_ge, 2.0 ** 23, A.mult))
                ts(si(b, 1), si(b, 0), 65535, A.bitwise_and)
                for u in range(2): tt(ap("FP" + b, ALL, u), si(b, 1 + u), un(b, 21), A.subtract)
                bn = bank(); at = lambda k: sl(CW * (k % 2) + 128 * (k // 2), CW * (k % 2) + 128 * (k // 2) + 128)
                group([(ap(bn, (96, 120), at(k)), ap("FP" + b, k), ap("I32")) for k in range(4)])
                group([(ap(bn, (0, 96), at(k)), ap("FO" + b, sl(4 * k, 4 * k + 8)), I) for k in range(4)])
                r120 = (0, 120); out = T["AC" + b]; r = sl(4 * bi, 4 * bi + 4)
                ts(ap("AC" + b, r120), ap(bn, r120), ap("BC", r120, sl(35, 36)), A.mult, ap("BC", r120, sl(36, 37)), A.max)
                dma("oyl" + b, T.yl[r, :], out[0:48, :], [ap("AC" + b)], [], 1e5)
                dma("oyt" + b, T.yt[r, :], out[96:108, :], [ap("AC" + b)], [], 3e4); dma("oyc" + b, T.yc[r, :], out[108:120, :], [ap("AC" + b)], [], 3e4)

    n = len(ops); succ = [[] for _ in ops]
    for k, o in enumerate(ops):
        for d in list(o["deps"]):
            if "pair" in ops[d] and ops[d]["pair"] not in o["deps"]: o["deps"].append(ops[d]["pair"])
    for o in ops:
        if "pair" in o: o["deps"].remove(o["pair"])
    for k, o in enumerate(ops):
        for d in o["deps"]: succ[d].append(k)
    opens = {v[0]: name for name, v in sess.items()}; member = {}
    for name, v in sess.items():
        for k in v: member.setdefault(k, []).append(name)
    pred = [list(o["deps"]) for o in ops]; lat = [o["lat"] for o in ops]; kind = [o["eng"] for o in ops]
    def cost(k, e): return ops[k]["cost"][e] if kind[k] == "F" else ops[k]["cost"]
    def lag(d, k): return lat[d] + (0.0 if kind[d] == kind[k] == "T" else LAG)

    def walk(pri, eng, back):
        pre, post = (succ, pred) if back else (pred, succ); eng = list(eng)
        todo = {name: len(v) for name, v in sess.items()}; at = {}; extra = []
        banks = {"B%d" % k: [None, 0.0] for k in range(8)}
        left = [len(p) for p in pre]; rdy = [lat[k] if back else 0.0 for k in range(n)]; free = dict.fromkeys("PTVASX", 0.0)
        pool = {e: [] for e in "PTVASXF"}; order = []; start = [0.0] * n; end = 0.0
        for k in range(n):
            if not left[k]: pool[eng[k]].append(k)
        while len(order) < n:
            idle = [(v[1], name) for name, v in banks.items() if v[0] is None or not todo[v[0]]]
            tb = min(idle)[0] + LAG if idle else 1e9
            when = (lambda k: rdy[k]) if back else (lambda k: max(rdy[k], tb) if k in opens else rdy[k])
            best = None
            for e in free:
                own = pool[e]; c = own + pool["F"] if e == "A" else own
                if e == "V":
                    to = min([max(free[e], when(k)) for k in own] + [1e9])
                    c = own + [k for k in pool["F"] if max(free[e], when(k)) + cost(k, "V") <= min(to + SLACK, max(free["A"], when(k)) + cost(k, "A") - GAIN)]
                if not c: continue
                t = max(free[e], min(when(k) for k in c))
                if best is None or t < best[0]: best = (t, e, c)
            t, e, c = best
            k = max((k for k in c if when(k) <= t + LOOK), key=lambda k: pri[k])
            pool[eng[k]].remove(k); t = max(t, when(k)); eng[k] = e
            if k in opens and not back:
                name = min(idle)[1]; old = banks[name][0]
                extra += [(d, k) for d in (sess[old] if old else [])]
                banks[name][0] = opens[k]; at[opens[k]] = name
            free[e] = t + cost(k, e); order.append(k); start[k] = t; end = max(end, free[e] + (0.0 if back else lat[k]))
            for name in (member.get(k, []) if not back else []):
                todo[name] -= 1; banks[at[name]][1] = max(banks[at[name]][1], free[e])
            for s in post[k]:
                rdy[s] = max(rdy[s], free[e] + (lag(s, k) if back else lag(k, s))); left[s] -= 1
                if not left[s]: pool[eng[s]].append(s)
        return end, order, start, eng, at, extra

    def replay(w, gc, slow, wire):
        more = {}; done = [0.0] * n; free = dict.fromkeys("PTVASX", 0.0)
        for d, k in w[5]: more.setdefault(k, []).append(d)
        for k in w[1]:
            e = w[3][k]; t = max([free[e]] + [done[d] + (wire if kind[d] == "X" else lag(d, k)) for d in pred[k] + more.get(k, [])])
            free[e] = done[k] = t + slow * (cost(k, e) + (gc - GC) * CYC * ops[k].get("gat", 0))
        return max(t + lat[k] for k, t in enumerate(done))

    if "plan" not in PLAN:
        pri = [0.0] * n
        for k in range(n - 1, -1, -1): pri[k] = cost(k, "A") + max([lag(k, s) + pri[s] for s in succ[k]] + [lat[k]])
        path = pri; shake = np.random.RandomState(0)
        for lead in LEADS + (None,) * SHAKES:
            if lead is None: pri = list(np.array(PLAN["pri"]) + np.repeat(shake.normal(0, 0.4, n // 8 + 1), 8)[:n])
            else: pri = [p - lead * (o["ch"] % NB) for p, o in zip(path, ops)]
            for k in range(PASSES if lead else 2):
                w = walk(pri, kind, False)
                score = w[0] + sum(replay(w, *c) / c[1] for c in OTHER) / len(OTHER)
                if "plan" not in PLAN or score < PLAN["score"]: PLAN["plan"], PLAN["score"], PLAN["pri"] = w, score, pri
                PLAN.setdefault("log", []).append(round(w[0], 1))
                b = walk([t + cost(k, e) for k, (t, e) in enumerate(zip(w[2], w[3]))], w[3], True)
                pri = [t + cost(k, e) for k, (t, e) in enumerate(zip(b[2], b[3]))]
    end, order, start, eng, at, extra = PLAN["plan"]; place.update(at)
    for d, k in extra:
        if d not in ops[k]["deps"]: ops[k]["deps"].append(d); succ[d].append(k)
    for k, o in enumerate(ops):
        if o["eng"] == "F": o["eng"], o["fn"], o["cost"] = eng[k], o["fn"][eng[k]], o["cost"][eng[k]]
        o["t"] = start[k]
    cnt = dict.fromkeys("PTVA", 0); total = {}
    for k in order:
        o = ops[k]
        if o["sem"] is None and any(not (o["eng"] == ops[s]["eng"] == "T") for s in succ[k]):
            cnt[o["eng"]] += 1; o["sem"], o["val"], o["inc"] = "s" + o["eng"], cnt[o["eng"]], 1
        elif o["eng"] == "S": o["inc"] = 16
        if o["val"] is not None: total[o["sem"]] = o["val"]
    seen = {e: {} for e in Q}
    for k in order:
        o = ops[k]; e = o["eng"]
        if e == "X": continue
        need = {}
        for d in o["deps"]:
            p = ops[d]
            if p["eng"] == e == "T": continue
            need[p["sem"]] = max(need.get(p["sem"], 0), p["val"])
        for s, v in need.items():
            if seen[e].get(s, 0) < v: Q[e].wait_ge(T.sem[s], v); seen[e][s] = v
        ins = o["fn"](Q[e])
        if "inc" in o: ins.then_inc(T.sem[o["sem"]], o["inc"])
    total["sent"] = 2 * NB * RO * sum(bin(m).count("1") for m in masks(T, topo, rank))
    for s, v in total.items(): g.wait_ge(T.sem[s], v)
    return ops, order
